import numpy as np, ml_dtypes
CORES = [2,6,10,14,18,22,26,30]
N = 8
BF = ml_dtypes.bfloat16
def gentries(a):
    return np.ascontiguousarray(a.reshape(8, 16, -1).transpose(0, 2, 1)).reshape(8, -1)
def gtable(e):
    e = np.asarray(e); return np.ascontiguousarray(e.reshape(8, -1, 16).transpose(0, 2, 1)).reshape(128, -1).astype(np.int32)
M, FAR, S, F, RO = 2048, 3, 384, 1536, 5
def trees(rng, top, share):
    on = ((np.arange(M) < top) | (rng.random((N, 8, M)) < share)).astype(np.int64)
    c = np.add.accumulate(on, axis=2) - 1; inner = (on == 1) & (2 * c + 2 <= M - 1)
    pi = np.concatenate([np.zeros((N, 8, 1), np.int64), 1 + np.argsort(rng.random((N, 8, M - 1)), axis=2)], axis=2)
    kl = np.zeros((N, 8, M), np.int64); kr = np.zeros((N, 8, M), np.int64)
    np.put_along_axis(kl, pi, np.where(inner, np.take_along_axis(pi, np.minimum(2 * c + 1, M - 1), 2), 0), 2)
    np.put_along_axis(kr, pi, np.where(inner, np.take_along_axis(pi, np.minimum(2 * c + 2, M - 1), 2), 0), 2)
    return kl, kr, pi
def starts(rng, pi, ia, ib):
    far = np.stack([np.concatenate([d * M + pi[(q + 1 + d) % N] for d in range(FAR)], axis=1) for q in range(N)])
    return np.take_along_axis(pi, ia, 2), np.take_along_axis(far, rng.integers(0, FAR, (N, 8, S)) * M + ib, 2)
def near(rng):
    return (M * rng.random((N, 8, S)) ** 3).astype(np.int64)
def signs(rng, v):
    q = rng.choice(np.array([0.004, 0.015, 0.03, 0.05]), (N, 8, 1, 1))
    return np.where(rng.random(v.shape) < 2 * q * rng.random((N, 8, 1, M)), -v, v)
def parts(rng):
    kl, kr, pi = trees(rng, M // 8, 0.75); a, b = starts(rng, pi, near(rng), near(rng))
    return signs(rng, rng.integers(0, 4097, (N, 8, 16, M))), kl, kr, pi, a, b
def pack(h, kl, kr, a, b):
    return {"h": np.ascontiguousarray(h.reshape(N, 128, M)).astype(np.float32).astype(BF), "kl": kl.astype(np.int32), "kr": kr.astype(np.int32),
            "sa": np.stack([gtable(x) for x in a]), "sb": np.stack([gtable(x) for x in b])}
def setup_inputs(rng):
    h, kl, kr, pi, a, b = parts(rng)
    return pack(h, kl, kr, a, b)
def setup_inputs_alike(rng):
    h, kl, kr, pi, a, b = parts(rng)
    a[:, 0] = np.tile(a[:, 0, :4], (1, S // 4)); b[:, 0] = np.tile(b[:, 0, :4], (1, S // 4))
    a[:, 1] = rng.choice(np.array([0, M - 1]), (N, S)); b[:, 1] = rng.choice(np.array([0, FAR * M - 1]), (N, S))
    a[:, 1, 0] = 0; b[:, 1, 0] = 0; kl[:, 1, 0] = 0; kr[:, 1, 0] = 0; h[:, 1, :, 0] = np.abs(h[:, 1, :, 0])
    la, lb = starts(rng, pi, M - 1 - rng.integers(0, M // 8, (N, 8, S)), M - 1 - rng.integers(0, M // 8, (N, 8, S)))
    a[:, 2] = la[:, 2]; b[:, 2] = lb[:, 2]
    inner = kl > 0; own = np.maximum(np.arange(M), 1)
    kl[:, 4] = np.where(inner[:, 4], own, 0); kr[:, 4] = np.where(inner[:, 4], own, 0)
    few = np.array([1, M // 2, M - 1])
    kl[:, 6] = np.where(inner[:, 6], rng.choice(few, (N, M)), 0); kr[:, 6] = np.where(inner[:, 6], rng.choice(few, (N, M)), 0)
    return pack(h, kl, kr, a, b)
def setup_inputs_cold(rng):
    h, kl, kr, pi, a, b = parts(rng); o = [int(x) for x in rng.permutation(8)]
    h[:, o[0]] = -1 - np.abs(h[:, o[0]])
    h[:, o[1]] = np.where(rng.random((N, 16, M)) < 0.1, -1, 1) * np.abs(h[:, o[1]])
    for g in (o[2], o[4], o[5]):
        h[:, g] = np.abs(h[:, g]); z = pi[:, g, M - 1]
        h[np.arange(N), g, 0, z] = -65536; a[:, g] = z[:, None]
    one = np.array([7, 9, 10, 11, 12, 13, 14]); level = np.arange(31, 63)
    for q in range(N):
        nx = (q + 1) % N
        h[q, o[4], 0, pi[q, o[4], one]] = -65536; h[q, o[5], 0, pi[q, o[5], level]] = -65536
        j = (0, S - 1)[q % 2]; a[q, o[2], j] = pi[q, o[2], 1]; b[q, o[2], j] = pi[nx, o[2], 1]
        j = (0, S - 1, S // 2, 17)[q % 4]
        a[q, o[4], j] = pi[q, o[4], M - 3]; b[q, o[4], j] = pi[nx, o[4], (M - 3, 1)[q % 2]]
        a[q, o[5], j] = pi[q, o[5], M - 3]; b[q, o[5], j] = pi[nx, o[5], (7, 3, 1, 0)[q % 4]]
    q = int(rng.integers(0, N)); h[q, o[3]] = -1 - np.abs(h[q, o[3]])
    return pack(h, kl, kr, a, b)
def setup_inputs_room(rng):
    kl, kr, pi = trees(rng, M, 1.0); h = rng.integers(0, 4097, (N, 8, 16, M))
    h[np.arange(N)[:, None], np.arange(8)[None, :], rng.integers(0, 16, (N, 8)), pi[:, :, M - 1]] = -65536
    ia = near(rng); ib = near(rng); w = S // 8; o = rng.permutation(8); low = M // 2 - 1; safe = low + M // 16
    for q in range(N):
        for g in range(8):
            c = int(o[g])
            if c == 7: continue
            leaf = rng.integers(low, M - 1, S); deep = rng.integers(0, M // 8 - 1, S)
            if c < 3: deep = rng.integers(M // 16 - 1, M // 8 - 1, S)
            if c == 4 or c == 5:
                t = M // 16 if c == 4 else M // 32
                deep = rng.integers(t - 1, 2 * t - 1, S); leaf = rng.integers(low, safe, S)
                dead = safe + np.flatnonzero(rng.random(M - 1 - safe) < 0.75)
                h[q, g, rng.integers(0, 16, len(dead)), pi[q, g, dead]] = -65536
            u = deep
            if c < 4:
                n = 3 * S + w + (0, 1, -1, (0, 1, -1)[q % 3])[c]; x = n // 7; y = n - 7 * x
                u = np.concatenate([deep[:x], rng.integers(M // 4 - 1, M // 2 - 1, y), np.full(w, M - 1, np.int64), rng.integers(M // 2 - 1, M - 1, S - x - y - w)])
                u = rng.permutation(u)
            flip = rng.random(S) < 0.5
            ia[q, g] = np.where(flip, leaf, u); ib[q, g] = np.where(flip, u, leaf)
    a, b = starts(rng, pi, ia, ib)
    return pack(h, kl, kr, a, b)
def setup_inputs_spread(rng):
    kl, kr, pi = trees(rng, 32, 0.55); a, b = starts(rng, pi, near(rng), near(rng))
    v = np.floor(np.exp2(16 * rng.random((N, 8, 1, M))) * rng.random((N, 8, 16, M))).astype(np.int64)
    v = np.where(rng.random(v.shape) < 0.01, 65536, v)
    return pack(signs(rng, v), kl, kr, a, b)
def setup_inputs_ties(rng):
    h, kl, kr, pi, a, b = parts(rng)
    u = rng.random((N, 8, 16, M)); h = np.where(u < 0.05, -1, np.where(u < 0.15, 0, 1)) * np.array([1, 128, 32768, 65536, 1, 2, 1, 4]).reshape(1, 8, 1, 1)
    h[:, 6, :8] = 65536
    q = np.arange(N); nx = (q + 1) % N
    h[q, 0, :, pi[q, 0, 1]] = -65536
    for j, v in ((3, 1), (4, 1), (M - 1, 1), (2, -2), (5, 0), (6, 0), (9, -1), (M - 2, 4), (M - 3, 4)): h[q, 0, :, pi[q, 0, j]] = v
    kl[q, 0, pi[q, 0, 9]] = pi[q, 0, M - 2]; kr[q, 0, pi[q, 0, 9]] = pi[q, 0, M - 3]
    a[q, 0, 0] = pi[q, 0, M - 1]; b[q, 0, 0] = pi[nx, 0, 1]
    a[q, 0, 1] = pi[q, 0, 1]; b[q, 0, 1] = pi[nx, 0, M - 1]
    a[q, 0, 2] = pi[q, 0, 2]; b[q, 0, 2] = pi[nx, 0, 9]
    d = pack(h, kl, kr, a, b); x = d["h"].astype(np.float32)
    d["h"] = np.where((x == 0) & (rng.random(x.shape) < 0.5), np.float32(-0.0), x).astype(BF)
    return d
def check_inputs(d):
    bad = []
    x = np.asarray(d["h"]).astype(np.float32)
    if not np.all(x == np.floor(x)): bad.append("whole numbers in h")
    if not np.max(np.abs(x)) <= 65536: bad.append("range of h")
    for k, hi in (("kl", M - 1), ("kr", M - 1), ("sa", M - 1), ("sb", FAR * M - 1)):
        if np.min(d[k]) < 0 or np.max(d[k]) > hi: bad.append("range of " + k)
    if not np.all((np.asarray(d["kl"]) == 0) == (np.asarray(d["kr"]) == 0)): bad.append("two kids or none")
    return bad
def reference(h, kl, kr, sa, sb):
    hw = h.astype(np.float32).astype(np.int64).reshape(N, 8, 16, M); left = kl.astype(np.int64); right = kr.astype(np.int64)
    ya = np.full((N, 8, F), -1.0, np.float32); yb = np.full((N, 8, F), -1.0, np.float32); ys = np.zeros((N, 8, F), np.float32)
    swap = np.arange(16) ^ 1
    for r in range(N):
        far = [(r + 1 + d) % N for d in range(FAR)]; first = gentries(sa[r]).astype(np.int64); second = gentries(sb[r]).astype(np.int64)
        for g in range(8):
            ha = hw[r, g]; hb = np.concatenate([hw[q, g] for q in far], axis=1); hs = hb[swap]
            la, ra = left[r, g], right[r, g]
            lb = np.concatenate([np.where(left[q, g] > 0, left[q, g] + d * M, 0) for d, q in enumerate(far)])
            rb = np.concatenate([np.where(right[q, g] > 0, right[q, g] + d * M, 0) for d, q in enumerate(far)])
            za = np.add.reduce(ha, axis=0); zb = np.add.reduce(hb, axis=0)
            a, b = first[g], second[g]
            for rnd in range(RO):
                fa = la[a] == 0; fb = lb[b] == 0
                oa = ~fa & (fb | (za[a] >= zb[b])); ob = ~fb & ~oa
                ca = np.stack([np.where(oa, la[a], a), np.where(oa, ra[a], a)], axis=1).reshape(-1)
                cb = np.stack([np.where(ob, lb[b], b), np.where(ob, rb[b], b)], axis=1).reshape(-1)
                there = np.stack([np.ones(len(a), bool), oa | ob], axis=1).reshape(-1)
                keep = there & np.all(ha[:, ca] + hs[:, cb] >= 0, axis=0)
                a = ca[keep][:F]; b = cb[keep][:F]
            ya[r, g, :len(a)] = a; yb[r, g, :len(a)] = b; ys[r, g, :len(a)] = za[a] + zb[b]
    return {"ya": ya, "yb": yb, "ys": ys}

@@ -1,0 +1,609 @@
+from concourse.bass import DstId, RemoteDMATransfer
+from concourse.mybir import AluOpType as A, ActivationFunctionType as AF
+
+M = 2048
+FAR = 3
+PITCH = M + 32
+NT = PITCH * (FAR + 1)
+WINW = 4704
+ZW = 1568
+HC = (0, 512, 1024, 1536, 2048)
+NH = len(HC) - 1
+REC = {"c": (0, 384), "k": (384, 896)}
+ITEMS = (0, "k", "c", 1, 2, 3)
+
+
+def base(t):
+    return 32 + PITCH * t
+
+
+SCRATCH = {
+    "TB": ("sbuf", [128, NT], "bfloat16"), "IT": ("sbuf", [128, NT], "bfloat16"),
+    "IN": ("sbuf", [128, 4 * M], "bfloat16"), "HN": ("sbuf", [128, M], "bfloat16"),
+    "CI": ("sbuf", [128, 4 * 896], "bfloat16"),
+    "W0": ("sbuf", [128, WINW], "bfloat16"), "W1": ("sbuf", [128, WINW], "bfloat16"), "W2": ("sbuf", [128, WINW], "bfloat16"),
+    "RP": ("sbuf", [128, 1536], "bfloat16"), "RQ": ("sbuf", [128, 1536], "bfloat16"), "NX": ("sbuf", [128, 1536], "bfloat16"),
+    "FL": ("sbuf", [128, 1536], "bfloat16"), "FR": ("sbuf", [128, 1536], "bfloat16"),
+    "SIN": ("sbuf", [128, 1536], "bfloat16"), "SRC": ("sbuf", [128, 1536], "bfloat16"),
+    "KI": ("sbuf", [128, 256], "int32"), "KF": ("sbuf", [128, 256], "float32"), "KT": ("sbuf", [128, 256], "float32"),
+    "KLR": ("sbuf", [128, 256], "float32"), "D2": ("sbuf", [128, 256], "float32"), "WK": ("sbuf", [128, 768], "float32"),
+    "SAB": ("sbuf", [128, 48], "int32"), "SF": ("sbuf", [128, 96], "float32"),
+    "Y": ("sbuf", [128, 160], "float32"), "Y16": ("sbuf", [128, 8], "float32"), "B32": ("sbuf", [128, 128], "float32"),
+    "V": ("sbuf", [128, 128], "float32"),
+    "PI": ("sbuf", [128, 8], "int32"), "PJ": ("sbuf", [128, 8], "int32"), "PF": ("sbuf", [128, 16], "float32"),
+    "Z": ("sbuf", [128, 160], "bfloat16"), "ZB": ("sbuf", [128, 160], "bfloat16"),
+    "ZS0": ("sbuf", [128, 160], "bfloat16"), "ZS1": ("sbuf", [128, 160], "bfloat16"),
+    "ZX0": ("sbuf", [128, 160], "bfloat16"), "ZX1": ("sbuf", [128, 160], "bfloat16"),
+    "ZF0": ("sbuf", [128, 160], "float32"), "ZF1": ("sbuf", [128, 160], "float32"),
+    "ZN0": ("sbuf", [128, 160], "float32"), "ZN1": ("sbuf", [128, 160], "float32"),
+    "IDF": ("sbuf", [128, 128], "float32"), "IDB": ("sbuf", [128, 128], "bfloat16"), "NBG": ("sbuf", [128, 128], "bfloat16"),
+    "TRF": ("sbuf", [128, 128], "float32"), "TRB": ("sbuf", [128, 128], "bfloat16"), "TRU": ("sbuf", [128, 128], "bfloat16"),
+    "TMP": ("sbuf", [128, 512], "float32"),
+    "GE": ("sbuf", [128, 24], "float32"), "E8": ("sbuf", [128, 8], "float32"), "RG": ("sbuf", [128, 16], "float32"),
+    "WA": ("sbuf", [128, 32], "bfloat16"), "WN": ("sbuf", [128, 32], "bfloat16"), "WS": ("sbuf", [128, 32], "bfloat16"),
+    "JH": ("sbuf", [128, 96], "bfloat16"), "JC": ("sbuf", [128, 96], "bfloat16"),
+    "OPQ": ("sbuf", [128, 6 * 192], "uint16"), "OV": ("sbuf", [128, 288], "uint16"), "OS": ("sbuf", [128, 96], "uint16"),
+    "MK": ("sbuf", [128, 256], "float32"), "MM": ("sbuf", [128, 384], "float32"), "VT": ("sbuf", [128, 384], "float32"),
+    "VW": ("sbuf", [128, 288], "float32"), "PC": ("sbuf", [128, 576], "bfloat16"),
+    "KP": ("sbuf", [128, 192], "bfloat16"), "TOT": ("sbuf", [128, 8], "float32"),
+    "SC": ("sbuf", [128, 192], "float32"), "PT": ("sbuf", [128, 256], "float32"),
+    "FIN": ("sbuf", [128, 864], "float32"), "YO": ("sbuf", [128, 288], "float32"),
+}
+for _b in range(8):
+    SCRATCH["P%d" % _b] = ("psum", [128, 512], "float32")
+
+SEMAPHORES = (["cg", "cv", "ca", "ct", "ls", "hxc", "hxk"] + ["hx%d" % k for k in range(NH)] + ["d%d" % i for i in range(14)]
+              + ["h%d_%d" % (t, k) for t in (1, 2, 3) for k in range(NH)] + ["%si%d" % (k, t) for t in (1, 2, 3) for k in "ck"])
+
+
+def routes(T, topo):
+    cores = list(T.cores)
+    n = len(cores)
+    first = {r: [] for r in range(n)}
+    relay = {}
+
+    def free(c0, die, ok):
+        return [c for c in topo.cores_of(c0) if c not in cores and c not in relay and topo.die(c) == die and ok(c)][0]
+
+    for s in range(n):
+        cs = cores[s]
+        by_chip = {}
+        for d in range(1, FAR + 1):
+            r = (s - d) % n
+            by_chip.setdefault(topo.chip(cores[r]), []).append(r)
+        for ch, rs in by_chip.items():
+            c0 = cores[rs[0]]
+            if ch == topo.chip(cs):
+                first[s].append((c0, rs[0], ITEMS))
+            elif len(rs) > 1:
+                c = free(c0, topo.die(cs), lambda c: topo.may_write(cs, c))
+                relay[c] = (s, rs, ITEMS)
+                first[s].append((c, None, ITEMS))
+            else:
+                dies = sorted(set(topo.die(c) for c in topo.cores_of(cs)), key=lambda d: d == topo.die(c0))
+                for d, items in zip(dies, ((0, "c", 2), ("k", 1, 3))):
+                    c = free(cs, d, lambda c: topo.may_write(c, c0))
+                    relay[c] = (s, rs, items)
+                    first[s].append((c, None, items))
+    return first, relay
+
+
+def bits(m):
+    return bin(m).count("1")
+
+
+def off_mask(T, topo, c):
+    return topo.mask(c, [x for x in T.cores if topo.chip(x) != topo.chip(c)][0])
+
+
+def staged(T, k):
+    return T.CI[:, REC[k][0]:REC[k][1]] if k in REC else T.HN[:, HC[k]:HC[k + 1]]
+
+
+def landing(T, t, k):
+    if t is None:
+        return staged(T, k), T.sem["hx%s" % k]
+    if k in REC:
+        return T.CI[:, 896 * t + REC[k][0]:896 * t + REC[k][1]], T.sem["%si%d" % (k, t)]
+    return T.TB[:, base(t) + HC[k]:base(t) + HC[k + 1]], T.sem["h%d_%d" % (t, k)]
+
+
+def transfer(T, topo, c, mask, t, k):
+    a = topo.addr(c)
+    d, sm = landing(T, t, k)
+    return RemoteDMATransfer(dst_ids=[DstId(rid=a[0], pnc=a[1])], dma_engine_mask=mask, remote_sem=sm, src=staged(T, k), dst=d)
+
+
+def relay_program(g, core, T, topo, s, rs, items):
+    n = len(T.cores)
+    off = off_mask(T, topo, core)
+    tot = 0
+    for k in items:
+        g.wait_ge(T.sem["hx%s" % k], bits(off))
+        masks = [off if j == 0 else topo.mask(core, T.cores[r]) & ~off for j, r in enumerate(rs)]
+        g.remote_dma_fused([transfer(T, topo, T.cores[r], m, (s - r) % n, k) for r, m in zip(rs, masks)], local_sem=T.sem.ls)
+        tot += sum(bits(m) for m in masks)
+    g.wait_ge(T.sem.ls, tot)
+
+
+def rank_program(g, core, T, topo):
+    first, relay = routes(T, topo)
+    rank = T.rank_of(core)
+    if rank is None:
+        if core in relay:
+            relay_program(g, core, T, topo, *relay[core])
+        return
+    n = len(T.cores)
+    Q = {"g": g, "v": g.vector, "a": g.scalar, "t": g.tensor, "s": g.sync}
+    ops = []
+    wr = {}
+    rd = {}
+    ndma = [0]
+
+    def op(e, fn, r=(), w=(), kind="c", ext=()):
+        me = len(ops)
+        deps = set()
+        for x in r:
+            if x in wr:
+                deps.add(wr[x])
+            if x[0] == "@":
+                deps.update(j for j in rd.get(x, []) if ops[j]["e"] != e)
+        for x in w:
+            js = rd.get(x, []) + ([wr[x]] if x in wr else [])
+            deps.update(j for j in js if ops[j]["e"] != e or ops[j]["kind"] != "c" or kind != "c")
+        if e == "t":
+            deps = set(j for j in deps if ops[j]["e"] != "t")
+        o = {"e": e, "fn": fn, "deps": deps, "kind": kind, "ext": list(ext), "need": False}
+        if kind == "d":
+            o["name"] = "d%d" % ndma[0]
+            ndma[0] += 1
+        ops.append(o)
+        for x in r:
+            rd.setdefault(x, []).append(me)
+        for x in w:
+            wr[x] = me
+            rd[x] = []
+        return me
+
+    vec, act, pe = g.vector, g.scalar, g.tensor
+
+    def ts(out, in0, s1, o0, r, w, s2=None, o1=None):
+        if o1 is None:
+            op("v", lambda: vec.tensor_scalar(out, in0, s1, None, o0), r, w)
+        else:
+            op("v", lambda: vec.tensor_scalar(out, in0, s1, s2, o0, o1), r, w)
+
+    def tt(out, a, b, o, r, w, ext=()):
+        op("v", lambda: vec.tensor_tensor(out, a, b, o), r, w, ext=ext)
+
+    def cp(out, a, r, w, ext=()):
+        op("v", lambda: vec.tensor_copy(out, a), r, w, ext=ext)
+
+    def ms(out, c, w):
+        op("v", lambda: vec.memset(out, c), (), w)
+
+    def ac(out, a, r, w, scale=1.0, ext=()):
+        op("a", lambda: act.activation(out, a, AF.Copy, scale=scale), r, w, ext=ext)
+
+    def af(out, a, f, scale, bias, r, w):
+        op("a", lambda: act.activation(out, a, f, bias=bias, scale=scale), r, w)
+
+    def mm(lst, r, w):
+        def fn():
+            ins = None
+            for (out, l, x, st, sp) in lst:
+                ins = pe.matmul(out, l, x, st, sp)
+            return ins
+        op("t", fn, r, w)
+
+    def grp(out, terms):
+        return [(out, l, x, j == 0, j == len(terms) - 1) for j, (l, x) in enumerate(terms)]
+
+    def run(trip, opens, closes):
+        return [(o_, l, x, opens and j == 0, closes and j == len(trip) - 1) for j, (o_, l, x) in enumerate(trip)]
+
+    def dma(e, out, in_, r, w):
+        op(e, lambda: Q[e].dma_start(out, in_), r, w, kind="d")
+
+    def iota(out, pat, b, w):
+        op("g", lambda: g.iota(out, pat, b, 0, allow_small_or_imprecise_dtypes=True), (), w)
+
+    P = [T["P%d" % b] for b in range(8)]
+    col = lambda t, j: t[:, j:j + 1]
+    HNT = ["HN%d" % k for k in range(NH)]
+
+    dma("s", T.HN[:, HC[0]:HC[1]], T.h[:, HC[0]:HC[1]], (), ["HN0"])
+    dma("a", T.KI[1:128:2, :], T.kr[:], (), ["KIb"])
+    dma("s", T.KI[0:128:2, :], T.kl[:], (), ["KIa"])
+    dma("a", T.HN[:, HC[1]:HC[2]], T.h[:, HC[1]:HC[2]], (), ["HN1"])
+    dma("s", T.HN[:, HC[2]:HC[3]], T.h[:, HC[2]:HC[3]], (), ["HN2"])
+    dma("a", T.HN[:, HC[3]:HC[4]], T.h[:, HC[3]:HC[4]], (), ["HN3"])
+    dma("s", T.SAB[:, 0:24], T.sa[:], (), ["SA"])
+    dma("s", T.SAB[:, 24:48], T.sb[:], (), ["SB"])
+    b0 = base(0)
+    dma("s", T.TB[0:128:2, b0:b0 + M], T.h[1:128:2, :], HNT, ["T0a"])
+    dma("s", T.TB[1:128:2, b0:b0 + M], T.h[0:128:2, :], (), ["T0b"])
+
+    op("g", lambda: g.iota(T.PI[:], [[0, 8]], 0, 1), (), ["PI"])
+    iota(T.Y[:], [[1, 160]], 0, ["Y"])
+    iota(T.B32[:], [[32, 64], [0, 2]], 0, ["B32"])
+    iota(T.Y16[:], [[16, 8]], 0, ["Y16"])
+    for j, mk in enumerate((127, 15, 112, 31, 96, 16)):
+        ts(col(T.PJ, j), col(T.PI, j), mk, A.bitwise_and, ["PI"], ["PJ%d" % j])
+    cp(T.PF[:, 0:6], T.PJ[:, 0:6], ["PJ%d" % j for j in range(6)], ["PF"])
+    cP, cI, cG16, cP32, cG32, cH16 = [col(T.PF, j) for j in range(6)]
+    ts(col(T.PF, 6), cH16, 64.0, A.mult, ["PF"], ["PF6"])
+    ts(col(T.PF, 7), cH16, -64.0, A.mult, ["PF"], ["PF7"], 1024.0, A.add)
+    ts(T.V[:], T.B32[:], cP32, A.add, ["B32", "PF"], ["V"])
+    ts(T.PF[:, 8:10], T.PF[:, 6:8], cG32, A.add, ["PF6", "PF7"], ["PF8"], 31.0, A.add)
+    ts(T.PF[:, 10:12], T.PF[:, 6:8], cP, A.add, ["PF6", "PF7"], ["PF10"], 16.0, A.add)
+    ZS, ZX, ZF, ZN = (T.ZS0, T.ZS1), (T.ZX0, T.ZX1), (T.ZF0, T.ZF1), (T.ZN0, T.ZN1)
+    for x in (0, 1):
+        ts(ZS[x][:], T.Y[:], col(T.PF, 8 + x), A.is_equal, ["Y", "PF8"], ["ZS%d" % x])
+
+    lst = []
+    for x in (0, 1):
+        lst += grp(P[0][:, x:128:2], [(ZS[x][:, 31 - y:159 - y], T.HN[:, y:M:32]) for y in range(32)])
+    mm(lst, ["ZS0", "ZS1"] + HNT, ["@0"])
+
+    cp(T.KF[:], T.KI[:], ["KIa", "KIb"], ["KF"])
+    op("v", lambda: vec.transpose(T.KT[:], T.KF[:]), ["KF"], ["KT"])
+    for side in (0, 1):
+        for sg in range(8):
+            c0 = 128 * side + 16 * sg
+            (ac if side else cp)(T.KLR[:, c0:c0 + 16], T.KT[:, 2 * sg + side:256:16], ["KT"], ["K%d%d" % (side, sg)])
+    KL, KR = T.KLR[:, 0:128], T.KLR[:, 128:256]
+    wk = lambda j: T.WK[:, 128 * j:128 * j + 128]
+    ci = lambda j, k=1, t=0: T.CI[:, 896 * t + 128 * j:896 * t + 128 * (j + k)]
+    ts(wk(2), KL, 0.0, A.is_equal, ["K0%d" % sg for sg in range(8)], ["leaf"])
+    tt(wk(3), wk(2), T.V[:], A.mult, ["leaf", "V"], ["w3"])
+    tt(T.D2[:, 128:256], KR, wk(2), A.subtract, ["leaf"] + ["K1%d" % sg for sg in range(8)], ["D2b"])
+    tt(T.D2[:, 0:128], KL, wk(3), A.add, ["w3"], ["D2a"])
+    af(wk(4), wk(2), AF.Identity, -float(2 ** 22), float(2 ** 21), ["leaf"], ["w4"])
+    cp(ci(3, 2), T.D2[:], ["D2a", "D2b"], ["c3"])
+    tt(ci(5, 2), T.D2[:], ci(3, 2), A.subtract, ["c3"], ["c5"])
+    tt(wk(5), P[0][:, 0:128], wk(4), A.min, ["@0", "w4"], ["key"])
+    cp(ci(0), wk(5), ["key"], ["c0"])
+    tt(wk(0), wk(5), ci(0), A.subtract, ["c0"], ["r1"])
+    cp(ci(1), wk(0), ["r1"], ["c1"])
+    tt(ci(2), wk(0), ci(1), A.subtract, ["c1"], ["c2"])
+    CIT = {"c": ["c0", "c1", "c2"], "k": ["c3", "c5"]}
+
+    ls = [0]
+    offm = off_mask(T, topo, core)
+    ARR = bits(offm)
+
+    def send(k):
+        trs = []
+        for (c, r, items) in first[rank]:
+            if k in items:
+                m = topo.mask(core, c) & ~offm if topo.chip(c) == topo.chip(core) else topo.mask(core, c)
+                trs.append(transfer(T, topo, c, m, None if r is None else (rank - r) % n, k))
+                ls[0] += bits(m)
+        op("g", lambda: g.remote_dma_fused(trs, local_sem=T.sem.ls), CIT[k] if k in REC else ["HN%d" % k], (), kind="r")
+
+    for k in ITEMS:
+        send(k)
+    for t in range(4):
+        iota(T.TB[:, PITCH * t:PITCH * t + 32], [[0, 32]], -131072, ["TD%d" % t])
+        if t:
+            iota(T.IT[:, PITCH * t:PITCH * t + 32], [[0, 32]], 0, ["ID%d" % t])
+    WIN = (T.W0, T.W1, T.W2)
+    iota(T.SIN[:], [[0, 1536]], 0, ["SIN"])
+    for k in range(3):
+        iota(WIN[k][:, 0:ZW], [[0, ZW]], 0, ["W%d" % k])
+
+    LANE = (0, 1, 2, 4, 7, 5, 8)
+
+    def lane(t, l, k=1):
+        return T.IN[:, M * t + l:M * (t + k):16]
+
+    src512 = T.HN[:, 0:512]
+    CL = []
+    for l in range(11, 16):
+        if l < 14:
+            ac(lane(0, l, 4), src512, ["HN0"], ["cl%d" % l], scale=0.0)
+        else:
+            ms(lane(0, l, 4), 0.0, ["cl%d" % l])
+        CL.append("cl%d" % l)
+    af(lane(0, 10, 4), src512, AF.Identity, 0.0, cP32, ["HN0", "PF"], ["cl10"])
+    ms(lane(0, 3), 0.5, ["cl3"])
+    ms(lane(1, 3, 3), 0.0, ["cl3f"])
+    CL += ["cl10", "cl3", "cl3f"]
+    for t in range(4):
+        ms(lane(t, 6), float(base(t)), ["cb%d" % t])
+        ac(lane(t, 9), T.B32[:], ["B32"], ["cc%d" % t])
+
+    def fill(t, k, js, f):
+        for j in js:
+            f(lane(t, LANE[j]), ci(j, 1, t), [] if t else CIT[k], ["IN%d_%d" % (t, j)], ext=[("%si%d" % (k, t), ARR)] if t else [])
+
+    def turn_tree(t):
+        op("v", lambda: vec.transpose(T.IT[:, base(t):base(t) + M], T.IN[:, M * t:M * t + M]),
+           ["IN%d_%d" % (t, j) for j in range(7)] + CL + ["cb%d" % t, "cc%d" % t], ["IT%d" % t])
+
+    Y128 = T.Y[:, 0:128]
+    RANGES = ((0, 3), (4, 6), (6, 8), (9, 10), (2, 5), (0, 1), (6, 7), (8, 9), (2, 3), (6, 6))
+
+    def ranges(js):
+        for j in js:
+            ts(col(T.RG, j), col(T.GE, RANGES[j][0]), col(T.GE, RANGES[j][1] + 1), A.subtract, ["GE"], ["RG%d" % j])
+    ts(T.GE[:, 0:17], T.Y[:, 0:17], cI, A.is_le, ["PF"], ["GE"])
+    ts(T.E8[:], T.Y16[:], cG16, A.is_equal, ["Y16", "PF"], ["E8"])
+    ts(col(T.PF, 12), cI, 0.0, A.is_equal, ["PF"], ["PF12"], float(2 ** 22), A.mult)
+    ts(col(T.PF, 14), cG16, 15.0, A.add, ["PF"], ["PF14"])
+    ranges((3, 9, 0, 1, 2))
+    ts(col(T.RG, 12), col(T.RG, 3), col(T.RG, 9), A.add, ["RG3", "RG9"], ["RG12"])
+    ts(T.IDF[:], Y128, cP, A.is_equal, ["PF"], ["IDF"])
+    for q, j in enumerate((0, 1, 2, 12)):
+        ts(T.WA[:, 8 * q:8 * q + 8], T.E8[:], col(T.RG, j), A.mult, ["E8", "RG%d" % j], ["WA%d" % q], 2.0 if q == 0 else 1.0, A.mult)
+    WAT = ["WA%d" % q for q in range(4)]
+    WST = ["WS%d" % q for q in range(4)]
+    ts(T.IT[:, 0:32], T.Y[:, 0:32], 0.0, A.mult, ["PF12"], ["ID0"], col(T.PF, 12), A.add)
+    ts(T.Z[:], T.Y[:], col(T.PF, 14), A.is_equal, ["PF14"], ["Z"])
+    tm = lambda j: T.TMP[:, 128 * j:128 * j + 128]
+
+    def later(k):
+        if k == 0:
+            ranges((4, 5, 6, 7, 8))
+        elif k == 1:
+            ts(col(T.RG, 10), col(T.RG, 6), col(T.RG, 8), A.subtract, ["RG6", "RG8"], ["RG10"])
+            ts(col(T.RG, 11), col(T.RG, 7), col(T.RG, 5), A.subtract, ["RG7", "RG5"], ["RG11"])
+            ts(col(T.PF, 13), cI, 96.0, A.mult, ["PF"], ["PF13"], 96.0 * 33, A.add)
+            for x in (0, 1):
+                ts(ZF[x][:], T.Y[:], col(T.PF, 10 + x), A.is_equal, ["PF10"], ["ZF%d" % x])
+        elif k == 2:
+            for q, j in enumerate((4, 5, 10, 11)):
+                ts(T.WS[:, 8 * q:8 * q + 8], T.E8[:], col(T.RG, j), A.mult, ["E8", "RG%d" % j], ["WS%d" % q])
+            ts(tm(0), Y128, cP, A.is_gt, ["PF"], ["t0"])
+            for x in (0, 1):
+                ac(ZX[x][:], ZF[x][:], ["ZF%d" % x], ["ZX%d" % x])
+                ac(ZN[x][:], ZF[x][:], ["ZF%d" % x], ["ZN%d" % x], scale=-1.0)
+            ac(T.IDB[:], T.IDF[:], ["IDF"], ["IDB"])
+            ac(T.NBG[:], T.IDF[:], ["IDF"], ["NBG"], scale=-8192.0)
+            af(T.JH[:], T.Y[:, 0:96], AF.Identity, 0.0, col(T.PF, 13), ["Y", "PF13"], ["JH"])
+            ac(T.JC[:], T.Y[:, 0:96], ["Y"], ["JC"])
+        elif k == 3:
+            ts(tm(1), Y128, col(T.PF, 14), A.is_le, ["PF14"], ["t1"])
+            ts(tm(2), Y128, cP, A.is_lt, ["PF"], ["t2"])
+            ts(tm(3), Y128, cG16, A.is_ge, ["PF"], ["t3"])
+        else:
+            tt(T.TRF[:], tm(0), tm(1), A.mult, ["t0", "t1"], ["TRF"])
+            tt(T.TRU[:], tm(2), tm(3), A.mult, ["t2", "t3"], ["TRU"])
+            ac(T.TRB[:], T.TRF[:], ["TRF"], ["TRB"])
+
+    offp = lambda k, c0, c1: T.OPQ[:, 192 * k + c0:192 * k + c1]
+    offq = lambda k, c0, c1: T.OPQ[:, 192 * k + 96 + c0:192 * k + 96 + c1]
+    SBI = T.SAB[:, 24:48]
+    ts(offp(0, 0, 24), T.SAB[:, 0:24], float(b0), A.add, ["SA"], ["OP0"])
+    ts(T.SF[:, 0:24], SBI, 2048.0, A.is_ge, ["SB"], ["s0"], 32.0, A.mult)
+    ts(T.SF[:, 24:48], SBI, 4096.0, A.is_ge, ["SB"], ["s1"], 32.0, A.mult)
+    ts(T.SF[:, 48:72], SBI, float(base(1)), A.add, ["SB"], ["s2"])
+    tt(T.SF[:, 72:96], T.SF[:, 0:24], T.SF[:, 24:48], A.add, ["s0", "s1"], ["s3"])
+    tt(T.SF[:, 0:24], T.SF[:, 72:96], T.SF[:, 48:72], A.add, ["s2", "s3"], ["s4"])
+    cp(offq(0, 0, 24), T.SF[:, 0:24], ["s4"], ["OQ0"])
+    fill(0, "k", (3, 4, 5, 6), ac)
+    fill(0, "c", (0, 1, 2), ac)
+    turn_tree(0)
+    ac(T.WN[:], T.WA[:], WAT, ["WN"], scale=-1.0)
+    ac(T.ZB[:], T.Z[:], ["Z"], ["ZB"], scale=-16384.0)
+
+    def late(t):
+        return topo.chip(T.cores[(rank + t) % n]) != topo.chip(core)
+    for t in (1, 2, 3):
+        if not late(t):
+            fill(t, "k", (3, 4, 5, 6), ac)
+            fill(t, "c", (0, 1, 2), ac)
+            turn_tree(t)
+    far = [t for t in (1, 2, 3) if late(t)]
+    for t in far:
+        fill(t, "k", (3, 4), ac)
+        fill(t, "k", (5, 6), cp)
+    for j, t in enumerate(far):
+        fill(t, "c", (0,) if j == 0 else (0, 1, 2), ac)
+        fill(t, "c", (1, 2) if j == 0 else (), cp)
+        turn_tree(t)
+    ITT = ["IT%d" % t for t in range(4)] + ["ID%d" % t for t in range(4)]
+    TBT = ["T0a", "T0b"] + ["TD%d" % t for t in range(4)]
+    HEXT = [("h%d_%d" % (t, k), ARR) for t in (1, 2, 3) for k in range(NH)]
+    sel = lambda i: T.Z[:, 15 - i:143 - i]
+    sw = lambda zz, x, gg: zz[x][:, 16 - 16 * (gg - x):144 - 16 * (gg - x)]
+
+    def turn(out, in_, c, r, w):
+        op("t", lambda: pe.transpose(out, in_, T.IDF[0:c, 0:c]), r + ["IDF"], w)
+
+    def gather_pq(tab, k, C, r):
+        h = C // 2
+        rp, rq = r + ["OP%d" % k, "OPb%d" % k], r + ["OQ%d" % k, "OQb%d" % k]
+        ac(T.RP[:, 0:16 * h], tab[:, 0:NT].indirect(offp(k, 0, h)), rp, ["RPa"])
+        cp(T.RP[:, 16 * h:16 * C], tab[:, 0:NT].indirect(offp(k, h, C)), rp, ["RPb"])
+        ac(T.RQ[:, 0:16 * h], tab[:, 0:NT].indirect(offq(k, 0, h)), rq, ["RQa"])
+        cp(T.RQ[:, 16 * h:16 * C], tab[:, 0:NT].indirect(offq(k, h, C)), rq, ["RQb"])
+
+    for rn in range(5):
+        C = min(24 << rn, 96)
+        nn = 16 * C
+        press = rn >= 2
+        gather_pq(T.IT, rn, C, ITT)
+        mm(run([(P[0][0:C, i:512:16], T.RP[:, i:nn:16], T.WN[:]) for i in range(16)], True, False), ["RPa", "RPb", "WN"], ["@0"])
+        mm(run([(P[1][0:C, i:384:16], T.RP[:, i:nn:16], T.WA[:, 8:32]) for i in range(16)], True, True), ["RPa", "RPb"] + WAT, ["@1"])
+        mm(run([(P[0][0:C, i:512:16], T.RQ[:, i:nn:16], T.WA[:]) for i in range(16)], False, True), ["RQa", "RQb"], ["@0"])
+        if rn < 3:
+            later(2 * rn)
+        D = P[0][0:C, 0:128]
+        ts(T.MK[0:C, 128:256], D, 0.0, A.is_lt, ["@0"], ["po"])
+        ts(T.MK[0:C, 0:128], D, 0.0, A.is_ge, ["@0"], ["qo"])
+        tt(T.MM[0:C, 256:384], P[0][0:C, 384:512], T.MK[0:C, 128:256], A.mult, ["@0", "po"], ["mX"])
+        tt(T.MM[0:C, 0:128], P[0][0:C, 128:256], T.MK[0:C, 0:128], A.mult, ["@0", "qo"], ["mL"])
+        tt(T.VT[0:C, 256:384], P[1][0:C, 256:384], T.MM[0:C, 256:384], A.add, ["@1", "mX"], ["vX"])
+        turn(P[2][:, 0:C], T.VT[0:C, 256:384], C, ["vX"], ["@2"])
+        tt(T.VT[0:C, 0:128], P[1][0:C, 0:128], T.MM[0:C, 0:128], A.add, ["@1", "mL"], ["vL"])
+        turn(P[3][:, 0:C], T.VT[0:C, 0:128], C, ["vL"], ["@3"])
+        tt(T.MM[0:C, 128:256], P[0][0:C, 256:384], T.MK[0:C, 0:128], A.mult, ["@0", "qo"], ["mR"])
+        cp(T.OV[:, 0:C], P[2][:, 0:C], ["@2"], ["OX"])
+        tt(T.VT[0:C, 128:256], P[1][0:C, 128:256], T.MM[0:C, 128:256], A.add, ["@1", "mR"], ["vR"])
+        turn(P[7][:, 0:C], T.VT[0:C, 128:256], C, ["vR"], ["@7"])
+        cp(T.OV[:, 96:96 + C], P[3][:, 0:C], ["@3"], ["O0"])
+        cp(T.OV[:, 192:192 + C], P[7][:, 0:C], ["@7"], ["O1"])
+        cuts = {24: (0, 8, 24), 48: (0, 12, 48), 96: (0, 12, 42, 96)}[C]
+        nch = len(cuts) - 1
+        for j in range(nch):
+            c0, c1 = cuts[j], cuts[j + 1]
+            ac(T.NX[:, 16 * c0:16 * c1], T.TB[:, 0:NT].indirect(T.OV[:, c0:c1]), TBT + ["OX"], ["NX%d" % j], scale=-1.0,
+               ext=HEXT if rn == 0 and j == 0 else ())
+            if press and j == 1:
+                ac(T.VW[:, 0:96], P[2][:, 0:96], ["@2"], ["VWx"])
+                ac(T.VW[:, 96:192], P[3][:, 0:96], ["@3"], ["VWl"])
+                ac(T.VW[:, 192:288], P[7][:, 0:96], ["@7"], ["VWr"])
+        if press:
+            lst = []
+            for x in (0, 1):
+                lst += grp(P[6][:, x:96:2], [(sw(ZF, x, gg), T.VW[:, gg:96:2]) for gg in (0, 1)])
+                lst += grp(P[6][:, 96 + x:192:2], [(sw(ZF, x, gg), T.VW[:, 96 + gg:192:2]) for gg in (0, 1)])
+                lst += grp(P[6][:, 192 + x:288:2], [(sw(ZF, x, gg), T.VW[:, 192 + gg:288:2]) for gg in (0, 1)]
+                           + [(sw(ZN, x, gg), T.VW[:, 96 + gg:192:2]) for gg in (0, 1)])
+            mm(lst, ["VWx", "VWl", "VWr", "ZF0", "ZF1", "ZN0", "ZN1"], ["@6"])
+            mm([(P[2][:, 0:96], T.IDB[:], T.JH[:], True, False), (P[2][:, 0:96], T.IDB[:], T.JC[:], False, False)],
+               ["IDB", "JH", "JC"], ["@2"])
+            ac(T.PC[:, 0:288], P[6][:, 0:288], ["@6"], ["PCh"])
+            for l, c0 in ((0, 0), (2, 96)):
+                ac(T.SIN[:, l:1536:16], T.PC[:, c0:c0 + 96], ["PCh", "SIN"], ["S%d" % l])
+        else:
+            for side in (0, 1):
+                mm([(P[4 + side][:, 0:C], T.VT[0:C, 128 * side:128 * side + 128], T.IDF[0:C, 0:C], True, False)],
+                   ["vL", "vR"], ["@%d" % (4 + side)])
+        FF = (T.FL, T.FR)
+        for j in range(nch):
+            c0, c1 = cuts[j], cuts[j + 1]
+            for side in (0, 1):
+                o0 = 96 + side * 96
+                tt(FF[side][:, 16 * c0:16 * c1], T.TB[:, 0:NT].indirect(T.OV[:, o0 + c0:o0 + c1]), T.NX[:, 16 * c0:16 * c1], A.is_lt,
+                   TBT + ["O%d" % side, "NX%d" % j], ["F%d%d" % (side, j)], ext=HEXT if rn == 0 and j == 0 and side == 0 else ())
+            if not press and j == 0:
+                for side in (0, 1):
+                    o0 = 192 * (rn + 1) + 96
+                    cp(T.OPQ[:, o0 + side:o0 + 2 * C:2], P[2][:, 0:C], ["@2"], ["OQ%s%d" % ("b" * side, rn + 1)])
+        if not press:
+            later(2 * rn + 1)
+            for side in (0, 1):
+                mm(run([(P[4 + side][:, 0:C], T.ZB[:, 15 - i:143 - i], FF[side][:, i:nn:16]) for i in range(16)], False, True),
+                   ["ZB"] + ["F%d%d" % (side, j) for j in range(nch)], ["@%d" % (4 + side)])
+                o0 = 192 * (rn + 1)
+                cp(T.OPQ[:, o0 + side:o0 + 2 * C:2], P[4 + side][:, 0:C], ["@%d" % (4 + side)], ["OP%s%d" % ("b" * side, rn + 1)])
+            continue
+        tt(T.PC[:, 288:576], P[6][:, 0:288], T.PC[:, 0:288], A.subtract, ["@6", "PCh"], ["PCl"])
+        for l, c0 in ((1, 288), (3, 384)):
+            cp(T.SIN[:, l:1536:16], T.PC[:, c0:c0 + 96], ["PCl", "SIN"], ["S%d" % l])
+        kL, kR = T.KP[:, 0:96], T.KP[:, 96:192]
+
+        def count(side, c0, c1, js):
+            mm(grp(P[4 * side][:, c0:c1], [(sel(i), FF[side][:, 16 * c0 + i:16 * c1:16]) for i in range(16)]),
+               ["Z"] + ["F%d%d" % (side, j) for j in js], ["@%d" % (4 * side)])
+
+        def keep(side):
+            op("a", lambda: act.activation(T.KP[:, 96 * side:96 * side + 96], P[4 * side][:, 0:96], AF.Relu, bias=1.0, scale=-1.0,
+                                           accum_out=T.TOT[:, side:side + 1]), ["@%d" % (4 * side)], ["KP%d" % side])
+
+        def place(side):
+            if rn == 2:
+                lst = [(P[5][:, 0:96], T.IDB[:], kL)] if side == 0 else []
+                for e in range(4):
+                    c0 = 96 * side + e
+                    lst.append((P[5][:, 0:96:4], T.TRB[:], T.KP[:, c0:96 * side + 96:4]))
+                    lst.append((P[5][:, 4:96:4], T.TRU[:], T.KP[:, c0:96 * side + 92:4]))
+            else:
+                lst = [(P[5][:, 0:1], T.TRF[:], T.TOT[:, side:side + 1])]
+            mm(run(lst, side == 0, side == 1), ["KP%d" % side, "TRF", "TRB", "TRU", "IDB"], ["@5"])
+            mm([(P[2][:, 0:96], T.NBG[:], (kL, kR)[side], False, side == 1)], ["KP%d" % side, "NBG"], ["@2"])
+
+        def masks(bank, side, opens, closes):
+            mm(run([(P[bank][:, x:96:2], sw(ZX, x, gg), T.KP[:, 96 * side + gg:96 * side + 96:2]) for x in (0, 1) for gg in (0, 1)],
+                   opens, closes), ["KP%d" % side, "ZX0", "ZX1"], ["@%d" % bank])
+        count(1, 0, cuts[2], (0, 1))
+        count(0, 0, 96, (0, 1, 2))
+        keep(0)
+        place(0)
+        masks(1, 0, True, False)
+        count(1, cuts[2], 96, (2,))
+        keep(1)
+        place(1)
+        masks(1, 1, False, True)
+        masks(3, 1, True, True)
+        if rn == 2:
+            op("v", lambda: vec.tensor_tensor_scan(T.SC[:, 0:96], P[5][:, 0:96], T.KP[:, 96:192], 0.0, A.add, A.add), ["@5", "KP1"], ["SC"])
+        else:
+            op("v", lambda: vec.tensor_tensor_scan(T.SC[:, 0:96], T.KP[:, 0:96], T.KP[:, 96:192], P[5][:, 0:1], A.add, A.add),
+               ["@5", "KP0", "KP1"], ["SC"])
+        prods = ((6, 96, 1), (7, 384, 1), (8, 0, 1), (9, 288, 1), (4, 192, 3), (5, 480, 3))
+        for j, (l, c0, bank) in enumerate(prods):
+            tt(T.SIN[:, l:1536:16], P[bank][:, 0:96], T.PC[:, c0:c0 + 96], A.mult, ["@%d" % bank, "PCh", "PCl", "SIN"], ["S%d" % l])
+            if j == 0:
+                tt(T.SC[:, 96:192], P[2][:, 0:96], T.SC[:, 0:96], A.max, ["@2", "SC"], ["SO"])
+        cp(T.OS[:], T.SC[:, 96:192], ["SO"], ["OS"])
+        op("v", lambda: vec.transpose(T.SRC[:], T.SIN[:]), ["S%d" % l for l in range(10)], ["SRC"])
+        wn = WIN[rn - 2]
+        wt = "W%d" % (rn - 2)
+        cp(wn[:, 0:WINW].indirect(T.OS[:]), T.SRC[:], ["OS", "SRC", wt], [wt])
+        lst = []
+        for i in range(16):
+            lst += grp(P[7][0:96, i:256:16], [(wn[:, 96 * i + 1:96 * i + 97], T.WS[:, 0:16]), (wn[:, 96 * i + 2:96 * i + 98], T.WS[:, 16:32])])
+        mm(lst, [wt] + WST, ["@7"])
+        cp(T.PT[0:96, 0:128], P[7][0:96, 0:128], ["@7"], ["PTp"])
+        turn(P[2][:, 0:96], T.PT[0:96, 0:128], 96, ["PTp"], ["@2"])
+        cp(T.PT[0:96, 128:256], P[7][0:96, 128:256], ["@7"], ["PTq"])
+        turn(P[3][:, 0:96], T.PT[0:96, 128:256], 96, ["PTq"], ["@3"])
+        cp(offp(rn + 1, 0, 96), P[2][:, 0:96], ["@2"], ["OP%d" % (rn + 1)])
+        cp(offq(rn + 1, 0, 96), P[3][:, 0:96], ["@3"], ["OQ%d" % (rn + 1)])
+
+    fi = lambda j: T.FIN[:, 96 * j:96 * j + 96]
+    gather_pq(T.TB, 5, 96, [])
+    mm(run([(P[4][:, 0:96], sel(i), T.RP[:, i:1536:16]) for i in range(16)], True, False), ["RPa", "RPb"], ["@4"])
+    mm(run([(P[4][:, 0:96], sel(i), T.RQ[:, i:1536:16]) for i in range(16)], False, True), ["RQa", "RQb"], ["@4"])
+    ac(fi(0), P[2][:, 0:96], ["@2"], ["pp"])
+    tt(fi(3), P[3][:, 0:96], fi(0), A.max, ["@3", "pp"], ["mx"])
+    tt(fi(2), P[3][:, 0:96], fi(0), A.min, ["@3", "pp"], ["mn"])
+    af(fi(7), fi(2), AF.Sign, 1.0, 0.0, ["mn"], ["ok"])
+    af(fi(8), fi(2), AF.Relu, 1.0, 1.0 - b0, ["mn"], ["f8"])
+    af(T.YO[:, 0:96], fi(8), AF.Identity, 1.0, -1.0, ["f8"], ["YA"])
+    dma("a", T.ya[:], T.YO[:, 0:96], ["YA"], ["oa_"])
+    ts(fi(4), fi(3), float(base(2)), A.is_ge, ["mx"], ["f4"], -32.0, A.mult)
+    ts(fi(5), fi(3), float(base(3)), A.is_ge, ["mx"], ["f5"], -32.0, A.mult)
+    tt(fi(6), fi(3), fi(4), A.add, ["f4"], ["f6"])
+    tt(fi(1), fi(6), fi(5), A.add, ["f6", "f5"], ["f7"])
+    tt(T.YO[:, 192:288], P[4][:, 0:96], fi(7), A.mult, ["@4", "ok"], ["YS"])
+    dma("s", T.ys[:], T.YO[:, 192:288], ["YS"], ["os_"])
+    ts(T.YO[:, 96:192], fi(1), -float(base(1)), A.add, ["f7"], ["YB"], -1.0, A.max)
+    dma("a", T.yb[:], T.YO[:, 96:192], ["YB"], ["ob_"])
+    op("s", None, ["oa_", "ob_", "os_"], (), kind="w")
+    op("g", None, (), (), kind="w", ext=[("ls", ls[0])])
+
+    for o in ops:
+        for j in o["deps"]:
+            ops[j]["need"] = True
+    cnt = {}
+    for o in ops:
+        if o["kind"] == "c" and o["need"]:
+            cnt[o["e"]] = cnt.get(o["e"], 0) + 1
+            o["name"] = "c" + o["e"]
+            o["val"] = cnt[o["e"]]
+        elif o["kind"] == "d":
+            o["val"] = 16
+    seen = {}
+    for o in ops:
+        e = o["e"]
+        want = {}
+        for j in o["deps"]:
+            want[ops[j]["name"]] = max(want.get(ops[j]["name"], 0), ops[j]["val"])
+        for (nm, v) in o["ext"]:
+            want[nm] = max(want.get(nm, 0), v)
+        for nm in sorted(want):
+            if seen.get((e, nm), 0) < want[nm]:
+                Q[e].wait_ge(T.sem[nm], want[nm])
+                seen[(e, nm)] = want[nm]
+        if o["fn"] is None:
+            continue
+        ins = o["fn"]()
+        if o["kind"] == "d":
+            ins.then_inc(T.sem[o["name"]], 16)
+        elif o["kind"] == "c" and o["need"]:
+            ins.then_inc(T.sem[o["name"]], 1)

@@ -7,6 +7,7 @@ PITCH = M + 32
 NT = PITCH * (FAR + 1)
 WINW = 4704
 ZW = 1568
+CA = 56
 HC = (0, 512, 1024, 1536, 2048)
 NH = len(HC) - 1
 REC = {"c": (0, 384), "k": (384, 896)}
@@ -17,38 +18,22 @@ def base(t):
     return 32 + PITCH * t
 
 
-SCRATCH = {
-    "TB": ("sbuf", [128, NT], "bfloat16"), "IT": ("sbuf", [128, NT], "bfloat16"),
-    "IN": ("sbuf", [128, 4 * M], "bfloat16"), "HN": ("sbuf", [128, M], "bfloat16"),
-    "CI": ("sbuf", [128, 4 * 896], "bfloat16"),
-    "W0": ("sbuf", [128, WINW], "bfloat16"), "W1": ("sbuf", [128, WINW], "bfloat16"), "W2": ("sbuf", [128, WINW], "bfloat16"),
-    "RP": ("sbuf", [128, 1536], "bfloat16"), "RQ": ("sbuf", [128, 1536], "bfloat16"), "NX": ("sbuf", [128, 1536], "bfloat16"),
-    "FL": ("sbuf", [128, 1536], "bfloat16"), "FR": ("sbuf", [128, 1536], "bfloat16"),
-    "SIN": ("sbuf", [128, 1536], "bfloat16"), "SRC": ("sbuf", [128, 1536], "bfloat16"),
-    "KI": ("sbuf", [128, 256], "int32"), "KF": ("sbuf", [128, 256], "float32"), "KT": ("sbuf", [128, 256], "float32"),
-    "KLR": ("sbuf", [128, 256], "float32"), "D2": ("sbuf", [128, 256], "float32"), "WK": ("sbuf", [128, 768], "float32"),
-    "SAB": ("sbuf", [128, 48], "int32"), "SF": ("sbuf", [128, 96], "float32"),
-    "Y": ("sbuf", [128, 160], "float32"), "Y16": ("sbuf", [128, 8], "float32"), "B32": ("sbuf", [128, 128], "float32"),
-    "V": ("sbuf", [128, 128], "float32"),
-    "PI": ("sbuf", [128, 8], "int32"), "PJ": ("sbuf", [128, 8], "int32"), "PF": ("sbuf", [128, 16], "float32"),
-    "Z": ("sbuf", [128, 160], "bfloat16"), "ZB": ("sbuf", [128, 160], "bfloat16"),
-    "ZS0": ("sbuf", [128, 160], "bfloat16"), "ZS1": ("sbuf", [128, 160], "bfloat16"),
-    "ZX0": ("sbuf", [128, 160], "bfloat16"), "ZX1": ("sbuf", [128, 160], "bfloat16"),
-    "ZF0": ("sbuf", [128, 160], "float32"), "ZF1": ("sbuf", [128, 160], "float32"),
-    "ZN0": ("sbuf", [128, 160], "float32"), "ZN1": ("sbuf", [128, 160], "float32"),
-    "IDF": ("sbuf", [128, 128], "float32"), "IDB": ("sbuf", [128, 128], "bfloat16"), "NBG": ("sbuf", [128, 128], "bfloat16"),
-    "TRF": ("sbuf", [128, 128], "float32"), "TRB": ("sbuf", [128, 128], "bfloat16"), "TRU": ("sbuf", [128, 128], "bfloat16"),
-    "TMP": ("sbuf", [128, 512], "float32"),
-    "GE": ("sbuf", [128, 24], "float32"), "E8": ("sbuf", [128, 8], "float32"), "RG": ("sbuf", [128, 16], "float32"),
-    "WA": ("sbuf", [128, 32], "bfloat16"), "WN": ("sbuf", [128, 32], "bfloat16"), "WS": ("sbuf", [128, 32], "bfloat16"),
-    "JH": ("sbuf", [128, 96], "bfloat16"), "JC": ("sbuf", [128, 96], "bfloat16"),
-    "OPQ": ("sbuf", [128, 6 * 192], "uint16"), "OV": ("sbuf", [128, 288], "uint16"), "OS": ("sbuf", [128, 96], "uint16"),
-    "MK": ("sbuf", [128, 256], "float32"), "MM": ("sbuf", [128, 384], "float32"), "VT": ("sbuf", [128, 384], "float32"),
-    "VW": ("sbuf", [128, 288], "float32"), "PC": ("sbuf", [128, 576], "bfloat16"),
-    "KP": ("sbuf", [128, 192], "bfloat16"), "TOT": ("sbuf", [128, 8], "float32"),
-    "SC": ("sbuf", [128, 192], "float32"), "PT": ("sbuf", [128, 256], "float32"),
-    "FIN": ("sbuf", [128, 864], "float32"), "YO": ("sbuf", [128, 288], "float32"),
-}
+SCRATCH = {}
+for _n, _w in (("TB", NT), ("IT", NT), ("IN", 4 * M), ("HN", M), ("CI", 4 * 896), ("W0", WINW), ("W1", WINW), ("W2", WINW),
+               ("RP", 1536), ("RQ", 1536), ("NX", 1536), ("FL", 1536), ("FR", 1536), ("SIN", 1536), ("SRC", 1536),
+               ("Z", 160), ("ZB", 160), ("ZS0", 160), ("ZS1", 160), ("ZX0", 160), ("ZX1", 160), ("IDB", 128), ("NIB", 128),
+               ("NBG", 128), ("TRB", 128), ("TRU", 128), ("WA", 32), ("WN", 32), ("WS", 32), ("JH", 96), ("JC", 96),
+               ("PC", 576), ("KP", 192)):
+    SCRATCH[_n] = ("sbuf", [128, _w], "bfloat16")
+for _n, _w in (("KF", 256), ("KT", 256), ("KLR", 256), ("WK", 128), ("SF", 96), ("Y", 160), ("Y16", 8), ("B32", 128),
+               ("V", 128), ("PF", 16), ("ZF0", 160), ("ZF1", 160), ("ZN0", 160), ("ZN1", 160), ("IDF", 128), ("TMP", 512),
+               ("GE", 24), ("E8", 8), ("RG", 16), ("MK", 256), ("MM", 384), ("VT", 384), ("VW", 288), ("SC", 192), ("PT", 256),
+               ("FIN", 864), ("YO", 288)):
+    SCRATCH[_n] = ("sbuf", [128, _w], "float32")
+for _n, _w in (("KI", 256), ("SAB", 48), ("PI", 8), ("PJ", 8)):
+    SCRATCH[_n] = ("sbuf", [128, _w], "int32")
+for _n, _w in (("OPQ", 6 * 192), ("OV", 288), ("OS", 96)):
+    SCRATCH[_n] = ("sbuf", [128, _w], "uint16")
 for _b in range(8):
     SCRATCH["P%d" % _b] = ("psum", [128, 512], "float32")
 
@@ -61,6 +46,8 @@ def routes(T, topo):
     n = len(cores)
     first = {r: [] for r in range(n)}
     relay = {}
+    recs = tuple(k for k in ITEMS if k in REC)
+    bnds = tuple(k for k in ITEMS if k not in REC)
 
     def free(c0, die, ok):
         return [c for c in topo.cores_of(c0) if c not in cores and c not in relay and topo.die(c) == die and ok(c)][0]
@@ -69,22 +56,33 @@ def routes(T, topo):
         cs = cores[s]
         by_chip = {}
         for d in range(1, FAR + 1):
-            r = (s - d) % n
-            by_chip.setdefault(topo.chip(cores[r]), []).append(r)
+            by_chip.setdefault(topo.chip(cores[(s - d) % n]), []).append((cores[(s - d) % n], d))
+        lone = [ch for ch, rs in by_chip.items() if ch != topo.chip(cs) and len(rs) == 1]
+        fan = None
         for ch, rs in by_chip.items():
-            c0 = cores[rs[0]]
             if ch == topo.chip(cs):
-                first[s].append((c0, rs[0], ITEMS))
+                first[s].append(rs[0] + (ITEMS,))
             elif len(rs) > 1:
-                c = free(c0, topo.die(cs), lambda c: topo.may_write(cs, c))
-                relay[c] = (s, rs, ITEMS)
-                first[s].append((c, None, ITEMS))
+                c = free(rs[0][0], topo.die(cs), lambda c: topo.may_write(cs, c))
+                if lone and topo.mates(lone[0], ch):
+                    fan = c
+                relay[c] = (rs, recs + bnds if fan else ITEMS)
+                first[s].append((c, None, recs if fan else ITEMS))
+        for ch in lone:
+            rs = by_chip[ch]
+            c0 = rs[0][0]
+            other = [d for d in set(topo.die(c) for c in topo.cores_of(cs)) if d != topo.die(cs)][0]
+            if fan:
+                c = free(c0, topo.die(cs), lambda c: topo.may_write(c, fan))
+                relay[c] = ([(fan, None)] + rs, bnds)
+                first[s].append((c, None, bnds))
+                split = ((other, recs),)
             else:
-                dies = sorted(set(topo.die(c) for c in topo.cores_of(cs)), key=lambda d: d == topo.die(c0))
-                for d, items in zip(dies, ((0, "c", 2), ("k", 1, 3))):
-                    c = free(cs, d, lambda c: topo.may_write(c, c0))
-                    relay[c] = (s, rs, items)
-                    first[s].append((c, None, items))
+                split = ((topo.die(cs), ITEMS[:-1]), (other, ITEMS[-1:]))
+            for d, items in split:
+                c = free(cs, d, lambda c: topo.may_write(c, c0))
+                relay[c] = (rs, items)
+                first[s].append((c, None, items))
     return first, relay
 
 
@@ -114,14 +112,13 @@ def transfer(T, topo, c, mask, t, k):
     return RemoteDMATransfer(dst_ids=[DstId(rid=a[0], pnc=a[1])], dma_engine_mask=mask, remote_sem=sm, src=staged(T, k), dst=d)
 
 
-def relay_program(g, core, T, topo, s, rs, items):
-    n = len(T.cores)
+def relay_program(g, core, T, topo, dsts, items):
     off = off_mask(T, topo, core)
     tot = 0
     for k in items:
         g.wait_ge(T.sem["hx%s" % k], bits(off))
-        masks = [off if j == 0 else topo.mask(core, T.cores[r]) & ~off for j, r in enumerate(rs)]
-        g.remote_dma_fused([transfer(T, topo, T.cores[r], m, (s - r) % n, k) for r, m in zip(rs, masks)], local_sem=T.sem.ls)
+        masks = [off if j == 0 else topo.mask(core, c) & ~off for j, (c, t) in enumerate(dsts)]
+        g.remote_dma_fused([transfer(T, topo, c, m, t, k) for (c, t), m in zip(dsts, masks)], local_sem=T.sem.ls)
         tot += sum(bits(m) for m in masks)
     g.wait_ge(T.sem.ls, tot)
 
@@ -240,6 +237,7 @@ def rank_program(g, core, T, topo):
     ZS, ZX, ZF, ZN = (T.ZS0, T.ZS1), (T.ZX0, T.ZX1), (T.ZF0, T.ZF1), (T.ZN0, T.ZN1)
     for x in (0, 1):
         ts(ZS[x][:], T.Y[:], col(T.PF, 8 + x), A.is_equal, ["Y", "PF8"], ["ZS%d" % x])
+    ts(T.IDF[:], T.Y[:, 0:128], cP, A.is_equal, ["Y", "PF"], ["IDF"])
 
     lst = []
     for x in (0, 1):
@@ -253,20 +251,20 @@ def rank_program(g, core, T, topo):
             c0 = 128 * side + 16 * sg
             (ac if side else cp)(T.KLR[:, c0:c0 + 16], T.KT[:, 2 * sg + side:256:16], ["KT"], ["K%d%d" % (side, sg)])
     KL, KR = T.KLR[:, 0:128], T.KLR[:, 128:256]
-    wk = lambda j: T.WK[:, 128 * j:128 * j + 128]
     ci = lambda j, k=1, t=0: T.CI[:, 896 * t + 128 * j:896 * t + 128 * (j + k)]
-    ts(wk(2), KL, 0.0, A.is_equal, ["K0%d" % sg for sg in range(8)], ["leaf"])
-    tt(wk(3), wk(2), T.V[:], A.mult, ["leaf", "V"], ["w3"])
-    tt(T.D2[:, 128:256], KR, wk(2), A.subtract, ["leaf"] + ["K1%d" % sg for sg in range(8)], ["D2b"])
-    tt(T.D2[:, 0:128], KL, wk(3), A.add, ["w3"], ["D2a"])
-    af(wk(4), wk(2), AF.Identity, -float(2 ** 22), float(2 ** 21), ["leaf"], ["w4"])
-    cp(ci(3, 2), T.D2[:], ["D2a", "D2b"], ["c3"])
-    tt(ci(5, 2), T.D2[:], ci(3, 2), A.subtract, ["c3"], ["c5"])
-    tt(wk(5), P[0][:, 0:128], wk(4), A.min, ["@0", "w4"], ["key"])
-    cp(ci(0), wk(5), ["key"], ["c0"])
-    tt(wk(0), wk(5), ci(0), A.subtract, ["c0"], ["r1"])
-    cp(ci(1), wk(0), ["r1"], ["c1"])
-    tt(ci(2), wk(0), ci(1), A.subtract, ["c1"], ["c2"])
+    leaf, d2, key, r1 = P[1][:, 0:128], P[2][:, 0:256], P[3][:, 0:128], P[4][:, 0:128]
+    ts(leaf, KL, 0.0, A.is_equal, ["K0%d" % sg for sg in range(8)], ["@1"])
+    tt(P[5][:, 0:128], leaf, T.V[:], A.mult, ["@1", "V"], ["@5"])
+    tt(P[2][:, 128:256], KR, leaf, A.subtract, ["@1"] + ["K1%d" % sg for sg in range(8)], ["@2"])
+    ts(T.WK[:], leaf, -float(2 ** 22), A.mult, ["@1"], ["w4"], float(2 ** 21), A.add)
+    tt(P[2][:, 0:128], P[5][:, 0:128], KL, A.add, ["@5"], ["@2"])
+    tt(key, P[0][:, 0:128], T.WK[:], A.min, ["@0", "w4"], ["@3"])
+    cp(ci(0), key, ["@3"], ["c0"])
+    ac(ci(3, 2), d2, ["@2"], ["c3"])
+    tt(r1, key, ci(0), A.subtract, ["@3", "c0"], ["@4"])
+    tt(ci(5, 2), d2, ci(3, 2), A.subtract, ["@2", "c3"], ["c5"])
+    cp(ci(1), r1, ["@4"], ["c1"])
+    tt(ci(2), r1, ci(1), A.subtract, ["@4", "c1"], ["c2"])
     CIT = {"c": ["c0", "c1", "c2"], "k": ["c3", "c5"]}
 
     ls = [0]
@@ -275,10 +273,10 @@ def rank_program(g, core, T, topo):
 
     def send(k):
         trs = []
-        for (c, r, items) in first[rank]:
+        for (c, t, items) in first[rank]:
             if k in items:
                 m = topo.mask(core, c) & ~offm if topo.chip(c) == topo.chip(core) else topo.mask(core, c)
-                trs.append(transfer(T, topo, c, m, None if r is None else (rank - r) % n, k))
+                trs.append(transfer(T, topo, c, m, t, k))
                 ls[0] += bits(m)
         op("g", lambda: g.remote_dma_fused(trs, local_sem=T.sem.ls), CIT[k] if k in REC else ["HN%d" % k], (), kind="r")
 
@@ -334,7 +332,6 @@ def rank_program(g, core, T, topo):
     ts(col(T.PF, 14), cG16, 15.0, A.add, ["PF"], ["PF14"])
     ranges((3, 9, 0, 1, 2))
     ts(col(T.RG, 12), col(T.RG, 3), col(T.RG, 9), A.add, ["RG3", "RG9"], ["RG12"])
-    ts(T.IDF[:], Y128, cP, A.is_equal, ["PF"], ["IDF"])
     for q, j in enumerate((0, 1, 2, 12)):
         ts(T.WA[:, 8 * q:8 * q + 8], T.E8[:], col(T.RG, j), A.mult, ["E8", "RG%d" % j], ["WA%d" % q], 2.0 if q == 0 else 1.0, A.mult)
     WAT = ["WA%d" % q for q in range(4)]
@@ -359,7 +356,9 @@ def rank_program(g, core, T, topo):
             for x in (0, 1):
                 ac(ZX[x][:], ZF[x][:], ["ZF%d" % x], ["ZX%d" % x])
                 ac(ZN[x][:], ZF[x][:], ["ZF%d" % x], ["ZN%d" % x], scale=-1.0)
+        elif k == 5:
             ac(T.IDB[:], T.IDF[:], ["IDF"], ["IDB"])
+            ac(T.NIB[:], T.IDF[:], ["IDF"], ["NIB"], scale=-1.0)
             ac(T.NBG[:], T.IDF[:], ["IDF"], ["NBG"], scale=-8192.0)
             af(T.JH[:], T.Y[:, 0:96], AF.Identity, 0.0, col(T.PF, 13), ["Y", "PF13"], ["JH"])
             ac(T.JC[:], T.Y[:, 0:96], ["Y"], ["JC"])
@@ -368,9 +367,8 @@ def rank_program(g, core, T, topo):
             ts(tm(2), Y128, cP, A.is_lt, ["PF"], ["t2"])
             ts(tm(3), Y128, cG16, A.is_ge, ["PF"], ["t3"])
         else:
-            tt(T.TRF[:], tm(0), tm(1), A.mult, ["t0", "t1"], ["TRF"])
+            tt(T.TRB[:], tm(0), tm(1), A.mult, ["t0", "t1"], ["TRB"])
             tt(T.TRU[:], tm(2), tm(3), A.mult, ["t2", "t3"], ["TRU"])
-            ac(T.TRB[:], T.TRF[:], ["TRF"], ["TRB"])
 
     offp = lambda k, c0, c1: T.OPQ[:, 192 * k + c0:192 * k + c1]
     offq = lambda k, c0, c1: T.OPQ[:, 192 * k + 96 + c0:192 * k + 96 + c1]
@@ -387,6 +385,20 @@ def rank_program(g, core, T, topo):
     turn_tree(0)
     ac(T.WN[:], T.WA[:], WAT, ["WN"], scale=-1.0)
     ac(T.ZB[:], T.Z[:], ["Z"], ["ZB"], scale=-16384.0)
+
+    def gather(out, nm, win, k, C, r):
+        h = C // 2 + (2 if C == 96 else 0)
+        off = offp if nm == "P" else offq
+        r = r + ["O%s%d" % (nm, k), "O%sb%d" % (nm, k)]
+        ac(out[:, 0:16 * h], win.indirect(off(k, 0, h)), r, ["R%sa" % nm])
+        cp(out[:, 16 * h:16 * C], win.indirect(off(k, h, C)), r, ["R%sb" % nm])
+
+    def p_terms(C):
+        mm(run([(P[1][0:C, i:384:16], T.RP[:, i:16 * C:16], T.WA[:, 8:32]) for i in range(16)], True, True), ["RPa", "RPb"] + WAT, ["@1"])
+        mm(run([(P[0][0:C, i:512:16], T.RP[:, i:16 * C:16], T.WN[:]) for i in range(16)], True, False), ["RPa", "RPb", "WN"], ["@0"])
+
+    gather(T.RP, "P", T.IT[:, 0:PITCH], 0, 24, ["IT0", "ID0"])
+    p_terms(24)
 
     def late(t):
         return topo.chip(T.cores[(rank + t) % n]) != topo.chip(core)
@@ -412,141 +424,146 @@ def rank_program(g, core, T, topo):
     def turn(out, in_, c, r, w):
         op("t", lambda: pe.transpose(out, in_, T.IDF[0:c, 0:c]), r + ["IDF"], w)
 
-    def gather_pq(tab, k, C, r):
-        h = C // 2
-        rp, rq = r + ["OP%d" % k, "OPb%d" % k], r + ["OQ%d" % k, "OQb%d" % k]
-        ac(T.RP[:, 0:16 * h], tab[:, 0:NT].indirect(offp(k, 0, h)), rp, ["RPa"])
-        cp(T.RP[:, 16 * h:16 * C], tab[:, 0:NT].indirect(offp(k, h, C)), rp, ["RPb"])
-        ac(T.RQ[:, 0:16 * h], tab[:, 0:NT].indirect(offq(k, 0, h)), rq, ["RQa"])
-        cp(T.RQ[:, 16 * h:16 * C], tab[:, 0:NT].indirect(offq(k, h, C)), rq, ["RQb"])
-
     for rn in range(5):
         C = min(24 << rn, 96)
         nn = 16 * C
         press = rn >= 2
-        gather_pq(T.IT, rn, C, ITT)
-        mm(run([(P[0][0:C, i:512:16], T.RP[:, i:nn:16], T.WN[:]) for i in range(16)], True, False), ["RPa", "RPb", "WN"], ["@0"])
-        mm(run([(P[1][0:C, i:384:16], T.RP[:, i:nn:16], T.WA[:, 8:32]) for i in range(16)], True, True), ["RPa", "RPb"] + WAT, ["@1"])
+        if rn:
+            gather(T.RP, "P", T.IT[:, 0:NT], rn, C, ITT)
+            p_terms(C)
+        gather(T.RQ, "Q", T.IT[:, 0:NT], rn, C, ITT)
+        ac(T.VT[0:C, :], P[1][0:C, 0:384], ["@1"], ["VT"])
         mm(run([(P[0][0:C, i:512:16], T.RQ[:, i:nn:16], T.WA[:]) for i in range(16)], False, True), ["RQa", "RQb"], ["@0"])
+        idc = T.IDF[0:C, 0:C]
+        banks = ((2, 2), (3, 0), (7, 1)) + (() if press else ((4, 0), (5, 1)))
+        for (b, q) in banks:
+            mm([(P[b][:, 0:C], T.VT[0:C, 128 * q:128 * q + 128], idc, True, False)], ["VT", "IDF"], ["@%d" % b])
+
+        def add_turn(b, q):
+            mm([(P[b][:, 0:C], T.MM[0:C, 128 * q:128 * q + 128], idc, False, b not in (4, 5))], ["m%d" % q], ["@%d" % b])
         if rn < 3:
             later(2 * rn)
         D = P[0][0:C, 0:128]
         ts(T.MK[0:C, 128:256], D, 0.0, A.is_lt, ["@0"], ["po"])
         ts(T.MK[0:C, 0:128], D, 0.0, A.is_ge, ["@0"], ["qo"])
-        tt(T.MM[0:C, 256:384], P[0][0:C, 384:512], T.MK[0:C, 128:256], A.mult, ["@0", "po"], ["mX"])
-        tt(T.MM[0:C, 0:128], P[0][0:C, 128:256], T.MK[0:C, 0:128], A.mult, ["@0", "qo"], ["mL"])
-        tt(T.VT[0:C, 256:384], P[1][0:C, 256:384], T.MM[0:C, 256:384], A.add, ["@1", "mX"], ["vX"])
-        turn(P[2][:, 0:C], T.VT[0:C, 256:384], C, ["vX"], ["@2"])
-        tt(T.VT[0:C, 0:128], P[1][0:C, 0:128], T.MM[0:C, 0:128], A.add, ["@1", "mL"], ["vL"])
-        turn(P[3][:, 0:C], T.VT[0:C, 0:128], C, ["vL"], ["@3"])
-        tt(T.MM[0:C, 128:256], P[0][0:C, 256:384], T.MK[0:C, 0:128], A.mult, ["@0", "qo"], ["mR"])
+        tt(T.MM[0:C, 256:384], P[0][0:C, 384:512], T.MK[0:C, 128:256], A.mult, ["@0", "po"], ["m2"])
+        add_turn(2, 2)
+        tt(T.MM[0:C, 0:128], P[0][0:C, 128:256], T.MK[0:C, 0:128], A.mult, ["@0", "qo"], ["m0"])
+        add_turn(3, 0)
+        tt(T.MM[0:C, 128:256], P[0][0:C, 256:384], T.MK[0:C, 0:128], A.mult, ["@0", "qo"], ["m1"])
+        add_turn(7, 1)
+        if not press:
+            add_turn(4, 0)
+            add_turn(5, 1)
         cp(T.OV[:, 0:C], P[2][:, 0:C], ["@2"], ["OX"])
-        tt(T.VT[0:C, 128:256], P[1][0:C, 128:256], T.MM[0:C, 128:256], A.add, ["@1", "mR"], ["vR"])
-        turn(P[7][:, 0:C], T.VT[0:C, 128:256], C, ["vR"], ["@7"])
         cp(T.OV[:, 96:96 + C], P[3][:, 0:C], ["@3"], ["O0"])
         cp(T.OV[:, 192:192 + C], P[7][:, 0:C], ["@7"], ["O1"])
-        cuts = {24: (0, 8, 24), 48: (0, 12, 48), 96: (0, 12, 42, 96)}[C]
+        cuts = {24: (0, 8, 24), 48: (0, 12, 48), 96: (0, 16, 36, 64)}[C]
         nch = len(cuts) - 1
         for j in range(nch):
             c0, c1 = cuts[j], cuts[j + 1]
             ac(T.NX[:, 16 * c0:16 * c1], T.TB[:, 0:NT].indirect(T.OV[:, c0:c1]), TBT + ["OX"], ["NX%d" % j], scale=-1.0,
                ext=HEXT if rn == 0 and j == 0 else ())
-            if press and j == 1:
+            if press and j == 0:
                 ac(T.VW[:, 0:96], P[2][:, 0:96], ["@2"], ["VWx"])
                 ac(T.VW[:, 96:192], P[3][:, 0:96], ["@3"], ["VWl"])
                 ac(T.VW[:, 192:288], P[7][:, 0:96], ["@7"], ["VWr"])
         if press:
-            lst = []
-            for x in (0, 1):
-                lst += grp(P[6][:, x:96:2], [(sw(ZF, x, gg), T.VW[:, gg:96:2]) for gg in (0, 1)])
-                lst += grp(P[6][:, 96 + x:192:2], [(sw(ZF, x, gg), T.VW[:, 96 + gg:192:2]) for gg in (0, 1)])
-                lst += grp(P[6][:, 192 + x:288:2], [(sw(ZF, x, gg), T.VW[:, 192 + gg:288:2]) for gg in (0, 1)]
-                           + [(sw(ZN, x, gg), T.VW[:, 96 + gg:192:2]) for gg in (0, 1)])
-            mm(lst, ["VWx", "VWl", "VWr", "ZF0", "ZF1", "ZN0", "ZN1"], ["@6"])
-            mm([(P[2][:, 0:96], T.IDB[:], T.JH[:], True, False), (P[2][:, 0:96], T.IDB[:], T.JC[:], False, False)],
-               ["IDB", "JH", "JC"], ["@2"])
+            lst = [(P[6][:, x:288:2], sw(ZF, x, gg), T.VW[:, gg:288:2]) for x in (0, 1) for gg in (0, 1)]
+            lst += [(P[6][:, 192 + x:288:2], sw(ZN, x, gg), T.VW[:, 96 + gg:192:2]) for x in (0, 1) for gg in (0, 1)]
+            mm(run(lst, True, True), ["VWx", "VWl", "VWr", "ZF0", "ZF1", "ZN0", "ZN1"], ["@6"])
+            ac(T.NX[:, 1024:1536], T.TB[:, 0:NT].indirect(T.OV[:, 64:96]), ["OX"], ["NXB"], scale=-1.0)
             ac(T.PC[:, 0:288], P[6][:, 0:288], ["@6"], ["PCh"])
             for l, c0 in ((0, 0), (2, 96)):
                 ac(T.SIN[:, l:1536:16], T.PC[:, c0:c0 + 96], ["PCh", "SIN"], ["S%d" % l])
-        else:
-            for side in (0, 1):
-                mm([(P[4 + side][:, 0:C], T.VT[0:C, 128 * side:128 * side + 128], T.IDF[0:C, 0:C], True, False)],
-                   ["vL", "vR"], ["@%d" % (4 + side)])
         FF = (T.FL, T.FR)
+
+        def test(side, c0, c1, r, w, ext=()):
+            o0 = 96 + side * 96
+            tt(FF[side][:, 16 * c0:16 * c1], T.TB[:, 0:NT].indirect(T.OV[:, o0 + c0:o0 + c1]), T.NX[:, 16 * c0:16 * c1], A.is_lt,
+               TBT + ["O%d" % side, r], [w], ext=ext)
         for j in range(nch):
-            c0, c1 = cuts[j], cuts[j + 1]
             for side in (0, 1):
-                o0 = 96 + side * 96
-                tt(FF[side][:, 16 * c0:16 * c1], T.TB[:, 0:NT].indirect(T.OV[:, o0 + c0:o0 + c1]), T.NX[:, 16 * c0:16 * c1], A.is_lt,
-                   TBT + ["O%d" % side, "NX%d" % j], ["F%d%d" % (side, j)], ext=HEXT if rn == 0 and j == 0 and side == 0 else ())
+                test(side, cuts[j], min(cuts[j + 1], CA), "NX%d" % j, "F%d%d" % (side, j), HEXT if rn == 0 and j == 0 and side == 0 else ())
             if not press and j == 0:
                 for side in (0, 1):
                     o0 = 192 * (rn + 1) + 96
                     cp(T.OPQ[:, o0 + side:o0 + 2 * C:2], P[2][:, 0:C], ["@2"], ["OQ%s%d" % ("b" * side, rn + 1)])
         if not press:
             later(2 * rn + 1)
+            if rn == 0:
+                later(5)
             for side in (0, 1):
                 mm(run([(P[4 + side][:, 0:C], T.ZB[:, 15 - i:143 - i], FF[side][:, i:nn:16]) for i in range(16)], False, True),
                    ["ZB"] + ["F%d%d" % (side, j) for j in range(nch)], ["@%d" % (4 + side)])
                 o0 = 192 * (rn + 1)
                 cp(T.OPQ[:, o0 + side:o0 + 2 * C:2], P[4 + side][:, 0:C], ["@%d" % (4 + side)], ["OP%s%d" % ("b" * side, rn + 1)])
             continue
+        for side in (0, 1):
+            test(side, CA, 64, "NX%d" % (nch - 1), "FC%d" % side)
         tt(T.PC[:, 288:576], P[6][:, 0:288], T.PC[:, 0:288], A.subtract, ["@6", "PCh"], ["PCl"])
         for l, c0 in ((1, 288), (3, 384)):
             cp(T.SIN[:, l:1536:16], T.PC[:, c0:c0 + 96], ["PCl", "SIN"], ["S%d" % l])
-        kL, kR = T.KP[:, 0:96], T.KP[:, 96:192]
-
-        def count(side, c0, c1, js):
-            mm(grp(P[4 * side][:, c0:c1], [(sel(i), FF[side][:, 16 * c0 + i:16 * c1:16]) for i in range(16)]),
-               ["Z"] + ["F%d%d" % (side, j) for j in js], ["@%d" % (4 * side)])
-
-        def keep(side):
-            op("a", lambda: act.activation(T.KP[:, 96 * side:96 * side + 96], P[4 * side][:, 0:96], AF.Relu, bias=1.0, scale=-1.0,
-                                           accum_out=T.TOT[:, side:side + 1]), ["@%d" % (4 * side)], ["KP%d" % side])
-
-        def place(side):
-            if rn == 2:
-                lst = [(P[5][:, 0:96], T.IDB[:], kL)] if side == 0 else []
-                for e in range(4):
-                    c0 = 96 * side + e
-                    lst.append((P[5][:, 0:96:4], T.TRB[:], T.KP[:, c0:96 * side + 96:4]))
-                    lst.append((P[5][:, 4:96:4], T.TRU[:], T.KP[:, c0:96 * side + 92:4]))
-            else:
-                lst = [(P[5][:, 0:1], T.TRF[:], T.TOT[:, side:side + 1])]
-            mm(run(lst, side == 0, side == 1), ["KP%d" % side, "TRF", "TRB", "TRU", "IDB"], ["@5"])
-            mm([(P[2][:, 0:96], T.NBG[:], (kL, kR)[side], False, side == 1)], ["KP%d" % side, "NBG"], ["@2"])
-
-        def masks(bank, side, opens, closes):
-            mm(run([(P[bank][:, x:96:2], sw(ZX, x, gg), T.KP[:, 96 * side + gg:96 * side + 96:2]) for x in (0, 1) for gg in (0, 1)],
-                   opens, closes), ["KP%d" % side, "ZX0", "ZX1"], ["@%d" % bank])
-        count(1, 0, cuts[2], (0, 1))
-        count(0, 0, 96, (0, 1, 2))
-        keep(0)
-        place(0)
-        masks(1, 0, True, False)
-        count(1, cuts[2], 96, (2,))
-        keep(1)
-        place(1)
-        masks(1, 1, False, True)
-        masks(3, 1, True, True)
-        if rn == 2:
-            op("v", lambda: vec.tensor_tensor_scan(T.SC[:, 0:96], P[5][:, 0:96], T.KP[:, 96:192], 0.0, A.add, A.add), ["@5", "KP1"], ["SC"])
-        else:
-            op("v", lambda: vec.tensor_tensor_scan(T.SC[:, 0:96], T.KP[:, 0:96], T.KP[:, 96:192], P[5][:, 0:1], A.add, A.add),
-               ["@5", "KP0", "KP1"], ["SC"])
-        prods = ((6, 96, 1), (7, 384, 1), (8, 0, 1), (9, 288, 1), (4, 192, 3), (5, 480, 3))
-        for j, (l, c0, bank) in enumerate(prods):
-            tt(T.SIN[:, l:1536:16], P[bank][:, 0:96], T.PC[:, c0:c0 + 96], A.mult, ["@%d" % bank, "PCh", "PCl", "SIN"], ["S%d" % l])
-            if j == 0:
-                tt(T.SC[:, 96:192], P[2][:, 0:96], T.SC[:, 0:96], A.max, ["@2", "SC"], ["SO"])
-        cp(T.OS[:], T.SC[:, 96:192], ["SO"], ["OS"])
-        op("v", lambda: vec.transpose(T.SRC[:], T.SIN[:]), ["S%d" % l for l in range(10)], ["SRC"])
         wn = WIN[rn - 2]
         wt = "W%d" % (rn - 2)
-        cp(wn[:, 0:WINW].indirect(T.OS[:]), T.SRC[:], ["OS", "SRC", wt], [wt])
+        E = 4 if rn == 2 else 1
+
+        def kp(side, c0, c1, st=1):
+            return T.KP[:, 96 * side + c0:96 * side + c1:st]
+
+        def count(side, c0, c1, r):
+            b = 4 * side
+            mm(grp(P[b][:, c0:c1], [(sel(i), FF[side][:, 16 * c0 + i:16 * c1:16]) for i in range(16)]), ["Z"] + r, ["@%d" % b])
+            af(kp(side, c0, c1), P[b][:, c0:c1], AF.Relu, -1.0, 1.0, ["@%d" % b], ["KP%d%d" % (side, c0)])
+
+        def places(c0, c1):
+            kt = ["KP%d%d" % (sd, c) for sd in (0, 1) for c in (0, c0)]
+            u0 = max(c0, E)
+            lst = [(P[5][:, c0:c1], T.IDB[:], kp(0, c0, c1))]
+            for side in (0, 1):
+                for e in range(E):
+                    lst.append((P[5][:, c0:c1:E], T.TRB[:], kp(side, c0 + e, c1, E)))
+                    lst.append((P[5][:, u0:c1:E], T.TRU[:], kp(side, u0 - E + e, c1 - E, E)))
+            mm(run(lst, True, True), kt + ["TRB", "TRU", "IDB"], ["@5"])
+            for bank, sides in ((1, (0, 1)), (3, (1,))):
+                mm(run([(P[bank][:, c0 + x:c1:2], sw(ZX, x, gg), kp(sd, c0 + gg, c1, 2)) for sd in sides for x in (0, 1) for gg in (0, 1)],
+                       True, True), kt + ["ZX0", "ZX1"], ["@%d" % bank])
+                if bank == 1:
+                    mm(grp(P[2][:, c0:c1], [(T.IDB[:], T.JH[:, c0:c1]), (T.IDB[:], T.JC[:, c0:c1]), (T.NBG[:], kp(0, c0, c1)),
+                                            (T.NBG[:], kp(1, c0, c1))]), kt + ["NBG", "JH", "JC"], ["@2"])
+
+        def scatter(c0, c1):
+            init = T.SC[:, c0 - 1:c0] if c0 else 0.0
+            op("v", lambda: vec.tensor_tensor_scan(T.SC[:, c0:c1], P[5][:, c0:c1], kp(1, c0, c1), init, A.add, A.add),
+               ["@5", "KP1%d" % c0] + (["SC0"] if c0 else []), ["SC%d" % c0])
+            prods = ((6, 96, 1), (7, 384, 1), (8, 0, 1), (9, 288, 1), (4, 192, 3), (5, 480, 3))
+            for j, (l, p0, bank) in enumerate(prods):
+                tt(T.SIN[:, 16 * c0 + l:16 * c1:16], P[bank][:, c0:c1], T.PC[:, p0 + c0:p0 + c1], A.mult,
+                   ["@%d" % bank, "PCh", "PCl", "SIN"], ["S%d_%d" % (l, c0)])
+                if j == 1:
+                    tt(T.SC[:, 96 + c0:96 + c1], P[2][:, c0:c1], T.SC[:, c0:c1], A.max, ["@2", "SC%d" % c0], ["SO%d" % c0])
+            cp(T.OS[:, c0:c1], T.SC[:, 96 + c0:96 + c1], ["SO%d" % c0], ["OS%d" % c0])
+            op("v", lambda: vec.transpose(T.SRC[:, 16 * c0:16 * c1], T.SIN[:, 16 * c0:16 * c1]),
+               ["S0", "S1", "S2", "S3"] + ["S%d_%d" % (l, c0) for l in range(4, 10)], ["SRC%d" % c0])
+            cp(wn[:, 0:WINW].indirect(T.OS[:, c0:c1]), T.SRC[:, 16 * c0:16 * c1], ["OS%d" % c0, "SRC%d" % c0, wt], [wt])
+        for side in (0, 1):
+            count(side, 0, CA, ["F%d%d" % (side, j) for j in range(nch)])
+        places(0, CA)
+        for side, raw, nm, b in ((0, T.RP, "RP", 7), (1, T.RQ, "RQ", 6)):
+            o0 = 96 + 96 * side
+            ac(raw[:, 0:512], T.TB[:, 0:NT].indirect(T.OV[:, o0 + 64:o0 + 96]), ["O%d" % side], [nm + "a", nm + "b"])
+            mm(grp(P[b][:, 0:512], [(T.IDB[:], raw[:, 0:512]), (T.NIB[:], T.NX[:, 1024:1536])]), [nm + "a", "NXB", "NIB"], ["@%d" % b])
+        for side, b in ((0, 7), (1, 6)):
+            af(FF[side][:, 1024:1536], P[b][:, 0:512], AF.Relu, -1.0, 0.0, ["@%d" % b], ["FB%d" % side])
+        scatter(0, CA)
+        for side in (0, 1):
+            count(side, CA, 96, ["FB%d" % side, "FC%d" % side])
+        places(CA, 96)
+        scatter(CA, 96)
         lst = []
         for i in range(16):
-            lst += grp(P[7][0:96, i:256:16], [(wn[:, 96 * i + 1:96 * i + 97], T.WS[:, 0:16]), (wn[:, 96 * i + 2:96 * i + 98], T.WS[:, 16:32])])
+            sl = (lambda d: wn[:, 96 * i + d:96 * i + d + 96]) if rn == 4 else (lambda d: wn[:, i + d:i + d + 1536:16])
+            lst += grp(P[7][0:96, i:256:16], [(sl(1), T.WS[:, 0:16]), (sl(2), T.WS[:, 16:32])])
         mm(lst, [wt] + WST, ["@7"])
         cp(T.PT[0:96, 0:128], P[7][0:96, 0:128], ["@7"], ["PTp"])
         turn(P[2][:, 0:96], T.PT[0:96, 0:128], 96, ["PTp"], ["@2"])
@@ -556,7 +573,8 @@ def rank_program(g, core, T, topo):
         cp(offq(rn + 1, 0, 96), P[3][:, 0:96], ["@3"], ["OQ%d" % (rn + 1)])
 
     fi = lambda j: T.FIN[:, 96 * j:96 * j + 96]
-    gather_pq(T.TB, 5, 96, [])
+    gather(T.RP, "P", T.TB[:, 0:NT], 5, 96, [])
+    gather(T.RQ, "Q", T.TB[:, 0:NT], 5, 96, [])
     mm(run([(P[4][:, 0:96], sel(i), T.RP[:, i:1536:16]) for i in range(16)], True, False), ["RPa", "RPb"], ["@4"])
     mm(run([(P[4][:, 0:96], sel(i), T.RQ[:, i:1536:16]) for i in range(16)], False, True), ["RQa", "RQb"], ["@4"])
     ac(fi(0), P[2][:, 0:96], ["@2"], ["pp"])

@@ -3,95 +3,88 @@ from concourse.mybir import AluOpType as A, ActivationFunctionType as AF
 
 M = 2048
 FAR = 3
-PITCH = M + 32
-NT = PITCH * (FAR + 1)
+NT = 32 + M * (FAR + 1)
+BIG = 16384
 WINW = 4704
 ZW = 1568
-CA = 56
-HC = (0, 512, 1024, 1536, 2048)
-NH = len(HC) - 1
+LOADS = (0, 512, 1152, 1664, 2048)
+HC = (0, 256, 512, 1152, 1664, 2048)
 REC = {"c": (0, 384), "k": (384, 896)}
-ITEMS = (0, "k", "c", 1, 2, 3)
+ITEMS = (0, "k", "c", 1, 2, 3, 4)
+HELD = (0, 1, 4, 2, 3)
+STREAM = (0, "k", "c")
+CALLS = ((0, 1), (2,), ("k", 3), ("c", 4))
+PLANE = {False: (1, 2, 3, 4), True: (1, 2, 3)}
+OWN_DIE = (0, "k", "c", 3)
+PARTS = {3: (48, 72, 96), 4: (44, 64, 96), 5: (44, 64, 96)}
+PIECES = {1: ((0, 24),), 2: ((0, 48),), 3: ((0, 96),), 4: ((0, 96),), 5: ((0, 96),)}
+SHARE = {2: (16, 24), 3: (64, 32)}
+FIRST, NEAR_STEP, FAR_STEP = 8, 20, 32
+APART = (7, 0, 2, 3)
+CYCLE, PE_CYCLE, GATHER, SCATTER, CALL, HOP, PE_HOP, SLACK = 0.83e-3, 0.36e-3, 1.5, 3.5, 0.02, 0.21, -0.03, 0.02
+DUE, NEAR = {"k": 9.0, "c": 10.0, "h": 13.0}, 2.0
 
 
 def base(t):
-    return 32 + PITCH * t
+    return 32 + M * t
 
 
 SCRATCH = {}
 for _n, _w in (("TB", NT), ("IT", NT), ("IN", 4 * M), ("HN", M), ("CI", 4 * 896), ("W0", WINW), ("W1", WINW), ("W2", WINW),
                ("RP", 1536), ("RQ", 1536), ("NX", 1536), ("FL", 1536), ("FR", 1536), ("SIN", 1536), ("SRC", 1536),
-               ("Z", 160), ("ZB", 160), ("ZS0", 160), ("ZS1", 160), ("ZX0", 160), ("ZX1", 160), ("IDB", 128), ("NIB", 128),
-               ("NBG", 128), ("TRB", 128), ("TRU", 128), ("WA", 32), ("WN", 32), ("WS", 32), ("JH", 96), ("JC", 96),
-               ("PC", 576), ("KP", 192)):
+               ("NXS", 1152), ("FS", 2304), ("RW", 2048), ("CN", 144),
+               ("Z", 160), ("ZS0", 160), ("ZS1", 160), ("ZX0", 160), ("ZX1", 160), ("IDB", 128), ("NIB", 128),
+               ("NBG", 128), ("TRB", 128), ("TRU", 128), ("TRI", 128), ("WA", 32), ("WN", 32), ("WS", 40), ("WB", 48), ("ONB", 160),
+               ("JH", 96), ("JC", 96), ("KP", 192)):
     SCRATCH[_n] = ("sbuf", [128, _w], "bfloat16")
-for _n, _w in (("KF", 256), ("KT", 256), ("KLR", 256), ("WK", 128), ("SF", 96), ("Y", 160), ("Y16", 8), ("B32", 128),
-               ("V", 128), ("PF", 16), ("ZF0", 160), ("ZF1", 160), ("ZN0", 160), ("ZN1", 160), ("IDF", 128), ("TMP", 512),
-               ("GE", 24), ("E8", 8), ("RG", 16), ("MK", 256), ("MM", 384), ("VT", 384), ("VW", 288), ("SC", 192), ("PT", 256),
-               ("FIN", 864), ("YO", 288)):
+for _n, _w in (("KF", 256), ("KT", 256), ("KLR", 256), ("WK", 128), ("K7", 128), ("SF", 24), ("YZ", 160), ("ONF", 160), ("B32", 128),
+               ("V", 128), ("PF", 4), ("ZF0", 160), ("ZF1", 160), ("IDF", 128), ("MK", 128), ("MM", 384), ("VT", 256),
+               ("VW", 288), ("SC", 192), ("PT", 640), ("XF", 64), ("FIN", 288), ("YO", 288), ("SEL", 240)):
     SCRATCH[_n] = ("sbuf", [128, _w], "float32")
-for _n, _w in (("KI", 256), ("SAB", 48), ("PI", 8), ("PJ", 8)):
+for _n, _w in (("KI", 256), ("SAB", 48), ("PI", 2), ("PJ", 2)):
     SCRATCH[_n] = ("sbuf", [128, _w], "int32")
-for _n, _w in (("OPQ", 6 * 192), ("OV", 288), ("OS", 96)):
+for _n, _w in (("OPQ", 4 * 192), ("OV", 5 * 288), ("OS", 96)):
     SCRATCH[_n] = ("sbuf", [128, _w], "uint16")
 for _b in range(8):
     SCRATCH["P%d" % _b] = ("psum", [128, 512], "float32")
 
-SEMAPHORES = (["cg", "cv", "ca", "ct", "ls", "hxc", "hxk"] + ["hx%d" % k for k in range(NH)] + ["d%d" % i for i in range(14)]
-              + ["h%d_%d" % (t, k) for t in (1, 2, 3) for k in range(NH)] + ["%si%d" % (k, t) for t in (1, 2, 3) for k in "ck"])
+SEMAPHORES = ["cg", "cv", "ca", "ct", "ls"] + ["d%d" % i for i in range(14)] + ["x%s_%d" % (k, s) for k in ITEMS for s in range(FAR + 1)]
 
 
 def routes(T, topo):
     cores = list(T.cores)
     n = len(cores)
-    first = {r: [] for r in range(n)}
-    relay = {}
-    recs = tuple(k for k in ITEMS if k in REC)
-    bnds = tuple(k for k in ITEMS if k not in REC)
+    sends = {c: (s, []) for s, c in enumerate(cores)}
 
-    def free(c0, die, ok):
-        return [c for c in topo.cores_of(c0) if c not in cores and c not in relay and topo.die(c) == die and ok(c)][0]
+    but = lambda items: tuple(k for k in ITEMS if k not in items)
+
+    def relay(s, c0, die, to, items):
+        c = [c for c in topo.cores_of(c0) if c not in sends and topo.die(c) == die and all(topo.may_write(c, x[0]) for x in to)][0]
+        sends[c] = (s, to)
+        sends[cores[s]][1].append((c, None, items))
+        return c
 
     for s in range(n):
-        cs = cores[s]
+        cs, die = cores[s], topo.die(cores[s])
+        other = [d for d in set(topo.die(c) for c in topo.cores_of(cs)) if d != die][0]
         by_chip = {}
         for d in range(1, FAR + 1):
             by_chip.setdefault(topo.chip(cores[(s - d) % n]), []).append((cores[(s - d) % n], d))
-        lone = [ch for ch, rs in by_chip.items() if ch != topo.chip(cs) and len(rs) == 1]
-        fan = None
-        for ch, rs in by_chip.items():
-            if ch == topo.chip(cs):
-                first[s].append(rs[0] + (ITEMS,))
-            elif len(rs) > 1:
-                c = free(rs[0][0], topo.die(cs), lambda c: topo.may_write(cs, c))
-                if lone and topo.mates(lone[0], ch):
-                    fan = c
-                relay[c] = (rs, recs + bnds if fan else ITEMS)
-                first[s].append((c, None, recs if fan else ITEMS))
-        for ch in lone:
-            rs = by_chip[ch]
-            c0 = rs[0][0]
-            other = [d for d in set(topo.die(c) for c in topo.cores_of(cs)) if d != topo.die(cs)][0]
-            if fan:
-                c = free(c0, topo.die(cs), lambda c: topo.may_write(c, fan))
-                relay[c] = ([(fan, None)] + rs, bnds)
-                first[s].append((c, None, bnds))
-                split = ((other, recs),)
-            else:
-                split = ((topo.die(cs), ITEMS[:-1]), (other, ITEMS[-1:]))
-            for d, items in split:
-                c = free(cs, d, lambda c: topo.may_write(c, c0))
-                relay[c] = (rs, items)
-                first[s].append((c, None, items))
-    return first, relay
-
-
-def bits(m):
-    return bin(m).count("1")
-
-
-def off_mask(T, topo, c):
-    return topo.mask(c, [x for x in T.cores if topo.chip(x) != topo.chip(c)][0])
+        pair = [rs for rs in by_chip.values() if len(rs) > 1][0]
+        one = [rs[0] for rs in by_chip.values() if len(rs) == 1][0]
+        home = topo.chip(one[0]) == topo.chip(cs)
+        far = not topo.mates(topo.chip(cs), topo.chip(pair[0][0]))
+        plane = PLANE[home] if far else ()
+        fan = relay(s, pair[0][0], die, [r + (ITEMS,) for r in pair], but(plane))
+        if far:
+            c0 = [c for c in cores if topo.mates(topo.chip(c), topo.chip(fan))][0]
+            relay(s, c0, die, [(fan, None, plane)] + ([] if home else [one + (plane,)]), plane)
+        if home:
+            sends[cs][1].append(one + (ITEMS,))
+        else:
+            for d, items in ((other, but(plane)),) if far else ((die, OWN_DIE), (other, but(OWN_DIE))):
+                relay(s, cs, d, [one + (items,)], items)
+    return sends
 
 
 def staged(T, k):
@@ -100,57 +93,83 @@ def staged(T, k):
 
 def landing(T, t, k):
     if t is None:
-        return staged(T, k), T.sem["hx%s" % k]
+        return staged(T, k)
     if k in REC:
-        return T.CI[:, 896 * t + REC[k][0]:896 * t + REC[k][1]], T.sem["%si%d" % (k, t)]
-    return T.TB[:, base(t) + HC[k]:base(t) + HC[k + 1]], T.sem["h%d_%d" % (t, k)]
+        return T.CI[:, 896 * t + REC[k][0]:896 * t + REC[k][1]]
+    return T.TB[:, base(t) + HC[k]:base(t) + HC[k + 1]]
 
 
-def transfer(T, topo, c, mask, t, k):
-    a = topo.addr(c)
-    d, sm = landing(T, t, k)
-    return RemoteDMATransfer(dst_ids=[DstId(rid=a[0], pnc=a[1])], dma_engine_mask=mask, remote_sem=sm, src=staged(T, k), dst=d)
+def signal(s, k):
+    return "x%s_%d" % (k, s % (FAR + 1))
 
 
-def relay_program(g, core, T, topo, dsts, items):
-    off = off_mask(T, topo, core)
-    tot = 0
-    for k in items:
-        g.wait_ge(T.sem["hx%s" % k], bits(off))
-        masks = [off if j == 0 else topo.mask(core, c) & ~off for j, (c, t) in enumerate(dsts)]
-        g.remote_dma_fused([transfer(T, topo, c, m, t, k) for (c, t), m in zip(dsts, masks)], local_sem=T.sem.ls)
-        tot += sum(bits(m) for m in masks)
-    g.wait_ge(T.sem.ls, tot)
+def transfers(T, topo, core, sends, k):
+    to = sorted([(c, t) for (c, t, items) in sends[core][1] if k in items], key=lambda x: topo.chip(x[0]) != topo.chip(core))
+    off = topo.engines(core, [c for c in T.cores if topo.chip(c) != topo.chip(core)][0])
+    out = []
+    for j, (c, t) in enumerate(to):
+        es = off if j or topo.chip(c) != topo.chip(core) else [e for e in topo.engines(core, c) if e not in off]
+        if core in T.cores:
+            es = es[:len(es) // 2] if k in STREAM else es[len(es) // 2:]
+        out.append((es, c, t))
+    return out
+
+
+def engines_in(T, topo, core, sends, s, k):
+    return [len(es) for a in sends if sends[a][0] == s for es, c, t in transfers(T, topo, a, sends, k) if c == core][0]
+
+
+def engines_out(T, topo, core, sends):
+    return sum(len(es) for k in ITEMS for es, c, t in transfers(T, topo, core, sends, k))
+
+
+def call(g, T, topo, core, sends, ks):
+    return g.remote_dma_fused([RemoteDMATransfer(dst_ids=[DstId(rid=topo.addr(c)[0], pnc=topo.addr(c)[1])], dma_engine_mask=sum(1 << e for e in es),
+                                                 remote_sem=T.sem[signal(sends[core][0], k)], src=staged(T, k), dst=landing(T, t, k))
+                               for k in ks for es, c, t in transfers(T, topo, core, sends, k)], local_sem=T.sem.ls)
+
+
+def relay_program(g, core, T, topo, sends):
+    s, to = sends[core]
+    for k in ITEMS if "k" in to[0][2] or to[0][1] is None else HELD:
+        if transfers(T, topo, core, sends, k):
+            g.wait_ge(T.sem[signal(s, k)], engines_in(T, topo, core, sends, s, k))
+            call(g, T, topo, core, sends, [k])
+    g.wait_ge(T.sem.ls, engines_out(T, topo, core, sends))
 
 
 def rank_program(g, core, T, topo):
-    first, relay = routes(T, topo)
+    sends = routes(T, topo)
     rank = T.rank_of(core)
     if rank is None:
-        if core in relay:
-            relay_program(g, core, T, topo, *relay[core])
+        if core in sends:
+            relay_program(g, core, T, topo, sends)
         return
     n = len(T.cores)
     Q = {"g": g, "v": g.vector, "a": g.scalar, "t": g.tensor, "s": g.sync}
     ops = []
     wr = {}
     rd = {}
+    last = {}
     ndma = [0]
 
-    def op(e, fn, r=(), w=(), kind="c", ext=()):
+    def op(e, fn, r=(), w=(), kind="c", ext=(), cost=0.06):
         me = len(ops)
-        deps = set()
+        deps, order = set(), set()
         for x in r:
             if x in wr:
                 deps.add(wr[x])
             if x[0] == "@":
                 deps.update(j for j in rd.get(x, []) if ops[j]["e"] != e)
         for x in w:
-            js = rd.get(x, []) + ([wr[x]] if x in wr else [])
-            deps.update(j for j in js if ops[j]["e"] != e or ops[j]["kind"] != "c" or kind != "c")
+            deps.update(rd.get(x, []) + ([wr[x]] if x in wr else []))
+        order.update(deps)
         if e == "t":
             deps = set(j for j in deps if ops[j]["e"] != "t")
-        o = {"e": e, "fn": fn, "deps": deps, "kind": kind, "ext": list(ext), "need": False}
+        if e in "gs" or kind == "d":
+            order.update([last[e]] if e in last else [])
+            last[e] = me
+        o = {"e": e, "fn": fn, "deps": deps, "order": order, "kind": kind, "ext": list(ext), "need": False, "cost": cost}
         if kind == "d":
             o["name"] = "d%d" % ndma[0]
             ndma[0] += 1
@@ -162,28 +181,38 @@ def rank_program(g, core, T, topo):
             rd[x] = []
         return me
 
+    def late(t):
+        return topo.chip(T.cores[(rank + t) % n]) != topo.chip(core)
+
     vec, act, pe = g.vector, g.scalar, g.tensor
+    wide = lambda x: "float32" in str(x.dtype) or "int32" in str(x.dtype).replace("uint", "")
+    els = lambda x, rate=1.0: CALL + CYCLE * max(64, rate * x.shape[1])
+    picked = lambda x, rate: 0.06 + CYCLE * rate * x.shape[1]
 
     def ts(out, in0, s1, o0, r, w, s2=None, o1=None):
         if o1 is None:
-            op("v", lambda: vec.tensor_scalar(out, in0, s1, None, o0), r, w)
+            op("v", lambda: vec.tensor_scalar(out, in0, s1, None, o0), r, w, cost=els(out))
         else:
-            op("v", lambda: vec.tensor_scalar(out, in0, s1, s2, o0, o1), r, w)
+            op("v", lambda: vec.tensor_scalar(out, in0, s1, s2, o0, o1), r, w, cost=els(out))
 
-    def tt(out, a, b, o, r, w, ext=()):
-        op("v", lambda: vec.tensor_tensor(out, a, b, o), r, w, ext=ext)
+    def tt(out, a, b, o, r, w, ext=(), pick=False):
+        psum = [x for x in list(r) + list(w) if x[0] == "@"]
+        op("v", lambda: vec.tensor_tensor(out, a, b, o), r, w, ext=ext, cost=picked(out, GATHER) if pick else els(out, 1.0 if psum else 2.0))
 
-    def cp(out, a, r, w, ext=()):
-        op("v", lambda: vec.tensor_copy(out, a), r, w, ext=ext)
+    def cp(out, a, r, w, ext=(), pick=False):
+        op("v", lambda: vec.tensor_copy(out, a), r, w, ext=ext, cost=picked(out, GATHER) if pick else els(out, 1.0 if wide(out) or wide(a) else 0.5))
 
     def ms(out, c, w):
-        op("v", lambda: vec.memset(out, c), (), w)
+        op("v", lambda: vec.memset(out, c), (), w, cost=els(out, 0.5))
 
-    def ac(out, a, r, w, scale=1.0, ext=()):
-        op("a", lambda: act.activation(out, a, AF.Copy, scale=scale), r, w, ext=ext)
+    def ac(out, a, r, w, scale=1.0, ext=(), pick=False):
+        op("a", lambda: act.activation(out, a, AF.Copy, scale=scale), r, w, ext=ext, cost=picked(out, GATHER) if pick else els(out))
 
     def af(out, a, f, scale, bias, r, w):
-        op("a", lambda: act.activation(out, a, f, bias=bias, scale=scale), r, w)
+        op("a", lambda: act.activation(out, a, f, bias=bias, scale=scale), r, w, cost=els(out))
+
+    def turn32(out, in_, r, w):
+        op("v", lambda: vec.transpose(out, in_), r, w, cost=els(out, 1.0 if wide(out) else 0.5))
 
     def mm(lst, r, w):
         def fn():
@@ -191,7 +220,7 @@ def rank_program(g, core, T, topo):
             for (out, l, x, st, sp) in lst:
                 ins = pe.matmul(out, l, x, st, sp)
             return ins
-        op("t", fn, r, w)
+        op("t", fn, r, w, cost=sum(PE_CYCLE * (4 if wide(l) else 1) * max(min(64, l.shape[1]), x.shape[1]) for (out, l, x, st, sp) in lst))
 
     def grp(out, terms):
         return [(out, l, x, j == 0, j == len(terms) - 1) for j, (l, x) in enumerate(terms)]
@@ -199,45 +228,53 @@ def rank_program(g, core, T, topo):
     def run(trip, opens, closes):
         return [(o_, l, x, opens and j == 0, closes and j == len(trip) - 1) for j, (o_, l, x) in enumerate(trip)]
 
-    def dma(e, out, in_, r, w):
-        op(e, lambda: Q[e].dma_start(out, in_), r, w, kind="d")
+    def dma(e, out, in_, r, w, cost=None):
+        op(e, lambda: Q[e].dma_start(out, in_), r, w, kind="d", cost=cost or 2.2 + 0.15 * ndma[0])
 
     def iota(out, pat, b, w):
-        op("g", lambda: g.iota(out, pat, b, 0, allow_small_or_imprecise_dtypes=True), (), w)
+        op("g", lambda: g.iota(out, pat, b, 0, allow_small_or_imprecise_dtypes=True), (), w, cost=0.13 + 2 * CYCLE * out.shape[1])
+
+    def steps(c0, c1, w):
+        return [(c, min(c + w, c1)) for c in range(c0, c1, w)]
 
     P = [T["P%d" % b] for b in range(8)]
     col = lambda t, j: t[:, j:j + 1]
-    HNT = ["HN%d" % k for k in range(NH)]
+    tok = lambda nm, c0, c1: ["%s_%d" % (nm, c) for c in range(c0 // 4, (c1 + 3) // 4)]
+    HNT = ["HN%d" % k for k in range(len(LOADS) - 1)]
 
-    dma("s", T.HN[:, HC[0]:HC[1]], T.h[:, HC[0]:HC[1]], (), ["HN0"])
+    load = lambda e, j: dma(e, T.HN[:, LOADS[j]:LOADS[j + 1]], T.h[:, LOADS[j]:LOADS[j + 1]], (), [HNT[j]])
+    load("s", 0)
     dma("a", T.KI[1:128:2, :], T.kr[:], (), ["KIb"])
     dma("s", T.KI[0:128:2, :], T.kl[:], (), ["KIa"])
-    dma("a", T.HN[:, HC[1]:HC[2]], T.h[:, HC[1]:HC[2]], (), ["HN1"])
-    dma("s", T.HN[:, HC[2]:HC[3]], T.h[:, HC[2]:HC[3]], (), ["HN2"])
-    dma("a", T.HN[:, HC[3]:HC[4]], T.h[:, HC[3]:HC[4]], (), ["HN3"])
-    dma("s", T.SAB[:, 0:24], T.sa[:], (), ["SA"])
-    dma("s", T.SAB[:, 24:48], T.sb[:], (), ["SB"])
+    for e, j in (("a", 1), ("s", 2), ("a", 3)):
+        load(e, j)
+    dma("s", T.SAB[:, 0:24], T.sa[:], (), ["SA"], 7.0)
+    dma("s", T.SAB[:, 24:48], T.sb[:], (), ["SB"], 7.0)
     b0 = base(0)
-    dma("s", T.TB[0:128:2, b0:b0 + M], T.h[1:128:2, :], HNT, ["T0a"])
-    dma("s", T.TB[1:128:2, b0:b0 + M], T.h[0:128:2, :], (), ["T0b"])
+    dma("s", T.TB[0:128:2, b0:b0 + M], T.h[1:128:2, :], HNT, ["T0a"], 5.0)
+    dma("s", T.TB[1:128:2, b0:b0 + M], T.h[0:128:2, :], (), ["T0b"], 5.0)
 
-    op("g", lambda: g.iota(T.PI[:], [[0, 8]], 0, 1), (), ["PI"])
-    iota(T.Y[:], [[1, 160]], 0, ["Y"])
+    def pick(out, in_, pat, cmp_, b, cm, r, w):
+        op("g", lambda: g.affine_select(out, in_, pat, cmp_, 0.0, b, cm), r, w, cost=0.17 + 2 * CYCLE * out.shape[1])
+
+    def band(out, in_, pat, lo, hi, r, w):
+        pick(out, in_, pat, A.is_ge, -lo, 1, r, w)
+        pick(out, out, [[-st, k] for st, k in pat], A.is_ge, hi, -1, w, w)
+
+    op("g", lambda: g.iota(T.PI[:], [[0, 2]], 0, 1), (), ["PI"], cost=0.14)
+    iota(T.YZ[:], [[32, 5], [1000, 32]], -31000, ["YZ"])
     iota(T.B32[:], [[32, 64], [0, 2]], 0, ["B32"])
-    iota(T.Y16[:], [[16, 8]], 0, ["Y16"])
-    for j, mk in enumerate((127, 15, 112, 31, 96, 16)):
+    iota(T.WA[:], [[0, 32]], 1, ["WA"])
+    band(T.WA[:], T.WA[:], [[-4, 4], [-16, 8]], 0, 3, ["WA"], ["WA"])
+    op("g", lambda: g.iota(col(T.PF, 2), [[0, 1]], 33, 1, allow_small_or_imprecise_dtypes=True), (), ["P33"], cost=0.14)
+    for j, mk in enumerate((112, 31)):
         ts(col(T.PJ, j), col(T.PI, j), mk, A.bitwise_and, ["PI"], ["PJ%d" % j])
-    cp(T.PF[:, 0:6], T.PJ[:, 0:6], ["PJ%d" % j for j in range(6)], ["PF"])
-    cP, cI, cG16, cP32, cG32, cH16 = [col(T.PF, j) for j in range(6)]
-    ts(col(T.PF, 6), cH16, 64.0, A.mult, ["PF"], ["PF6"])
-    ts(col(T.PF, 7), cH16, -64.0, A.mult, ["PF"], ["PF7"], 1024.0, A.add)
-    ts(T.V[:], T.B32[:], cP32, A.add, ["B32", "PF"], ["V"])
-    ts(T.PF[:, 8:10], T.PF[:, 6:8], cG32, A.add, ["PF6", "PF7"], ["PF8"], 31.0, A.add)
-    ts(T.PF[:, 10:12], T.PF[:, 6:8], cP, A.add, ["PF6", "PF7"], ["PF10"], 16.0, A.add)
-    ZS, ZX, ZF, ZN = (T.ZS0, T.ZS1), (T.ZX0, T.ZX1), (T.ZF0, T.ZF1), (T.ZN0, T.ZN1)
+    cp(T.PF[:, 0:2], T.PJ[:], ["PJ0", "PJ1"], ["PF"])
+    cG16, cP32 = col(T.PF, 0), col(T.PF, 1)
+    ZS, ZX, ZF = (T.ZS0, T.ZS1), (T.ZX0, T.ZX1), (T.ZF0, T.ZF1)
     for x in (0, 1):
-        ts(ZS[x][:], T.Y[:], col(T.PF, 8 + x), A.is_equal, ["Y", "PF8"], ["ZS%d" % x])
-    ts(T.IDF[:], T.Y[:, 0:128], cP, A.is_equal, ["Y", "PF"], ["IDF"])
+        ts(ZS[x][:], T.YZ[:], cG16, A.subtract, ["YZ", "PF"], ["ZS%d" % x], -16.0 * x, A.is_equal)
+    ts(T.V[:], T.B32[:], cP32, A.add, ["B32", "PF"], ["V"], 1.0 / BIG, A.mult)
 
     lst = []
     for x in (0, 1):
@@ -245,163 +282,140 @@ def rank_program(g, core, T, topo):
     mm(lst, ["ZS0", "ZS1"] + HNT, ["@0"])
 
     cp(T.KF[:], T.KI[:], ["KIa", "KIb"], ["KF"])
-    op("v", lambda: vec.transpose(T.KT[:], T.KF[:]), ["KF"], ["KT"])
+    turn32(T.KT[:], T.KF[:], ["KF"], ["KT"])
     for side in (0, 1):
         for sg in range(8):
             c0 = 128 * side + 16 * sg
-            (ac if side else cp)(T.KLR[:, c0:c0 + 16], T.KT[:, 2 * sg + side:256:16], ["KT"], ["K%d%d" % (side, sg)])
+            (ac if sg % 2 else cp)(T.KLR[:, c0:c0 + 16], T.KT[:, 2 * sg + side:256:16], ["KT"], ["K%d%d" % (side, sg)])
     KL, KR = T.KLR[:, 0:128], T.KLR[:, 128:256]
+    KLT = ["K0%d" % sg for sg in range(8)]
     ci = lambda j, k=1, t=0: T.CI[:, 896 * t + 128 * j:896 * t + 128 * (j + k)]
-    leaf, d2, key, r1 = P[1][:, 0:128], P[2][:, 0:256], P[3][:, 0:128], P[4][:, 0:128]
-    ts(leaf, KL, 0.0, A.is_equal, ["K0%d" % sg for sg in range(8)], ["@1"])
+    leaf, left, key, right = P[1][:, 0:128], P[2][:, 0:128], P[3][:, 0:128], P[4][:, 0:128]
+    ts(leaf, KL, 0.0, A.is_equal, KLT, ["@1"], float(BIG), A.mult)
     tt(P[5][:, 0:128], leaf, T.V[:], A.mult, ["@1", "V"], ["@5"])
-    tt(P[2][:, 128:256], KR, leaf, A.subtract, ["@1"] + ["K1%d" % sg for sg in range(8)], ["@2"])
-    ts(T.WK[:], leaf, -float(2 ** 22), A.mult, ["@1"], ["w4"], float(2 ** 21), A.add)
-    tt(P[2][:, 0:128], P[5][:, 0:128], KL, A.add, ["@5"], ["@2"])
+    tt(right, KR, leaf, A.subtract, ["@1"] + ["K1%d" % sg for sg in range(8)], ["@4"])
+    tt(left, P[5][:, 0:128], KL, A.add, ["@5"] + KLT, ["@2"])
+    ts(T.WK[:], leaf, -float(2 ** 22 // BIG), A.mult, ["@1"], ["w4"], float(2 ** 21), A.add)
+    ac(ci(4), right, ["@4"], ["c4"])
+    cp(ci(3), left, ["@2"], ["c3"])
+    tt(ci(5), left, ci(3), A.subtract, ["@2", "c3"], ["c5"])
+    tt(ci(6), right, ci(4), A.subtract, ["@4", "c4"], ["c6"])
     tt(key, P[0][:, 0:128], T.WK[:], A.min, ["@0", "w4"], ["@3"])
-    cp(ci(0), key, ["@3"], ["c0"])
-    ac(ci(3, 2), d2, ["@2"], ["c3"])
-    tt(r1, key, ci(0), A.subtract, ["@3", "c0"], ["@4"])
-    tt(ci(5, 2), d2, ci(3, 2), A.subtract, ["@2", "c3"], ["c5"])
-    cp(ci(1), r1, ["@4"], ["c1"])
-    tt(ci(2), r1, ci(1), A.subtract, ["@4", "c1"], ["c2"])
-    CIT = {"c": ["c0", "c1", "c2"], "k": ["c3", "c5"]}
+    ts(T.K7[:], key, 1.5 * 2 ** 30, A.add, ["@3"], ["k7"], 1.5 * 2 ** 30, A.subtract)
+    ts(ci(0), key, 1.5 * 2 ** 38, A.add, ["@3"], ["c0"], 1.5 * 2 ** 38, A.subtract)
+    tt(ci(2), key, T.K7[:], A.subtract, ["@3", "k7"], ["c2"])
+    tt(ci(1), T.K7[:], ci(0), A.subtract, ["k7", "c0"], ["c1"])
+    CIT = {"c": ["c0", "c1", "c2"], "k": ["c3", "c4", "c5", "c6"]}
 
-    ls = [0]
-    offm = off_mask(T, topo, core)
-    ARR = bits(offm)
-
-    def send(k):
-        trs = []
-        for (c, t, items) in first[rank]:
-            if k in items:
-                m = topo.mask(core, c) & ~offm if topo.chip(c) == topo.chip(core) else topo.mask(core, c)
-                trs.append(transfer(T, topo, c, m, t, k))
-                ls[0] += bits(m)
-        op("g", lambda: g.remote_dma_fused(trs, local_sem=T.sem.ls), CIT[k] if k in REC else ["HN%d" % k], (), kind="r")
-
-    for k in ITEMS:
-        send(k)
-    for t in range(4):
-        iota(T.TB[:, PITCH * t:PITCH * t + 32], [[0, 32]], -131072, ["TD%d" % t])
-        if t:
-            iota(T.IT[:, PITCH * t:PITCH * t + 32], [[0, 32]], 0, ["ID%d" % t])
+    arrival = lambda t, k: (signal(rank + t, k), engines_in(T, topo, core, sends, (rank + t) % n, k))
+    loaded = lambda k: [HNT[j] for j in range(len(HNT)) if LOADS[j] < HC[k + 1] and HC[k] < LOADS[j + 1]]
+    for ks in CALLS:
+        op("g", lambda ks=ks: call(g, T, topo, core, sends, ks), sum([CIT[k] if k in REC else loaded(k) for k in ks], []), (), kind="r",
+           cost=0.4 + 1.2 * (ks == CALLS[0]))
+    iota(T.ONF[:], [[0, 160]], 1, ["ONF"])
+    pick(T.IDF[:], T.ONF[:, 0:128], [[-1, 128]], A.is_equal, 0, 1, ["ONF"], ["IDF"])
+    SELS = {1: (0, [[0, 2], [-1, 24]]), 2: (48, [[0, 2], [-1, 24], [-24, 2]]), 3: (144, [[-1, 48], [-48, 2]])}
+    iota(T.IT[:, 0:32], [[0, 32]], 0, ["ID"])
+    for lv, (s0, pat) in SELS.items():
+        w = 48 if lv == 1 else 96
+        pick(T.SEL[:, s0:s0 + w], T.ONF[:, 0:w], pat, A.is_equal, 0, 1, ["ONF"], ["SEL%d" % lv])
+    iota(T.TB[:, 0:16], [[0, 16]], -131072, ["TD"])
+    iota(T.TB[:, 16:32], [[0, 16]], 0, ["TZ"])
+    iota(T.ONB[:], [[0, 160]], 1, ["ONB"])
+    pick(T.Z[:], T.ONB[:], [[0, 10], [1, 16]], A.is_equal, -15, 0, ["ONB"], ["Z"])
+    band(T.Z[:], T.Z[:], [[-1, 160]], -15, 0, ["Z"], ["Z"])
+    pick(T.ZF1[:], T.ONF[:], [[-1, 160]], A.is_equal, 16, 1, ["ONF"], ["ZF1"])
+    for x in (0, 1):
+        pick(ZF[x][:], T.ZF1[:], [[0, 5], [1, 2], [0, 16]], A.is_equal, x - 1, 0, ["ZF1"], ["ZF%d" % x])
+    band(T.TRU[:], T.ONB[:, 0:128], [[-16, 8], [0, 16]], 0, 15, ["ONB"], ["TRU"])
+    pick(T.TRB[:], T.TRU[:], [[1, 128]], A.is_gt, 0, -1, ["TRU"], ["TRB"])
+    pick(T.TRI[:], T.TRU[:], [[1, 128]], A.is_ge, 0, -1, ["TRU"], ["TRI"])
+    pick(T.TRU[:], T.TRU[:], [[-1, 128]], A.is_gt, 0, 1, ["TRU"], ["TRU"])
+    iota(T.JC[:], [[1, 96]], 0, ["JC"])
     WIN = (T.W0, T.W1, T.W2)
     iota(T.SIN[:], [[0, 1536]], 0, ["SIN"])
-    for k in range(3):
+    iota(WIN[0][:, 0:ZW], [[0, ZW]], 0, ["W0"])
+    iota(T.SIN[:, 8:1536:16], [[0, 96]], 1, ["SIN"])
+    iota(T.WB[:], [[0, 48]], BIG, ["WB"])
+    for j, lo in enumerate((2, 4, 0, 2, 0)):
+        band(T.WS[:, 8 * j:8 * j + 8], T.ONB[:, 0:8], [[-16, 8]], lo, lo + 1, ["ONB"], ["WS%d" % j])
+    for j, (lo, hi) in enumerate(((8, 8), (7, 7), (6, 7))):
+        band(T.WB[:, 16 * j:16 * j + 16], T.WB[:, 16 * j:16 * j + 16], [[0, 2], [-16, 8]], lo, hi, ["WB"], ["WB%d" % j])
+    for k in (1, 2):
         iota(WIN[k][:, 0:ZW], [[0, ZW]], 0, ["W%d" % k])
 
-    LANE = (0, 1, 2, 4, 7, 5, 8)
+    LANE = (0, 1, 2, 4, 8, 5, 9)
 
-    def lane(t, l, k=1):
-        return T.IN[:, M * t + l:M * (t + k):16]
+    def lane(t, l, k=1, st=16):
+        return T.IN[:, M * t + l:M * (t + k):st]
 
-    src512 = T.HN[:, 0:512]
-    CL = []
-    for l in range(11, 16):
-        if l < 14:
-            ac(lane(0, l, 4), src512, ["HN0"], ["cl%d" % l], scale=0.0)
-        else:
-            ms(lane(0, l, 4), 0.0, ["cl%d" % l])
-        CL.append("cl%d" % l)
-    af(lane(0, 10, 4), src512, AF.Identity, 0.0, cP32, ["HN0", "PF"], ["cl10"])
-    ms(lane(0, 3), 0.5, ["cl3"])
-    ms(lane(1, 3, 3), 0.0, ["cl3f"])
-    CL += ["cl10", "cl3", "cl3f"]
+    ms(lane(0, 2, 4, 4), 0.0, ["cz"])
     for t in range(4):
-        ms(lane(t, 6), float(base(t)), ["cb%d" % t])
-        ac(lane(t, 9), T.B32[:], ["B32"], ["cc%d" % t])
+        ms(lane(t, 3, 1, 4), float(base(t)), ["cb%d" % t])
+        ac(lane(t, 12), T.B32[:], ["B32"], ["cc%d" % t])
+    ms(lane(0, 3), 0.5, ["cb0"])
+    ms(lane(1, 3, 3), 0.0, ["cb1", "cb2", "cb3"])
+    af(lane(0, 13, 4), lane(0, 6, 4), AF.Identity, 0.0, cP32, ["cz", "PF"], ["cp"])
 
     def fill(t, k, js, f):
         for j in js:
-            f(lane(t, LANE[j]), ci(j, 1, t), [] if t else CIT[k], ["IN%d_%d" % (t, j)], ext=[("%si%d" % (k, t), ARR)] if t else [])
+            f(lane(t, LANE[j]), ci(j, 1, t), ["cz"] + ([] if t else CIT[k]), ["IN%d_%d" % (t, j)], ext=[arrival(t, k)] if t else [])
 
     def turn_tree(t):
-        op("v", lambda: vec.transpose(T.IT[:, base(t):base(t) + M], T.IN[:, M * t:M * t + M]),
-           ["IN%d_%d" % (t, j) for j in range(7)] + CL + ["cb%d" % t, "cc%d" % t], ["IT%d" % t])
+        turn32(T.IT[:, base(t):base(t) + M], T.IN[:, M * t:M * t + M],
+               ["IN%d_%d" % (t, j) for j in range(7)] + ["cz", "cp", "cb%d" % t, "cc%d" % t], ["IT%d" % t])
 
-    Y128 = T.Y[:, 0:128]
-    RANGES = ((0, 3), (4, 6), (6, 8), (9, 10), (2, 5), (0, 1), (6, 7), (8, 9), (2, 3), (6, 6))
-
-    def ranges(js):
-        for j in js:
-            ts(col(T.RG, j), col(T.GE, RANGES[j][0]), col(T.GE, RANGES[j][1] + 1), A.subtract, ["GE"], ["RG%d" % j])
-    ts(T.GE[:, 0:17], T.Y[:, 0:17], cI, A.is_le, ["PF"], ["GE"])
-    ts(T.E8[:], T.Y16[:], cG16, A.is_equal, ["Y16", "PF"], ["E8"])
-    ts(col(T.PF, 12), cI, 0.0, A.is_equal, ["PF"], ["PF12"], float(2 ** 22), A.mult)
-    ts(col(T.PF, 14), cG16, 15.0, A.add, ["PF"], ["PF14"])
-    ranges((3, 9, 0, 1, 2))
-    ts(col(T.RG, 12), col(T.RG, 3), col(T.RG, 9), A.add, ["RG3", "RG9"], ["RG12"])
-    for q, j in enumerate((0, 1, 2, 12)):
-        ts(T.WA[:, 8 * q:8 * q + 8], T.E8[:], col(T.RG, j), A.mult, ["E8", "RG%d" % j], ["WA%d" % q], 2.0 if q == 0 else 1.0, A.mult)
-    WAT = ["WA%d" % q for q in range(4)]
-    WST = ["WS%d" % q for q in range(4)]
-    ts(T.IT[:, 0:32], T.Y[:, 0:32], 0.0, A.mult, ["PF12"], ["ID0"], col(T.PF, 12), A.add)
-    ts(T.Z[:], T.Y[:], col(T.PF, 14), A.is_equal, ["PF14"], ["Z"])
-    tm = lambda j: T.TMP[:, 128 * j:128 * j + 128]
-
-    def later(k):
-        if k == 0:
-            ranges((4, 5, 6, 7, 8))
-        elif k == 1:
-            ts(col(T.RG, 10), col(T.RG, 6), col(T.RG, 8), A.subtract, ["RG6", "RG8"], ["RG10"])
-            ts(col(T.RG, 11), col(T.RG, 7), col(T.RG, 5), A.subtract, ["RG7", "RG5"], ["RG11"])
-            ts(col(T.PF, 13), cI, 96.0, A.mult, ["PF"], ["PF13"], 96.0 * 33, A.add)
-            for x in (0, 1):
-                ts(ZF[x][:], T.Y[:], col(T.PF, 10 + x), A.is_equal, ["PF10"], ["ZF%d" % x])
-        elif k == 2:
-            for q, j in enumerate((4, 5, 10, 11)):
-                ts(T.WS[:, 8 * q:8 * q + 8], T.E8[:], col(T.RG, j), A.mult, ["E8", "RG%d" % j], ["WS%d" % q])
-            ts(tm(0), Y128, cP, A.is_gt, ["PF"], ["t0"])
-            for x in (0, 1):
-                ac(ZX[x][:], ZF[x][:], ["ZF%d" % x], ["ZX%d" % x])
-                ac(ZN[x][:], ZF[x][:], ["ZF%d" % x], ["ZN%d" % x], scale=-1.0)
-        elif k == 5:
-            ac(T.IDB[:], T.IDF[:], ["IDF"], ["IDB"])
-            ac(T.NIB[:], T.IDF[:], ["IDF"], ["NIB"], scale=-1.0)
-            ac(T.NBG[:], T.IDF[:], ["IDF"], ["NBG"], scale=-8192.0)
-            af(T.JH[:], T.Y[:, 0:96], AF.Identity, 0.0, col(T.PF, 13), ["Y", "PF13"], ["JH"])
-            ac(T.JC[:], T.Y[:, 0:96], ["Y"], ["JC"])
-        elif k == 3:
-            ts(tm(1), Y128, col(T.PF, 14), A.is_le, ["PF14"], ["t1"])
-            ts(tm(2), Y128, cP, A.is_lt, ["PF"], ["t2"])
-            ts(tm(3), Y128, cG16, A.is_ge, ["PF"], ["t3"])
-        else:
-            tt(T.TRB[:], tm(0), tm(1), A.mult, ["t0", "t1"], ["TRB"])
-            tt(T.TRU[:], tm(2), tm(3), A.mult, ["t2", "t3"], ["TRU"])
+    ts(T.WA[:, 24:32], T.WA[:, 24:32], -1.0, A.mult, ["WA"], ["WA"])
+    WAT = ["WA"]
+    WST = ["WS%d" % j for j in range(5)]
 
     offp = lambda k, c0, c1: T.OPQ[:, 192 * k + c0:192 * k + c1]
     offq = lambda k, c0, c1: T.OPQ[:, 192 * k + 96 + c0:192 * k + 96 + c1]
-    SBI = T.SAB[:, 24:48]
-    ts(offp(0, 0, 24), T.SAB[:, 0:24], float(b0), A.add, ["SA"], ["OP0"])
-    ts(T.SF[:, 0:24], SBI, 2048.0, A.is_ge, ["SB"], ["s0"], 32.0, A.mult)
-    ts(T.SF[:, 24:48], SBI, 4096.0, A.is_ge, ["SB"], ["s1"], 32.0, A.mult)
-    ts(T.SF[:, 48:72], SBI, float(base(1)), A.add, ["SB"], ["s2"])
-    tt(T.SF[:, 72:96], T.SF[:, 0:24], T.SF[:, 24:48], A.add, ["s0", "s1"], ["s3"])
-    tt(T.SF[:, 0:24], T.SF[:, 72:96], T.SF[:, 48:72], A.add, ["s2", "s3"], ["s4"])
-    cp(offq(0, 0, 24), T.SF[:, 0:24], ["s4"], ["OQ0"])
+    ts(offp(0, 0, 24), T.SAB[:, 0:24], float(b0), A.add, ["SA"], tok("OP0", 0, 24))
+    ts(offq(0, 0, 24), T.SAB[:, 24:48], float(base(1)), A.add, ["SB"], tok("OQ0", 0, 24))
+    ts(T.SF[:], T.SAB[:, 24:48], float(base(1)), A.add, ["SB"], ["s0"])
     fill(0, "k", (3, 4, 5, 6), ac)
     fill(0, "c", (0, 1, 2), ac)
     turn_tree(0)
     ac(T.WN[:], T.WA[:], WAT, ["WN"], scale=-1.0)
-    ac(T.ZB[:], T.Z[:], ["Z"], ["ZB"], scale=-16384.0)
+    RR = {"P": T.RP, "Q": T.RQ}
 
-    def gather(out, nm, win, k, C, r):
-        h = C // 2 + (2 if C == 96 else 0)
-        off = offp if nm == "P" else offq
-        r = r + ["O%s%d" % (nm, k), "O%sb%d" % (nm, k)]
-        ac(out[:, 0:16 * h], win.indirect(off(k, 0, h)), r, ["R%sa" % nm])
-        cp(out[:, 16 * h:16 * C], win.indirect(off(k, h, C)), r, ["R%sb" % nm])
+    def gather(e, nm, win, off, c0, c1, r):
+        if c1 > c0:
+            (ac if e == "a" else cp)(RR[nm][:, 16 * c0:16 * c1], win.indirect(off(c0, c1)), r, tok("R" + nm, c0, c1), pick=True)
 
-    def p_terms(C):
-        mm(run([(P[1][0:C, i:384:16], T.RP[:, i:16 * C:16], T.WA[:, 8:32]) for i in range(16)], True, True), ["RPa", "RPb"] + WAT, ["@1"])
-        mm(run([(P[0][0:C, i:512:16], T.RP[:, i:16 * C:16], T.WN[:]) for i in range(16)], True, False), ["RPa", "RPb", "WN"], ["@0"])
+    def key_terms(nm, segs, opens, closes):
+        w = T.WN if nm == "P" else T.WA
+        lst = [(P[0][r0:r1, i:512:16], RR[nm][:, 16 * q0 + i:16 * (q0 + r1 - r0):16], w[:]) for i in range(16) for (r0, r1, q0) in segs]
+        if len(segs) > 1:
+            lst = [(P[0][0:segs[-1][1], 0:512:16], T.HN[:, 0:segs[-1][1]], T.IT[:, 0:32])] + lst
+        mm(run(lst, opens, closes), WAT + ["WN"] + ["ID"] * (len(segs) > 1) + sum([tok("R" + nm, q0, q0 + r1 - r0) for (r0, r1, q0) in segs], []), ["@0"])
 
-    gather(T.RP, "P", T.IT[:, 0:PITCH], 0, 24, ["IT0", "ID0"])
-    p_terms(24)
+    def kid_terms(c0, c1):
+        mm(run([(P[1][0:c1 - c0, i:256:16], T.RP[:, 16 * c0 + i:16 * c1:16], T.WA[:, 8:24]) for i in range(16)], True, True),
+           tok("RP", c0, c1) + WAT, ["@1"])
 
-    def late(t):
-        return topo.chip(T.cores[(rank + t) % n]) != topo.chip(core)
+    def kid_copy(n_):
+        ac(T.VT[0:n_, :], P[1][0:n_, 0:256], ["@1"], ["VT"])
+
+    for e, c0 in (("a", 0), ("v", 12)):
+        gather(e, "P", T.IT[:, 0:base(1)], lambda a, b: offp(0, a, b), c0, c0 + 12, ["IT0", "ID"] + tok("OP0", c0, c0 + 12))
+    kid_terms(0, 24)
+    key_terms("P", [(0, 24, 0)], True, False)
+    kid_copy(24)
+
+    def late_constants():
+        ac(T.IDB[:], T.IDF[:], ["IDF"], ["IDB"])
+        ac(T.NIB[:], T.IDF[:], ["IDF"], ["NIB"], scale=-1.0)
+        ac(T.NBG[:], T.IDF[:], ["IDF"], ["NBG"], scale=-8192.0)
+        for x in (0, 1):
+            ac(ZX[x][:], ZF[x][:], ["ZF%d" % x], ["ZX%d" % x])
+        ts(col(T.PF, 3), col(T.PF, 2), cG16, A.subtract, ["PF", "P33"], ["PF3"], 96.0, A.mult)
+        af(T.JH[:], T.B32[:, 0:96], AF.Identity, 0.0, col(T.PF, 3), ["B32", "PF3"], ["JH"])
+        w8 = lambda t, j, k: t[:, 8 * j:8 * (j + k)]
+        for j, k, jb, o in ((0, 1, 0, A.add), (0, 1, 2, A.subtract), (1, 1, 2, A.add), (2, 1, 0, A.add), (3, 2, 4, A.add), (3, 2, 0, A.subtract)):
+            tt(w8(T.WS, j, k), w8(T.WS, j, k), w8(T.WB, jb, k), o, ["WB%d" % (jb // 2)] + WST[j:j + k], WST[j:j + k])
+
     for t in (1, 2, 3):
         if not late(t):
             fill(t, "k", (3, 4, 5, 6), ac)
@@ -415,191 +429,299 @@ def rank_program(g, core, T, topo):
         fill(t, "c", (0,) if j == 0 else (0, 1, 2), ac)
         fill(t, "c", (1, 2) if j == 0 else (), cp)
         turn_tree(t)
-    ITT = ["IT%d" % t for t in range(4)] + ["ID%d" % t for t in range(4)]
-    TBT = ["T0a", "T0b"] + ["TD%d" % t for t in range(4)]
-    HEXT = [("h%d_%d" % (t, k), ARR) for t in (1, 2, 3) for k in range(NH)]
+    ITT = ["IT%d" % t for t in range(4)] + ["ID"]
+    TBT = ["T0a", "T0b", "TD", "TZ"]
+    HEXT = [arrival(t, k) for t in (1, 2, 3) for k in range(len(HC) - 1)]
     sel = lambda i: T.Z[:, 15 - i:143 - i]
     sw = lambda zz, x, gg: zz[x][:, 16 - 16 * (gg - x):144 - 16 * (gg - x)]
+    ITW, TBW = T.IT[:, 0:NT], T.TB[:, 0:NT]
 
-    def turn(out, in_, c, r, w):
-        op("t", lambda: pe.transpose(out, in_, T.IDF[0:c, 0:c]), r + ["IDF"], w)
+    XW = {1: 32, 2: 64}
+    piece = lambda rn, c: [x for x in PIECES[rn] if x[0] <= c][-1]
 
-    for rn in range(5):
-        C = min(24 << rn, 96)
-        nn = 16 * C
-        press = rn >= 2
-        if rn:
-            gather(T.RP, "P", T.IT[:, 0:NT], rn, C, ITT)
-            p_terms(C)
-        gather(T.RQ, "Q", T.IT[:, 0:NT], rn, C, ITT)
-        ac(T.VT[0:C, :], P[1][0:C, 0:384], ["@1"], ["VT"])
-        mm(run([(P[0][0:C, i:512:16], T.RQ[:, i:nn:16], T.WA[:]) for i in range(16)], False, True), ["RQa", "RQb"], ["@0"])
-        idc = T.IDF[0:C, 0:C]
-        banks = ((2, 2), (3, 0), (7, 1)) + (() if press else ((4, 0), (5, 1)))
-        for (b, q) in banks:
-            mm([(P[b][:, 0:C], T.VT[0:C, 128 * q:128 * q + 128], idc, True, False)], ["VT", "IDF"], ["@%d" % b])
+    def ov(rn, q, a, b):
+        c0, c1 = piece(rn, a)
+        w = XW.get(rn, c1 - c0)
+        o = 288 * (rn - 1) + 3 * c0 + (0, w, w + c1 - c0)[q] - c0
+        return T.OV[:, o + a:o + b]
+    otok = lambda rn, q, c: "O%d%d_%d" % (rn, min(q, 1), piece(rn, c)[0])
 
-        def add_turn(b, q):
-            mm([(P[b][:, 0:C], T.MM[0:C, 128 * q:128 * q + 128], idc, False, b not in (4, 5))], ["m%d" % q], ["@%d" % b])
+    def decide_base(rn, c0, c1):
+        n_ = c1 - c0
+        if rn == 1:
+            lst = [(P[2][:, 0:24], T.IDF[:], T.SF[:, 0:24]), (P[2][:, 24:32], T.IDF[:], T.SF[:, 0:8])]
+        elif rn < 4:
+            w = XW.get(rn, n_)
+            lst = [(P[2][:, s:w:2], T.IDF[:], T.XF[:, 0:w // 2]) for s in (0, 1)]
+        else:
+            lst = [(P[2][:, 0:n_], T.PT[0:n_, 128 * j:128 * j + 128], T.IDF[0:n_, 0:n_]) for j in (2, 4)]
+        mm(run(lst, True, False), ["s0", "XF", "IDF", "PT2", "PT4"], ["@2"])
+
+    def decide(rn, c0, c1):
+        n_ = c1 - c0
+        w = XW.get(rn, n_)
+        S, s0 = (T.SEL, SELS[rn][0]) if rn in SELS else (T.IDF, 0)
+        dst = ((P[3][:, 0:n_], n_), (P[3][:, n_:2 * n_], n_), (P[2][:, 0:w], w))
+        term = lambda src, q: (dst[q][0], src[0:n_, 128 * q:128 * q + 128], S[0:n_, s0:s0 + dst[q][1]])
+        st = ["SEL%d" % rn, "IDF"]
+        early = rn not in (2, 3)
+        kid_base = lambda opens, closes: mm(run([term(T.VT, 0), term(T.VT, 1)], opens, closes), ["VT"] + st, ["@3"])
+        if early:
+            kid_base(True, False)
+        ts(T.MK[0:n_, :], P[0][0:n_, 0:128], 0.0, A.is_ge, ["@0"], ["qo"])
+        for q in (2, 0, 1):
+            tt(T.MM[0:n_, 128 * q:128 * q + 128], P[0][0:n_, 128 * q + 128:128 * q + 256], T.MK[0:n_, :], A.mult, ["@0", "qo"], ["m%d" % q])
+            mm(run([term(T.MM, q)], q == 0 and not early, q == 2 or (q == 1 and early)), ["m%d" % q] + st, ["@2" if q == 2 else "@3"])
+        if not early:
+            kid_base(False, True)
+        cp(ov(rn, 0, c0, c0 + w), P[2][:, 0:w], ["@2"], [otok(rn, 0, c0)])
+
+    def kid_lists(rn, c0, c1):
+        cp(ov(rn, 1, c0, 2 * c1 - c0), P[3][:, 0:2 * (c1 - c0)], ["@3"], [otok(rn, 1, c0)])
+
+    S0 = {1: 0, 2: 384}
+    nxt = lambda rn, c0, c1: T.NXS[:, S0[rn] + 16 * c0:S0[rn] + 16 * c1] if rn < 3 else T.NX[:, 16 * c0:16 * c1]
+
+    def fft(rn, side, c0, c1, i=0, st=1):
         if rn < 3:
-            later(2 * rn)
-        D = P[0][0:C, 0:128]
-        ts(T.MK[0:C, 128:256], D, 0.0, A.is_lt, ["@0"], ["po"])
-        ts(T.MK[0:C, 0:128], D, 0.0, A.is_ge, ["@0"], ["qo"])
-        tt(T.MM[0:C, 256:384], P[0][0:C, 384:512], T.MK[0:C, 128:256], A.mult, ["@0", "po"], ["m2"])
-        add_turn(2, 2)
-        tt(T.MM[0:C, 0:128], P[0][0:C, 128:256], T.MK[0:C, 0:128], A.mult, ["@0", "qo"], ["m0"])
-        add_turn(3, 0)
-        tt(T.MM[0:C, 128:256], P[0][0:C, 256:384], T.MK[0:C, 0:128], A.mult, ["@0", "qo"], ["m1"])
-        add_turn(7, 1)
-        if not press:
-            add_turn(4, 0)
-            add_turn(5, 1)
-        cp(T.OV[:, 0:C], P[2][:, 0:C], ["@2"], ["OX"])
-        cp(T.OV[:, 96:96 + C], P[3][:, 0:C], ["@3"], ["O0"])
-        cp(T.OV[:, 192:192 + C], P[7][:, 0:C], ["@7"], ["O1"])
-        cuts = {24: (0, 8, 24), 48: (0, 12, 48), 96: (0, 16, 36, 64)}[C]
-        nch = len(cuts) - 1
-        for j in range(nch):
-            c0, c1 = cuts[j], cuts[j + 1]
-            ac(T.NX[:, 16 * c0:16 * c1], T.TB[:, 0:NT].indirect(T.OV[:, c0:c1]), TBT + ["OX"], ["NX%d" % j], scale=-1.0,
-               ext=HEXT if rn == 0 and j == 0 else ())
-            if press and j == 0:
-                ac(T.VW[:, 0:96], P[2][:, 0:96], ["@2"], ["VWx"])
-                ac(T.VW[:, 96:192], P[3][:, 0:96], ["@3"], ["VWl"])
-                ac(T.VW[:, 192:288], P[7][:, 0:96], ["@7"], ["VWr"])
-        if press:
-            lst = [(P[6][:, x:288:2], sw(ZF, x, gg), T.VW[:, gg:288:2]) for x in (0, 1) for gg in (0, 1)]
-            lst += [(P[6][:, 192 + x:288:2], sw(ZN, x, gg), T.VW[:, 96 + gg:192:2]) for x in (0, 1) for gg in (0, 1)]
-            mm(run(lst, True, True), ["VWx", "VWl", "VWr", "ZF0", "ZF1", "ZN0", "ZN1"], ["@6"])
-            ac(T.NX[:, 1024:1536], T.TB[:, 0:NT].indirect(T.OV[:, 64:96]), ["OX"], ["NXB"], scale=-1.0)
-            ac(T.PC[:, 0:288], P[6][:, 0:288], ["@6"], ["PCh"])
-            for l, c0 in ((0, 0), (2, 96)):
-                ac(T.SIN[:, l:1536:16], T.PC[:, c0:c0 + 96], ["PCh", "SIN"], ["S%d" % l])
-        FF = (T.FL, T.FR)
+            o = 2 * S0[rn] + 384 * (side + c0 // 24)
+            return T.FS[:, o + 16 * c0 + i:o + 16 * c1:st]
+        return (T.FL, T.FR)[side][:, 16 * c0 + i:16 * c1:st]
+    rtok = lambda nm, rn, c0, c1: tok("%s%d" % (nm, min(rn, 3)), c0, c1)
 
-        def test(side, c0, c1, r, w, ext=()):
-            o0 = 96 + side * 96
-            tt(FF[side][:, 16 * c0:16 * c1], T.TB[:, 0:NT].indirect(T.OV[:, o0 + c0:o0 + c1]), T.NX[:, 16 * c0:16 * c1], A.is_lt,
-               TBT + ["O%d" % side, r], [w], ext=ext)
-        for j in range(nch):
+    def other(rn, c0, c1):
+        ac(nxt(rn, c0, c1), TBW.indirect(ov(rn, 0, c0, c1)), TBT + [otok(rn, 0, c0)], rtok("NX", rn, c0, c1), scale=-1.0, ext=HEXT, pick=True)
+
+    def near_tests(rn, c0, c1, w=NEAR_STEP):
+        for a, b in steps(c0, c1, w):
+            other(rn, a, b)
             for side in (0, 1):
-                test(side, cuts[j], min(cuts[j + 1], CA), "NX%d" % j, "F%d%d" % (side, j), HEXT if rn == 0 and j == 0 and side == 0 else ())
-            if not press and j == 0:
-                for side in (0, 1):
-                    o0 = 192 * (rn + 1) + 96
-                    cp(T.OPQ[:, o0 + side:o0 + 2 * C:2], P[2][:, 0:C], ["@2"], ["OQ%s%d" % ("b" * side, rn + 1)])
-        if not press:
-            later(2 * rn + 1)
-            if rn == 0:
-                later(5)
-            for side in (0, 1):
-                mm(run([(P[4 + side][:, 0:C], T.ZB[:, 15 - i:143 - i], FF[side][:, i:nn:16]) for i in range(16)], False, True),
-                   ["ZB"] + ["F%d%d" % (side, j) for j in range(nch)], ["@%d" % (4 + side)])
-                o0 = 192 * (rn + 1)
-                cp(T.OPQ[:, o0 + side:o0 + 2 * C:2], P[4 + side][:, 0:C], ["@%d" % (4 + side)], ["OP%s%d" % ("b" * side, rn + 1)])
-            continue
+                tt(fft(rn, side, a, b), TBW.indirect(ov(rn, 1 + side, a, b)), nxt(rn, a, b), A.is_lt,
+                   TBT + [otok(rn, 1, a)] + rtok("NX", rn, a, b), rtok("F%d" % side, rn, a, b), ext=HEXT, pick=True)
+
+    turns = [0]
+
+    def apart(rn, side, c0, c1):
+        j = turns[0] % 4
+        turns[0] += 1
+        b, w = APART[j], 16 * (c1 - c0)
+        raw = T.RW[:, 512 * j:512 * j + w]
+        ac(raw, TBW.indirect(ov(rn, 1 + side, c0, c1)), TBT + [otok(rn, 1, c0)], ["RW%d" % j], ext=HEXT, pick=True)
+        mm(run([(P[b][:, 0:w], T.NIB[:], nxt(rn, c0, c1))], True, False), ["NIB"] + rtok("NX", rn, c0, c1), ["@%d" % b])
+        mm(run([(P[b][:, 0:w], T.IDB[:], raw)], False, True), ["RW%d" % j, "IDB"], ["@%d" % b])
+        return lambda: af(fft(rn, side, c0, c1), P[b][:, 0:w], AF.Relu, -1.0, 0.0, ["@%d" % b], rtok("F%d" % side, rn, c0, c1))
+
+    def far_tests(rn, c0, c1):
+        for a, b in steps(c0, c1, FAR_STEP):
+            other(rn, a, b)
+        rest = [lambda: None]
         for side in (0, 1):
-            test(side, CA, 64, "NX%d" % (nch - 1), "FC%d" % side)
-        tt(T.PC[:, 288:576], P[6][:, 0:288], T.PC[:, 0:288], A.subtract, ["@6", "PCh"], ["PCl"])
-        for l, c0 in ((1, 288), (3, 384)):
-            cp(T.SIN[:, l:1536:16], T.PC[:, c0:c0 + 96], ["PCl", "SIN"], ["S%d" % l])
-        wn = WIN[rn - 2]
-        wt = "W%d" % (rn - 2)
-        E = 4 if rn == 2 else 1
+            for a, b in steps(c0, c1, FAR_STEP):
+                rest.append(apart(rn, side, a, b))
+                rest.pop(0)()
+        rest.pop()()
 
-        def kp(side, c0, c1, st=1):
-            return T.KP[:, 96 * side + c0:96 * side + c1:st]
-
-        def count(side, c0, c1, r):
-            b = 4 * side
-            mm(grp(P[b][:, c0:c1], [(sel(i), FF[side][:, 16 * c0 + i:16 * c1:16]) for i in range(16)]), ["Z"] + r, ["@%d" % b])
-            af(kp(side, c0, c1), P[b][:, c0:c1], AF.Relu, -1.0, 1.0, ["@%d" % b], ["KP%d%d" % (side, c0)])
-
-        def places(c0, c1):
-            kt = ["KP%d%d" % (sd, c) for sd in (0, 1) for c in (0, c0)]
-            u0 = max(c0, E)
-            lst = [(P[5][:, c0:c1], T.IDB[:], kp(0, c0, c1))]
-            for side in (0, 1):
-                for e in range(E):
-                    lst.append((P[5][:, c0:c1:E], T.TRB[:], kp(side, c0 + e, c1, E)))
-                    lst.append((P[5][:, u0:c1:E], T.TRU[:], kp(side, u0 - E + e, c1 - E, E)))
-            mm(run(lst, True, True), kt + ["TRB", "TRU", "IDB"], ["@5"])
-            for bank, sides in ((1, (0, 1)), (3, (1,))):
-                mm(run([(P[bank][:, c0 + x:c1:2], sw(ZX, x, gg), kp(sd, c0 + gg, c1, 2)) for sd in sides for x in (0, 1) for gg in (0, 1)],
-                       True, True), kt + ["ZX0", "ZX1"], ["@%d" % bank])
-                if bank == 1:
-                    mm(grp(P[2][:, c0:c1], [(T.IDB[:], T.JH[:, c0:c1]), (T.IDB[:], T.JC[:, c0:c1]), (T.NBG[:], kp(0, c0, c1)),
-                                            (T.NBG[:], kp(1, c0, c1))]), kt + ["NBG", "JH", "JC"], ["@2"])
-
-        def scatter(c0, c1):
-            init = T.SC[:, c0 - 1:c0] if c0 else 0.0
-            op("v", lambda: vec.tensor_tensor_scan(T.SC[:, c0:c1], P[5][:, c0:c1], kp(1, c0, c1), init, A.add, A.add),
-               ["@5", "KP1%d" % c0] + (["SC0"] if c0 else []), ["SC%d" % c0])
-            prods = ((6, 96, 1), (7, 384, 1), (8, 0, 1), (9, 288, 1), (4, 192, 3), (5, 480, 3))
-            for j, (l, p0, bank) in enumerate(prods):
-                tt(T.SIN[:, 16 * c0 + l:16 * c1:16], P[bank][:, c0:c1], T.PC[:, p0 + c0:p0 + c1], A.mult,
-                   ["@%d" % bank, "PCh", "PCl", "SIN"], ["S%d_%d" % (l, c0)])
-                if j == 1:
-                    tt(T.SC[:, 96 + c0:96 + c1], P[2][:, c0:c1], T.SC[:, c0:c1], A.max, ["@2", "SC%d" % c0], ["SO%d" % c0])
-            cp(T.OS[:, c0:c1], T.SC[:, 96 + c0:96 + c1], ["SO%d" % c0], ["OS%d" % c0])
-            op("v", lambda: vec.transpose(T.SRC[:, 16 * c0:16 * c1], T.SIN[:, 16 * c0:16 * c1]),
-               ["S0", "S1", "S2", "S3"] + ["S%d_%d" % (l, c0) for l in range(4, 10)], ["SRC%d" % c0])
-            cp(wn[:, 0:WINW].indirect(T.OS[:, c0:c1]), T.SRC[:, 16 * c0:16 * c1], ["OS%d" % c0, "SRC%d" % c0, wt], [wt])
-        for side in (0, 1):
-            count(side, 0, CA, ["F%d%d" % (side, j) for j in range(nch)])
-        places(0, CA)
-        for side, raw, nm, b in ((0, T.RP, "RP", 7), (1, T.RQ, "RQ", 6)):
-            o0 = 96 + 96 * side
-            ac(raw[:, 0:512], T.TB[:, 0:NT].indirect(T.OV[:, o0 + 64:o0 + 96]), ["O%d" % side], [nm + "a", nm + "b"])
-            mm(grp(P[b][:, 0:512], [(T.IDB[:], raw[:, 0:512]), (T.NIB[:], T.NX[:, 1024:1536])]), [nm + "a", "NXB", "NIB"], ["@%d" % b])
-        for side, b in ((0, 7), (1, 6)):
-            af(FF[side][:, 1024:1536], P[b][:, 0:512], AF.Relu, -1.0, 0.0, ["@%d" % b], ["FB%d" % side])
-        scatter(0, CA)
-        for side in (0, 1):
-            count(side, CA, 96, ["FB%d" % side, "FC%d" % side])
-        places(CA, 96)
-        scatter(CA, 96)
+    def inherited(out, rn, c0, c1):
         lst = []
-        for i in range(16):
-            sl = (lambda d: wn[:, 96 * i + d:96 * i + d + 96]) if rn == 4 else (lambda d: wn[:, i + d:i + d + 1536:16])
-            lst += grp(P[7][0:96, i:256:16], [(sl(1), T.WS[:, 0:16]), (sl(2), T.WS[:, 16:32])])
-        mm(lst, [wt] + WST, ["@7"])
-        cp(T.PT[0:96, 0:128], P[7][0:96, 0:128], ["@7"], ["PTp"])
-        turn(P[2][:, 0:96], T.PT[0:96, 0:128], 96, ["PTp"], ["@2"])
-        cp(T.PT[0:96, 128:256], P[7][0:96, 128:256], ["@7"], ["PTq"])
-        turn(P[3][:, 0:96], T.PT[0:96, 128:256], 96, ["PTq"], ["@3"])
-        cp(offp(rn + 1, 0, 96), P[2][:, 0:96], ["@2"], ["OP%d" % (rn + 1)])
-        cp(offq(rn + 1, 0, 96), P[3][:, 0:96], ["@3"], ["OQ%d" % (rn + 1)])
+        for h in range(c0 // 48, (c1 + 47) // 48):
+            lo, hi = max(c0, 48 * h), min(c1, 48 * h + 48)
+            for s in (0, 1):
+                o = 48 * (rn - 2 + h) + 24 * s - 24 * h
+                lst.append((out(lo - c0 + s, hi - c0), T.IDB[:], T.CN[:, o + lo // 2:o + hi // 2]))
+        return lst, ["IDB"] + ["CN%d" % (rn - 2 + h) for h in range(c0 // 48, (c1 + 47) // 48)]
+
+    def hand_down(rn, c0):
+        j = rn - 1 + c0 // 24
+        lst, r = [], []
+        for side in (0, 1) if rn > 1 else ():
+            l, r = inherited(lambda a, b: P[1][:, 24 * side + a:24 * side + b:2], rn, c0, c0 + 24)
+            lst += l
+        lst += [(P[1][:, 0:48], sel(i), T.FS[:, 768 * j + i:768 * j + 768:16]) for i in range(16)]
+        mm(run(lst, True, True), ["Z"] + r + rtok("F0", rn, c0, c0 + 24) + rtok("F1", rn, c0, c0 + 24), ["@1"])
+        ac(T.CN[:, 48 * j:48 * j + 48], P[1][:, 0:48], ["@1"], ["CN%d" % j])
+
+    def mixed(c0, c1):
+        n_ = c1 - c0
+        ac(T.VW[:, 0:n_], P[2][:, 0:n_], ["@2"], ["VWx"])
+        ac(T.VW[:, n_:3 * n_], P[3][:, 0:2 * n_], ["@3"], ["VWk"])
+        for j, (x, gg) in enumerate(((0, 0), (0, 1), (1, 0), (1, 1))):
+            mm(run([(P[6][:, x:3 * n_:2], sw(ZF, x, gg), T.VW[:, gg:3 * n_:2])], j == 0, j == 3), ["VWx", "VWk", "ZF0", "ZF1"], ["@6"])
+
+    sin = lambda l, c0, c1: T.SIN[:, 16 * c0 + l:16 * c1:16]
+
+    def halves(c0, c1):
+        n_ = c1 - c0
+        for q, l in enumerate((0, 2, 4)):
+            ac(sin(l, c0, c1), P[6][:, q * n_:(q + 1) * n_], ["@6", "SIN"], tok("S%d" % l, c0, c1))
+        for q, l in enumerate((0, 2, 4)):
+            tt(sin(l + 1, c0, c1), P[6][:, q * n_:(q + 1) * n_], sin(l, c0, c1), A.subtract, ["@6", "SIN"] + tok("S%d" % l, c0, c1),
+               tok("S%d" % (l + 1), c0, c1))
+
+    def kp(side, c0, c1, st=1):
+        return T.KP[:, 96 * side + c0:96 * side + c1:st]
+
+    def places(rn, c0, c1):
+        dump = P[5][:, 96 + c0:96 + c1]
+        mm(run([(dump, T.IDB[:], T.JH[:, c0:c1]), (dump, T.IDB[:], T.JC[:, c0:c1])], True, False), ["IDB", "JH", "JC"], ["@5"])
+        for side in (0, 1):
+            lst = [(P[4][:, 96 * side + c0:96 * side + c1], sel(i), fft(rn, side, c0, c1, i, 16)) for i in range(16)]
+            mm(run(lst, side == 0, side == 1), ["Z"] + rtok("F%d" % side, rn, c0, c1), ["@4"])
+            if rn == 3 and side == 0:
+                terms = [inherited(lambda a, b: P[4][:, o + a:o + b:2], 3, c0, c1) for o in (c0, 96 + c0)]
+                mm(run(terms[0][0] + terms[1][0], False, False), terms[0][1], ["@4"])
+        for side in (0, 1):
+            af(kp(side, c0, c1), P[4][:, 96 * side + c0:96 * side + c1], AF.Relu, -1.0, 1.0, ["@4"], tok("KP%d" % side, c0, c1))
+        E = 4 if rn == 3 else 1
+        kt = tok("KP0", max(c0 - E, 0), c1) + tok("KP1", max(c0 - E, 0), c1)
+        u0 = max(c0, E)
+        lst = [(P[5][:, c0:c1], T.IDB[:] if E > 1 else T.TRI[:], kp(0, c0, c1))]
+        for side in (0, 1):
+            for e in range(E):
+                if E > 1 or side:
+                    lst.append((P[5][:, c0:c1:E], T.TRB[:], kp(side, c0 + e, c1, E)))
+                lst.append((P[5][:, u0:c1:E], T.TRU[:], kp(side, u0 - E + e, c1 - E, E)))
+        lst += [(dump, T.NBG[:], kp(0, c0, c1)), (dump, T.NBG[:], kp(1, c0, c1))]
+        mm(run(lst, False, True), kt + ["TRB", "TRU", "TRI", "IDB", "NBG"], ["@5"])
+        mm(run([(P[4][:, 192 + 96 * sd + c0 + x:192 + 96 * sd + c1:2], sw(ZX, x, gg), kp(sd, c0 + gg, c1, 2))
+                for sd in (0, 1) for x in (0, 1) for gg in (0, 1)], True, True), kt + ["ZX0", "ZX1"], ["@4"])
+
+    def scatter(rn, c0, c1):
+        wn, wt = WIN[rn - 3], "W%d" % (rn - 3)
+        init = T.SC[:, c0 - 1:c0] if c0 else 0.0
+        op("v", lambda: vec.tensor_tensor_scan(T.SC[:, c0:c1], P[5][:, c0:c1], kp(1, c0, c1), init, A.add, A.add),
+           ["@5"] + tok("KP1", c0, c1) + (tok("SC", c0 - 1, c0) if c0 else []), tok("SC", c0, c1))
+        tt(T.SC[:, 96 + c0:96 + c1], P[5][:, 96 + c0:96 + c1], T.SC[:, c0:c1], A.max, ["@5"] + tok("SC", c0, c1), ["SO"])
+        cp(T.OS[:, c0:c1], T.SC[:, 96 + c0:96 + c1], ["SO"], tok("OS", c0, c1))
+        for sd in (0, 1):
+            cp(sin(6 + sd, c0, c1), P[4][:, 192 + 96 * sd + c0:192 + 96 * sd + c1], ["@4", "SIN"], tok("S%d" % (6 + sd), c0, c1))
+        src = T.SRC[:, 16 * c0:16 * c1]
+        turn32(src, T.SIN[:, 16 * c0:16 * c1], sum([tok("S%d" % l, c0, c1) for l in range(8)], ["SIN"]), tok("SRC", c0, c1))
+        op("v", lambda: vec.tensor_copy(wn[:, 0:WINW].indirect(T.OS[:, c0:c1]), src), tok("OS", c0, c1) + tok("SRC", c0, c1) + [wt], [wt],
+           cost=picked(src, SCATTER))
+
+    def press(rn):
+        ca, cs, cb = PARTS[rn]
+        near_tests(rn, 0, FIRST)
+        mixed(0, 96)
+        near_tests(rn, FIRST, ca)
+        places(rn, 0, ca)
+        near_tests(rn, ca, cs)
+        halves(0, 96)
+        if rn == 3:
+            far_tests(2, 24, 48)
+            hand_down(2, 24)
+        scatter(rn, 0, ca)
+        for a, b in ((ca, cb), (cb, 96)):
+            if b > a:
+                far_tests(rn, max(a, cs), b)
+                places(rn, a, b)
+                scatter(rn, a, b)
+
+    def read_back(rn, c0, c1):
+        wn = WIN[rn - 3]
+        for d, b, w0, w in ((1, 7, 0, 24), (2, 6, 24, 16)):
+            sl = (lambda i: wn[:, 96 * i + d:96 * i + d + 96]) if rn == 5 else (lambda i: wn[:, i + d:1536 + i + d:16])
+            mm(run([(P[b][0:96, i:16 * w:16], sl(i), T.WS[:, w0:w0 + w]) for i in range(16)], True, True), ["W%d" % (rn - 3)] + WST, ["@%d" % b])
+        row = lambda j, k=1: T.PT[0:96, 128 * j:128 * (j + k)]
+        ts(row(0, 2), P[7][0:96, 0:256], -float(BIG), A.add, ["@7"], ["PT0"], 0.0, A.max)
+        af(row(3), P[6][0:96, 0:128], AF.Relu, 1.0, -float(BIG), ["@6"], ["PT3"])
+        ts(row(2), P[7][0:96, 256:384], -float(BIG), A.add, ["@7"], ["PT2"], 0.0, A.max)
+        af(row(4), P[6][0:96, 128:256], AF.Relu, 1.0, -float(BIG), ["@6"], ["PT4"])
+        term = lambda b, j: (P[b][:, 0:96], row(j), T.IDF[0:96, 0:96])
+        mm(run([term(4, 0), term(4, 1)], True, False), ["PT0", "IDF"], ["@4"])
+        mm(run([term(4, 3)], False, True), ["PT3"], ["@4"])
+        mm(run([term(5, 2), term(5, 4)], True, True), ["PT2", "PT4"], ["@5"])
+        empty = 16.0 if rn == 5 else 0.0
+        ts(offp(rn - 2, c0, c1), P[4][:, c0:c1], empty, A.max, ["@4"], tok("OP%d" % (rn - 2), c0, c1))
+        ts(offq(rn - 2, c0, c1), P[5][:, c0:c1], empty, A.max, ["@5"], tok("OQ%d" % (rn - 2), c0, c1))
+
+    def rec(rn, e, nm, c0, c1):
+        if rn > 3 or rn == 1:
+            k = max(rn - 3, 0)
+            gather(e, nm, ITW, lambda a, b: (offp if nm == "P" else offq)(k, a, b), c0, c1, ITT + tok("O%s%d" % (nm, k), c0, c1))
+        else:
+            q = 1 if nm == "P" else 0
+            gather(e, nm, ITW, lambda a, b: ov(rn - 1, q, a, b), c0, c1, ITT + [otok(rn - 1, q, 0)])
+
+    decide_base(1, 0, 24)
+    rec(1, "v", "Q", 12, 24)
+    rec(1, "a", "Q", 0, 12)
+    key_terms("Q", [(0, 24, 0)], False, True)
+    decide(1, 0, 24)
+    for rn in (2, 3):
+        C, W = 24 << (rn - 1), XW[rn - 1]
+        hq, hp = SHARE[rn]
+        rec(rn, "a", "Q", 0, hq)
+        kid_lists(rn - 1, 0, C // 2)
+        ac(T.XF[:, 0:W], P[2][:, 0:W], ["@2"], ["XF"])
+        rec(rn, "v", "Q", hq, W)
+        key_terms("Q", [(0, W, 0), (W, C, W - C // 2)], True, False)
+        decide_base(rn, 0, C)
+        rec(rn, "a", "P", 0, hp)
+        rec(rn, "v", "P", hp, C)
+        key_terms("P", [(0, C, 0)], False, True)
+        kid_terms(0, C)
+        kid_copy(C)
+        decide(rn, 0, C)
+    kid_lists(3, 0, 96)
+    late_constants()
+    for rn in (1, 2):
+        near_tests(rn, 0, 24, 12)
+        hand_down(rn, 0)
+    press(3)
+    for rn in (4, 5):
+        read_back(rn - 1, 0, 96)
+        for nm in "PQ":
+            rec(rn, "a", nm, 0, 52 if nm == "P" else 48)
+            rec(rn, "v", nm, 52 if nm == "P" else 48, 96)
+        kid_terms(0, 96)
+        key_terms("P", [(0, 96, 0)], True, False)
+        decide_base(rn, 0, 96)
+        key_terms("Q", [(0, 96, 0)], False, True)
+        kid_copy(96)
+        decide(rn, 0, 96)
+        kid_lists(rn, 0, 96)
+        press(rn)
+    read_back(5, 0, 96)
 
     fi = lambda j: T.FIN[:, 96 * j:96 * j + 96]
-    gather(T.RP, "P", T.TB[:, 0:NT], 5, 96, [])
-    gather(T.RQ, "Q", T.TB[:, 0:NT], 5, 96, [])
-    mm(run([(P[4][:, 0:96], sel(i), T.RP[:, i:1536:16]) for i in range(16)], True, False), ["RPa", "RPb"], ["@4"])
-    mm(run([(P[4][:, 0:96], sel(i), T.RQ[:, i:1536:16]) for i in range(16)], False, True), ["RQa", "RQb"], ["@4"])
-    ac(fi(0), P[2][:, 0:96], ["@2"], ["pp"])
-    tt(fi(3), P[3][:, 0:96], fi(0), A.max, ["@3", "pp"], ["mx"])
-    tt(fi(2), P[3][:, 0:96], fi(0), A.min, ["@3", "pp"], ["mn"])
-    af(fi(7), fi(2), AF.Sign, 1.0, 0.0, ["mn"], ["ok"])
-    af(fi(8), fi(2), AF.Relu, 1.0, 1.0 - b0, ["mn"], ["f8"])
-    af(T.YO[:, 0:96], fi(8), AF.Identity, 1.0, -1.0, ["f8"], ["YA"])
-    dma("a", T.ya[:], T.YO[:, 0:96], ["YA"], ["oa_"])
-    ts(fi(4), fi(3), float(base(2)), A.is_ge, ["mx"], ["f4"], -32.0, A.mult)
-    ts(fi(5), fi(3), float(base(3)), A.is_ge, ["mx"], ["f5"], -32.0, A.mult)
-    tt(fi(6), fi(3), fi(4), A.add, ["f4"], ["f6"])
-    tt(fi(1), fi(6), fi(5), A.add, ["f6", "f5"], ["f7"])
-    tt(T.YO[:, 192:288], P[4][:, 0:96], fi(7), A.mult, ["@4", "ok"], ["YS"])
-    dma("s", T.ys[:], T.YO[:, 192:288], ["YS"], ["os_"])
-    ts(T.YO[:, 96:192], fi(1), -float(base(1)), A.add, ["f7"], ["YB"], -1.0, A.max)
-    dma("a", T.yb[:], T.YO[:, 96:192], ["YB"], ["ob_"])
-    op("s", None, ["oa_", "ob_", "os_"], (), kind="w")
-    op("g", None, (), (), kind="w", ext=[("ls", ls[0])])
+
+    def sizes(nm, off, h):
+        for e, c0, c1 in (("a", 0, h), ("v", h, 96)):
+            gather(e, nm, TBW, lambda a, b: off(3, a, b), c0, c1, tok("O%s3" % nm, c0, c1))
+        mm(run([(P[2][:, 0:96], sel(i), RR[nm][:, i:1536:16]) for i in range(16)], nm == "P", nm == "Q"), tok("R" + nm, 0, 96), ["@2"])
+    cp(fi(0), P[4][:, 0:96], ["@4"], ["pp"])
+    sizes("P", offp, 52)
+    for o, j, b, out in ((A.min, 0, b0, T.ya), (A.max, 1, base(1), T.yb)):
+        tt(fi(1 + j), P[5][:, 0:96], fi(0), o, ["@5", "pp"], ["m%d" % j])
+        ts(T.YO[:, 96 * j:96 * j + 96], fi(1 + j), -float(b), A.add, ["m%d" % j], ["Y%d" % j], -1.0, A.max)
+        dma("s", out[:], T.YO[:, 96 * j:96 * j + 96], ["Y%d" % j], ["o%d" % j])
+    sizes("Q", offq, 56)
+    ac(T.YO[:, 192:288], P[2][:, 0:96], ["@2"], ["YS"])
+    dma("a", T.ys[:], T.YO[:, 192:288], ["YS"], ["o2"])
+    op("s", None, ["o0", "o1", "o2"], (), kind="w")
+    op("g", None, (), (), kind="w", ext=[("ls", engines_out(T, topo, core, sends))])
+
+    hop = lambda j, i: HOP + (PE_HOP if ops[j]["e"] == "t" else 0.0)
+    hold = lambda i: 0.06 if ops[i]["kind"] == "d" else ops[i]["cost"]
+    when = {signal(rank + t, k): DUE.get(k, DUE["h"]) - (0.0 if late(t) else NEAR) for t in (1, 2, 3) for k in ITEMS}
+    due = lambda nm: when.get(nm, 0.0)
+    at_, busy = [], {e: [] for e in Q}
+    for i, o in enumerate(ops):
+        t0 = max([at_[j] + (ops[j]["cost"] + hop(j, i) if j in o["deps"] else hold(j)) for j in o["order"]]
+                 + [due(nm) for nm, v in o["ext"]] + [0.0])
+        for a, b in sorted(busy[o["e"]]):
+            if b > t0 and a < t0 + hold(i) - SLACK:
+                t0 = b
+        at_.append(t0)
+        busy[o["e"]].append((t0, t0 + hold(i)))
+    issued = [ops[i] for i in sorted(range(len(ops)), key=lambda i: (at_[i], i))]
 
     for o in ops:
         for j in o["deps"]:
             ops[j]["need"] = True
     cnt = {}
-    for o in ops:
+    for o in issued:
         if o["kind"] == "c" and o["need"]:
             cnt[o["e"]] = cnt.get(o["e"], 0) + 1
             o["name"] = "c" + o["e"]
@@ -607,7 +729,7 @@ def rank_program(g, core, T, topo):
         elif o["kind"] == "d":
             o["val"] = 16
     seen = {}
-    for o in ops:
+    for o in issued:
         e = o["e"]
         want = {}
         for j in o["deps"]:

from concourse.bass import DstId, RemoteDMATransfer
from concourse.mybir import AluOpType as A, ActivationFunctionType as AF

M = 2048
FAR = 3
NT = 32 + M * (FAR + 1)
BIG = 16384
WINW = 4704
ZW = 1568
LOADS = (0, 512, 1152, 1664, 2048)
HC = (0, 256, 512, 1152, 1664, 2048)
REC = {"c": (0, 384), "k": (384, 896)}
ITEMS = (0, "k", "c", 1, 2, 3, 4)
HELD = (0, 1, 4, 2, 3)
STREAM = (0, "k", "c")
CALLS = ((0, 1), (2,), ("k", 3), ("c", 4))
PLANE = {False: (1, 2, 3, 4), True: (1, 2, 3)}
OWN_DIE = (0, "k", "c", 3)
PARTS = {3: (48, 72, 96), 4: (44, 64, 96), 5: (44, 64, 96)}
PIECES = {1: ((0, 24),), 2: ((0, 48),), 3: ((0, 96),), 4: ((0, 96),), 5: ((0, 96),)}
SHARE = {2: (16, 24), 3: (64, 32)}
FIRST, NEAR_STEP, FAR_STEP = 8, 20, 32
APART = (7, 0, 2, 3)
CYCLE, PE_CYCLE, GATHER, SCATTER, CALL, HOP, PE_HOP, SLACK = 0.83e-3, 0.36e-3, 1.5, 3.5, 0.02, 0.21, -0.03, 0.02
DUE, NEAR = {"k": 9.0, "c": 10.0, "h": 13.0}, 2.0


def base(t):
    return 32 + M * t


SCRATCH = {}
for _n, _w in (("TB", NT), ("IT", NT), ("IN", 4 * M), ("HN", M), ("CI", 4 * 896), ("W0", WINW), ("W1", WINW), ("W2", WINW),
               ("RP", 1536), ("RQ", 1536), ("NX", 1536), ("FL", 1536), ("FR", 1536), ("SIN", 1536), ("SRC", 1536),
               ("NXS", 1152), ("FS", 2304), ("RW", 2048), ("CN", 144),
               ("Z", 160), ("ZS0", 160), ("ZS1", 160), ("ZX0", 160), ("ZX1", 160), ("IDB", 128), ("NIB", 128),
               ("NBG", 128), ("TRB", 128), ("TRU", 128), ("TRI", 128), ("WA", 32), ("WN", 32), ("WS", 40), ("WB", 48), ("ONB", 160),
               ("JH", 96), ("JC", 96), ("KP", 192)):
    SCRATCH[_n] = ("sbuf", [128, _w], "bfloat16")
for _n, _w in (("KF", 256), ("KT", 256), ("KLR", 256), ("WK", 128), ("K7", 128), ("SF", 24), ("YZ", 160), ("ONF", 160), ("B32", 128),
               ("V", 128), ("PF", 4), ("ZF0", 160), ("ZF1", 160), ("IDF", 128), ("MK", 128), ("MM", 384), ("VT", 256),
               ("VW", 288), ("SC", 192), ("PT", 640), ("XF", 64), ("FIN", 288), ("YO", 288), ("SEL", 240)):
    SCRATCH[_n] = ("sbuf", [128, _w], "float32")
for _n, _w in (("KI", 256), ("SAB", 48), ("PI", 2), ("PJ", 2)):
    SCRATCH[_n] = ("sbuf", [128, _w], "int32")
for _n, _w in (("OPQ", 4 * 192), ("OV", 5 * 288), ("OS", 96)):
    SCRATCH[_n] = ("sbuf", [128, _w], "uint16")
for _b in range(8):
    SCRATCH["P%d" % _b] = ("psum", [128, 512], "float32")

SEMAPHORES = ["cg", "cv", "ca", "ct", "ls"] + ["d%d" % i for i in range(14)] + ["x%s_%d" % (k, s) for k in ITEMS for s in range(FAR + 1)]


def routes(T, topo):
    cores = list(T.cores)
    n = len(cores)
    sends = {c: (s, []) for s, c in enumerate(cores)}

    but = lambda items: tuple(k for k in ITEMS if k not in items)

    def relay(s, c0, die, to, items):
        c = [c for c in topo.cores_of(c0) if c not in sends and topo.die(c) == die and all(topo.may_write(c, x[0]) for x in to)][0]
        sends[c] = (s, to)
        sends[cores[s]][1].append((c, None, items))
        return c

    for s in range(n):
        cs, die = cores[s], topo.die(cores[s])
        other = [d for d in set(topo.die(c) for c in topo.cores_of(cs)) if d != die][0]
        by_chip = {}
        for d in range(1, FAR + 1):
            by_chip.setdefault(topo.chip(cores[(s - d) % n]), []).append((cores[(s - d) % n], d))
        pair = [rs for rs in by_chip.values() if len(rs) > 1][0]
        one = [rs[0] for rs in by_chip.values() if len(rs) == 1][0]
        home = topo.chip(one[0]) == topo.chip(cs)
        far = not topo.mates(topo.chip(cs), topo.chip(pair[0][0]))
        plane = PLANE[home] if far else ()
        fan = relay(s, pair[0][0], die, [r + (ITEMS,) for r in pair], but(plane))
        if far:
            c0 = [c for c in cores if topo.mates(topo.chip(c), topo.chip(fan))][0]
            relay(s, c0, die, [(fan, None, plane)] + ([] if home else [one + (plane,)]), plane)
        if home:
            sends[cs][1].append(one + (ITEMS,))
        else:
            for d, items in ((other, but(plane)),) if far else ((die, OWN_DIE), (other, but(OWN_DIE))):
                relay(s, cs, d, [one + (items,)], items)
    return sends


def staged(T, k):
    return T.CI[:, REC[k][0]:REC[k][1]] if k in REC else T.HN[:, HC[k]:HC[k + 1]]


def landing(T, t, k):
    if t is None:
        return staged(T, k)
    if k in REC:
        return T.CI[:, 896 * t + REC[k][0]:896 * t + REC[k][1]]
    return T.TB[:, base(t) + HC[k]:base(t) + HC[k + 1]]


def signal(s, k):
    return "x%s_%d" % (k, s % (FAR + 1))


def transfers(T, topo, core, sends, k):
    to = sorted([(c, t) for (c, t, items) in sends[core][1] if k in items], key=lambda x: topo.chip(x[0]) != topo.chip(core))
    off = topo.engines(core, [c for c in T.cores if topo.chip(c) != topo.chip(core)][0])
    out = []
    for j, (c, t) in enumerate(to):
        es = off if j or topo.chip(c) != topo.chip(core) else [e for e in topo.engines(core, c) if e not in off]
        if core in T.cores:
            es = es[:len(es) // 2] if k in STREAM else es[len(es) // 2:]
        out.append((es, c, t))
    return out


def engines_in(T, topo, core, sends, s, k):
    return [len(es) for a in sends if sends[a][0] == s for es, c, t in transfers(T, topo, a, sends, k) if c == core][0]


def engines_out(T, topo, core, sends):
    return sum(len(es) for k in ITEMS for es, c, t in transfers(T, topo, core, sends, k))


def call(g, T, topo, core, sends, ks):
    return g.remote_dma_fused([RemoteDMATransfer(dst_ids=[DstId(rid=topo.addr(c)[0], pnc=topo.addr(c)[1])], dma_engine_mask=sum(1 << e for e in es),
                                                 remote_sem=T.sem[signal(sends[core][0], k)], src=staged(T, k), dst=landing(T, t, k))
                               for k in ks for es, c, t in transfers(T, topo, core, sends, k)], local_sem=T.sem.ls)


def relay_program(g, core, T, topo, sends):
    s, to = sends[core]
    for k in ITEMS if "k" in to[0][2] or to[0][1] is None else HELD:
        if transfers(T, topo, core, sends, k):
            g.wait_ge(T.sem[signal(s, k)], engines_in(T, topo, core, sends, s, k))
            call(g, T, topo, core, sends, [k])
    g.wait_ge(T.sem.ls, engines_out(T, topo, core, sends))


def rank_program(g, core, T, topo):
    sends = routes(T, topo)
    rank = T.rank_of(core)
    if rank is None:
        if core in sends:
            relay_program(g, core, T, topo, sends)
        return
    n = len(T.cores)
    Q = {"g": g, "v": g.vector, "a": g.scalar, "t": g.tensor, "s": g.sync}
    ops = []
    wr = {}
    rd = {}
    last = {}
    ndma = [0]

    def op(e, fn, r=(), w=(), kind="c", ext=(), cost=0.06):
        me = len(ops)
        deps, order = set(), set()
        for x in r:
            if x in wr:
                deps.add(wr[x])
            if x[0] == "@":
                deps.update(j for j in rd.get(x, []) if ops[j]["e"] != e)
        for x in w:
            deps.update(rd.get(x, []) + ([wr[x]] if x in wr else []))
        order.update(deps)
        if e == "t":
            deps = set(j for j in deps if ops[j]["e"] != "t")
        if e in "gs" or kind == "d":
            order.update([last[e]] if e in last else [])
            last[e] = me
        o = {"e": e, "fn": fn, "deps": deps, "order": order, "kind": kind, "ext": list(ext), "need": False, "cost": cost}
        if kind == "d":
            o["name"] = "d%d" % ndma[0]
            ndma[0] += 1
        ops.append(o)
        for x in r:
            rd.setdefault(x, []).append(me)
        for x in w:
            wr[x] = me
            rd[x] = []
        return me

    def late(t):
        return topo.chip(T.cores[(rank + t) % n]) != topo.chip(core)

    vec, act, pe = g.vector, g.scalar, g.tensor
    wide = lambda x: "float32" in str(x.dtype) or "int32" in str(x.dtype).replace("uint", "")
    els = lambda x, rate=1.0: CALL + CYCLE * max(64, rate * x.shape[1])
    picked = lambda x, rate: 0.06 + CYCLE * rate * x.shape[1]

    def ts(out, in0, s1, o0, r, w, s2=None, o1=None):
        if o1 is None:
            op("v", lambda: vec.tensor_scalar(out, in0, s1, None, o0), r, w, cost=els(out))
        else:
            op("v", lambda: vec.tensor_scalar(out, in0, s1, s2, o0, o1), r, w, cost=els(out))

    def tt(out, a, b, o, r, w, ext=(), pick=False):
        psum = [x for x in list(r) + list(w) if x[0] == "@"]
        op("v", lambda: vec.tensor_tensor(out, a, b, o), r, w, ext=ext, cost=picked(out, GATHER) if pick else els(out, 1.0 if psum else 2.0))

    def cp(out, a, r, w, ext=(), pick=False):
        op("v", lambda: vec.tensor_copy(out, a), r, w, ext=ext, cost=picked(out, GATHER) if pick else els(out, 1.0 if wide(out) or wide(a) else 0.5))

    def ms(out, c, w):
        op("v", lambda: vec.memset(out, c), (), w, cost=els(out, 0.5))

    def ac(out, a, r, w, scale=1.0, ext=(), pick=False):
        op("a", lambda: act.activation(out, a, AF.Copy, scale=scale), r, w, ext=ext, cost=picked(out, GATHER) if pick else els(out))

    def af(out, a, f, scale, bias, r, w):
        op("a", lambda: act.activation(out, a, f, bias=bias, scale=scale), r, w, cost=els(out))

    def turn32(out, in_, r, w):
        op("v", lambda: vec.transpose(out, in_), r, w, cost=els(out, 1.0 if wide(out) else 0.5))

    def mm(lst, r, w):
        def fn():
            ins = None
            for (out, l, x, st, sp) in lst:
                ins = pe.matmul(out, l, x, st, sp)
            return ins
        op("t", fn, r, w, cost=sum(PE_CYCLE * (4 if wide(l) else 1) * max(min(64, l.shape[1]), x.shape[1]) for (out, l, x, st, sp) in lst))

    def grp(out, terms):
        return [(out, l, x, j == 0, j == len(terms) - 1) for j, (l, x) in enumerate(terms)]

    def run(trip, opens, closes):
        return [(o_, l, x, opens and j == 0, closes and j == len(trip) - 1) for j, (o_, l, x) in enumerate(trip)]

    def dma(e, out, in_, r, w, cost=None):
        op(e, lambda: Q[e].dma_start(out, in_), r, w, kind="d", cost=cost or 2.2 + 0.15 * ndma[0])

    def iota(out, pat, b, w):
        op("g", lambda: g.iota(out, pat, b, 0, allow_small_or_imprecise_dtypes=True), (), w, cost=0.13 + 2 * CYCLE * out.shape[1])

    def steps(c0, c1, w):
        return [(c, min(c + w, c1)) for c in range(c0, c1, w)]

    P = [T["P%d" % b] for b in range(8)]
    col = lambda t, j: t[:, j:j + 1]
    tok = lambda nm, c0, c1: ["%s_%d" % (nm, c) for c in range(c0 // 4, (c1 + 3) // 4)]
    HNT = ["HN%d" % k for k in range(len(LOADS) - 1)]

    load = lambda e, j: dma(e, T.HN[:, LOADS[j]:LOADS[j + 1]], T.h[:, LOADS[j]:LOADS[j + 1]], (), [HNT[j]])
    load("s", 0)
    dma("a", T.KI[1:128:2, :], T.kr[:], (), ["KIb"])
    dma("s", T.KI[0:128:2, :], T.kl[:], (), ["KIa"])
    for e, j in (("a", 1), ("s", 2), ("a", 3)):
        load(e, j)
    dma("s", T.SAB[:, 0:24], T.sa[:], (), ["SA"], 7.0)
    dma("s", T.SAB[:, 24:48], T.sb[:], (), ["SB"], 7.0)
    b0 = base(0)
    dma("s", T.TB[0:128:2, b0:b0 + M], T.h[1:128:2, :], HNT, ["T0a"], 5.0)
    dma("s", T.TB[1:128:2, b0:b0 + M], T.h[0:128:2, :], (), ["T0b"], 5.0)

    def pick(out, in_, pat, cmp_, b, cm, r, w):
        op("g", lambda: g.affine_select(out, in_, pat, cmp_, 0.0, b, cm), r, w, cost=0.17 + 2 * CYCLE * out.shape[1])

    def band(out, in_, pat, lo, hi, r, w):
        pick(out, in_, pat, A.is_ge, -lo, 1, r, w)
        pick(out, out, [[-st, k] for st, k in pat], A.is_ge, hi, -1, w, w)

    op("g", lambda: g.iota(T.PI[:], [[0, 2]], 0, 1), (), ["PI"], cost=0.14)
    iota(T.YZ[:], [[32, 5], [1000, 32]], -31000, ["YZ"])
    iota(T.B32[:], [[32, 64], [0, 2]], 0, ["B32"])
    iota(T.WA[:], [[0, 32]], 1, ["WA"])
    band(T.WA[:], T.WA[:], [[-4, 4], [-16, 8]], 0, 3, ["WA"], ["WA"])
    op("g", lambda: g.iota(col(T.PF, 2), [[0, 1]], 33, 1, allow_small_or_imprecise_dtypes=True), (), ["P33"], cost=0.14)
    for j, mk in enumerate((112, 31)):
        ts(col(T.PJ, j), col(T.PI, j), mk, A.bitwise_and, ["PI"], ["PJ%d" % j])
    cp(T.PF[:, 0:2], T.PJ[:], ["PJ0", "PJ1"], ["PF"])
    cG16, cP32 = col(T.PF, 0), col(T.PF, 1)
    ZS, ZX, ZF = (T.ZS0, T.ZS1), (T.ZX0, T.ZX1), (T.ZF0, T.ZF1)
    for x in (0, 1):
        ts(ZS[x][:], T.YZ[:], cG16, A.subtract, ["YZ", "PF"], ["ZS%d" % x], -16.0 * x, A.is_equal)
    ts(T.V[:], T.B32[:], cP32, A.add, ["B32", "PF"], ["V"], 1.0 / BIG, A.mult)

    lst = []
    for x in (0, 1):
        lst += grp(P[0][:, x:128:2], [(ZS[x][:, 31 - y:159 - y], T.HN[:, y:M:32]) for y in range(32)])
    mm(lst, ["ZS0", "ZS1"] + HNT, ["@0"])

    cp(T.KF[:], T.KI[:], ["KIa", "KIb"], ["KF"])
    turn32(T.KT[:], T.KF[:], ["KF"], ["KT"])
    for side in (0, 1):
        for sg in range(8):
            c0 = 128 * side + 16 * sg
            (ac if sg % 2 else cp)(T.KLR[:, c0:c0 + 16], T.KT[:, 2 * sg + side:256:16], ["KT"], ["K%d%d" % (side, sg)])
    KL, KR = T.KLR[:, 0:128], T.KLR[:, 128:256]
    KLT = ["K0%d" % sg for sg in range(8)]
    ci = lambda j, k=1, t=0: T.CI[:, 896 * t + 128 * j:896 * t + 128 * (j + k)]
    leaf, left, key, right = P[1][:, 0:128], P[2][:, 0:128], P[3][:, 0:128], P[4][:, 0:128]
    ts(leaf, KL, 0.0, A.is_equal, KLT, ["@1"], float(BIG), A.mult)
    tt(P[5][:, 0:128], leaf, T.V[:], A.mult, ["@1", "V"], ["@5"])
    tt(right, KR, leaf, A.subtract, ["@1"] + ["K1%d" % sg for sg in range(8)], ["@4"])
    tt(left, P[5][:, 0:128], KL, A.add, ["@5"] + KLT, ["@2"])
    ts(T.WK[:], leaf, -float(2 ** 22 // BIG), A.mult, ["@1"], ["w4"], float(2 ** 21), A.add)
    ac(ci(4), right, ["@4"], ["c4"])
    cp(ci(3), left, ["@2"], ["c3"])
    tt(ci(5), left, ci(3), A.subtract, ["@2", "c3"], ["c5"])
    tt(ci(6), right, ci(4), A.subtract, ["@4", "c4"], ["c6"])
    tt(key, P[0][:, 0:128], T.WK[:], A.min, ["@0", "w4"], ["@3"])
    ts(T.K7[:], key, 1.5 * 2 ** 30, A.add, ["@3"], ["k7"], 1.5 * 2 ** 30, A.subtract)
    ts(ci(0), key, 1.5 * 2 ** 38, A.add, ["@3"], ["c0"], 1.5 * 2 ** 38, A.subtract)
    tt(ci(2), key, T.K7[:], A.subtract, ["@3", "k7"], ["c2"])
    tt(ci(1), T.K7[:], ci(0), A.subtract, ["k7", "c0"], ["c1"])
    CIT = {"c": ["c0", "c1", "c2"], "k": ["c3", "c4", "c5", "c6"]}

    arrival = lambda t, k: (signal(rank + t, k), engines_in(T, topo, core, sends, (rank + t) % n, k))
    loaded = lambda k: [HNT[j] for j in range(len(HNT)) if LOADS[j] < HC[k + 1] and HC[k] < LOADS[j + 1]]
    for ks in CALLS:
        op("g", lambda ks=ks: call(g, T, topo, core, sends, ks), sum([CIT[k] if k in REC else loaded(k) for k in ks], []), (), kind="r",
           cost=0.4 + 1.2 * (ks == CALLS[0]))
    iota(T.ONF[:], [[0, 160]], 1, ["ONF"])
    pick(T.IDF[:], T.ONF[:, 0:128], [[-1, 128]], A.is_equal, 0, 1, ["ONF"], ["IDF"])
    SELS = {1: (0, [[0, 2], [-1, 24]]), 2: (48, [[0, 2], [-1, 24], [-24, 2]]), 3: (144, [[-1, 48], [-48, 2]])}
    iota(T.IT[:, 0:32], [[0, 32]], 0, ["ID"])
    for lv, (s0, pat) in SELS.items():
        w = 48 if lv == 1 else 96
        pick(T.SEL[:, s0:s0 + w], T.ONF[:, 0:w], pat, A.is_equal, 0, 1, ["ONF"], ["SEL%d" % lv])
    iota(T.TB[:, 0:16], [[0, 16]], -131072, ["TD"])
    iota(T.TB[:, 16:32], [[0, 16]], 0, ["TZ"])
    iota(T.ONB[:], [[0, 160]], 1, ["ONB"])
    pick(T.Z[:], T.ONB[:], [[0, 10], [1, 16]], A.is_equal, -15, 0, ["ONB"], ["Z"])
    band(T.Z[:], T.Z[:], [[-1, 160]], -15, 0, ["Z"], ["Z"])
    pick(T.ZF1[:], T.ONF[:], [[-1, 160]], A.is_equal, 16, 1, ["ONF"], ["ZF1"])
    for x in (0, 1):
        pick(ZF[x][:], T.ZF1[:], [[0, 5], [1, 2], [0, 16]], A.is_equal, x - 1, 0, ["ZF1"], ["ZF%d" % x])
    band(T.TRU[:], T.ONB[:, 0:128], [[-16, 8], [0, 16]], 0, 15, ["ONB"], ["TRU"])
    pick(T.TRB[:], T.TRU[:], [[1, 128]], A.is_gt, 0, -1, ["TRU"], ["TRB"])
    pick(T.TRI[:], T.TRU[:], [[1, 128]], A.is_ge, 0, -1, ["TRU"], ["TRI"])
    pick(T.TRU[:], T.TRU[:], [[-1, 128]], A.is_gt, 0, 1, ["TRU"], ["TRU"])
    iota(T.JC[:], [[1, 96]], 0, ["JC"])
    WIN = (T.W0, T.W1, T.W2)
    iota(T.SIN[:], [[0, 1536]], 0, ["SIN"])
    iota(WIN[0][:, 0:ZW], [[0, ZW]], 0, ["W0"])
    iota(T.SIN[:, 8:1536:16], [[0, 96]], 1, ["SIN"])
    iota(T.WB[:], [[0, 48]], BIG, ["WB"])
    for j, lo in enumerate((2, 4, 0, 2, 0)):
        band(T.WS[:, 8 * j:8 * j + 8], T.ONB[:, 0:8], [[-16, 8]], lo, lo + 1, ["ONB"], ["WS%d" % j])
    for j, (lo, hi) in enumerate(((8, 8), (7, 7), (6, 7))):
        band(T.WB[:, 16 * j:16 * j + 16], T.WB[:, 16 * j:16 * j + 16], [[0, 2], [-16, 8]], lo, hi, ["WB"], ["WB%d" % j])
    for k in (1, 2):
        iota(WIN[k][:, 0:ZW], [[0, ZW]], 0, ["W%d" % k])

    LANE = (0, 1, 2, 4, 8, 5, 9)

    def lane(t, l, k=1, st=16):
        return T.IN[:, M * t + l:M * (t + k):st]

    ms(lane(0, 2, 4, 4), 0.0, ["cz"])
    for t in range(4):
        ms(lane(t, 3, 1, 4), float(base(t)), ["cb%d" % t])
        ac(lane(t, 12), T.B32[:], ["B32"], ["cc%d" % t])
    ms(lane(0, 3), 0.5, ["cb0"])
    ms(lane(1, 3, 3), 0.0, ["cb1", "cb2", "cb3"])
    af(lane(0, 13, 4), lane(0, 6, 4), AF.Identity, 0.0, cP32, ["cz", "PF"], ["cp"])

    def fill(t, k, js, f):
        for j in js:
            f(lane(t, LANE[j]), ci(j, 1, t), ["cz"] + ([] if t else CIT[k]), ["IN%d_%d" % (t, j)], ext=[arrival(t, k)] if t else [])

    def turn_tree(t):
        turn32(T.IT[:, base(t):base(t) + M], T.IN[:, M * t:M * t + M],
               ["IN%d_%d" % (t, j) for j in range(7)] + ["cz", "cp", "cb%d" % t, "cc%d" % t], ["IT%d" % t])

    ts(T.WA[:, 24:32], T.WA[:, 24:32], -1.0, A.mult, ["WA"], ["WA"])
    WAT = ["WA"]
    WST = ["WS%d" % j for j in range(5)]

    offp = lambda k, c0, c1: T.OPQ[:, 192 * k + c0:192 * k + c1]
    offq = lambda k, c0, c1: T.OPQ[:, 192 * k + 96 + c0:192 * k + 96 + c1]
    ts(offp(0, 0, 24), T.SAB[:, 0:24], float(b0), A.add, ["SA"], tok("OP0", 0, 24))
    ts(offq(0, 0, 24), T.SAB[:, 24:48], float(base(1)), A.add, ["SB"], tok("OQ0", 0, 24))
    ts(T.SF[:], T.SAB[:, 24:48], float(base(1)), A.add, ["SB"], ["s0"])
    fill(0, "k", (3, 4, 5, 6), ac)
    fill(0, "c", (0, 1, 2), ac)
    turn_tree(0)
    ac(T.WN[:], T.WA[:], WAT, ["WN"], scale=-1.0)
    RR = {"P": T.RP, "Q": T.RQ}

    def gather(e, nm, win, off, c0, c1, r):
        if c1 > c0:
            (ac if e == "a" else cp)(RR[nm][:, 16 * c0:16 * c1], win.indirect(off(c0, c1)), r, tok("R" + nm, c0, c1), pick=True)

    def key_terms(nm, segs, opens, closes):
        w = T.WN if nm == "P" else T.WA
        lst = [(P[0][r0:r1, i:512:16], RR[nm][:, 16 * q0 + i:16 * (q0 + r1 - r0):16], w[:]) for i in range(16) for (r0, r1, q0) in segs]
        if len(segs) > 1:
            lst = [(P[0][0:segs[-1][1], 0:512:16], T.HN[:, 0:segs[-1][1]], T.IT[:, 0:32])] + lst
        mm(run(lst, opens, closes), WAT + ["WN"] + ["ID"] * (len(segs) > 1) + sum([tok("R" + nm, q0, q0 + r1 - r0) for (r0, r1, q0) in segs], []), ["@0"])

    def kid_terms(c0, c1):
        mm(run([(P[1][0:c1 - c0, i:256:16], T.RP[:, 16 * c0 + i:16 * c1:16], T.WA[:, 8:24]) for i in range(16)], True, True),
           tok("RP", c0, c1) + WAT, ["@1"])

    def kid_copy(n_):
        ac(T.VT[0:n_, :], P[1][0:n_, 0:256], ["@1"], ["VT"])

    for e, c0 in (("a", 0), ("v", 12)):
        gather(e, "P", T.IT[:, 0:base(1)], lambda a, b: offp(0, a, b), c0, c0 + 12, ["IT0", "ID"] + tok("OP0", c0, c0 + 12))
    kid_terms(0, 24)
    key_terms("P", [(0, 24, 0)], True, False)
    kid_copy(24)

    def late_constants():
        ac(T.IDB[:], T.IDF[:], ["IDF"], ["IDB"])
        ac(T.NIB[:], T.IDF[:], ["IDF"], ["NIB"], scale=-1.0)
        ac(T.NBG[:], T.IDF[:], ["IDF"], ["NBG"], scale=-8192.0)
        for x in (0, 1):
            ac(ZX[x][:], ZF[x][:], ["ZF%d" % x], ["ZX%d" % x])
        ts(col(T.PF, 3), col(T.PF, 2), cG16, A.subtract, ["PF", "P33"], ["PF3"], 96.0, A.mult)
        af(T.JH[:], T.B32[:, 0:96], AF.Identity, 0.0, col(T.PF, 3), ["B32", "PF3"], ["JH"])
        w8 = lambda t, j, k: t[:, 8 * j:8 * (j + k)]
        for j, k, jb, o in ((0, 1, 0, A.add), (0, 1, 2, A.subtract), (1, 1, 2, A.add), (2, 1, 0, A.add), (3, 2, 4, A.add), (3, 2, 0, A.subtract)):
            tt(w8(T.WS, j, k), w8(T.WS, j, k), w8(T.WB, jb, k), o, ["WB%d" % (jb // 2)] + WST[j:j + k], WST[j:j + k])

    for t in (1, 2, 3):
        if not late(t):
            fill(t, "k", (3, 4, 5, 6), ac)
            fill(t, "c", (0, 1, 2), ac)
            turn_tree(t)
    far = [t for t in (1, 2, 3) if late(t)]
    for t in far:
        fill(t, "k", (3, 4), ac)
        fill(t, "k", (5, 6), cp)
    for j, t in enumerate(far):
        fill(t, "c", (0,) if j == 0 else (0, 1, 2), ac)
        fill(t, "c", (1, 2) if j == 0 else (), cp)
        turn_tree(t)
    ITT = ["IT%d" % t for t in range(4)] + ["ID"]
    TBT = ["T0a", "T0b", "TD", "TZ"]
    HEXT = [arrival(t, k) for t in (1, 2, 3) for k in range(len(HC) - 1)]
    sel = lambda i: T.Z[:, 15 - i:143 - i]
    sw = lambda zz, x, gg: zz[x][:, 16 - 16 * (gg - x):144 - 16 * (gg - x)]
    ITW, TBW = T.IT[:, 0:NT], T.TB[:, 0:NT]

    XW = {1: 32, 2: 64}
    piece = lambda rn, c: [x for x in PIECES[rn] if x[0] <= c][-1]

    def ov(rn, q, a, b):
        c0, c1 = piece(rn, a)
        w = XW.get(rn, c1 - c0)
        o = 288 * (rn - 1) + 3 * c0 + (0, w, w + c1 - c0)[q] - c0
        return T.OV[:, o + a:o + b]
    otok = lambda rn, q, c: "O%d%d_%d" % (rn, min(q, 1), piece(rn, c)[0])

    def decide_base(rn, c0, c1):
        n_ = c1 - c0
        if rn == 1:
            lst = [(P[2][:, 0:24], T.IDF[:], T.SF[:, 0:24]), (P[2][:, 24:32], T.IDF[:], T.SF[:, 0:8])]
        elif rn < 4:
            w = XW.get(rn, n_)
            lst = [(P[2][:, s:w:2], T.IDF[:], T.XF[:, 0:w // 2]) for s in (0, 1)]
        else:
            lst = [(P[2][:, 0:n_], T.PT[0:n_, 128 * j:128 * j + 128], T.IDF[0:n_, 0:n_]) for j in (2, 4)]
        mm(run(lst, True, False), ["s0", "XF", "IDF", "PT2", "PT4"], ["@2"])

    def decide(rn, c0, c1):
        n_ = c1 - c0
        w = XW.get(rn, n_)
        S, s0 = (T.SEL, SELS[rn][0]) if rn in SELS else (T.IDF, 0)
        dst = ((P[3][:, 0:n_], n_), (P[3][:, n_:2 * n_], n_), (P[2][:, 0:w], w))
        term = lambda src, q: (dst[q][0], src[0:n_, 128 * q:128 * q + 128], S[0:n_, s0:s0 + dst[q][1]])
        st = ["SEL%d" % rn, "IDF"]
        early = rn not in (2, 3)
        kid_base = lambda opens, closes: mm(run([term(T.VT, 0), term(T.VT, 1)], opens, closes), ["VT"] + st, ["@3"])
        if early:
            kid_base(True, False)
        ts(T.MK[0:n_, :], P[0][0:n_, 0:128], 0.0, A.is_ge, ["@0"], ["qo"])
        for q in (2, 0, 1):
            tt(T.MM[0:n_, 128 * q:128 * q + 128], P[0][0:n_, 128 * q + 128:128 * q + 256], T.MK[0:n_, :], A.mult, ["@0", "qo"], ["m%d" % q])
            mm(run([term(T.MM, q)], q == 0 and not early, q == 2 or (q == 1 and early)), ["m%d" % q] + st, ["@2" if q == 2 else "@3"])
        if not early:
            kid_base(False, True)
        cp(ov(rn, 0, c0, c0 + w), P[2][:, 0:w], ["@2"], [otok(rn, 0, c0)])

    def kid_lists(rn, c0, c1):
        cp(ov(rn, 1, c0, 2 * c1 - c0), P[3][:, 0:2 * (c1 - c0)], ["@3"], [otok(rn, 1, c0)])

    S0 = {1: 0, 2: 384}
    nxt = lambda rn, c0, c1: T.NXS[:, S0[rn] + 16 * c0:S0[rn] + 16 * c1] if rn < 3 else T.NX[:, 16 * c0:16 * c1]

    def fft(rn, side, c0, c1, i=0, st=1):
        if rn < 3:
            o = 2 * S0[rn] + 384 * (side + c0 // 24)
            return T.FS[:, o + 16 * c0 + i:o + 16 * c1:st]
        return (T.FL, T.FR)[side][:, 16 * c0 + i:16 * c1:st]
    rtok = lambda nm, rn, c0, c1: tok("%s%d" % (nm, min(rn, 3)), c0, c1)

    def other(rn, c0, c1):
        ac(nxt(rn, c0, c1), TBW.indirect(ov(rn, 0, c0, c1)), TBT + [otok(rn, 0, c0)], rtok("NX", rn, c0, c1), scale=-1.0, ext=HEXT, pick=True)

    def near_tests(rn, c0, c1, w=NEAR_STEP):
        for a, b in steps(c0, c1, w):
            other(rn, a, b)
            for side in (0, 1):
                tt(fft(rn, side, a, b), TBW.indirect(ov(rn, 1 + side, a, b)), nxt(rn, a, b), A.is_lt,
                   TBT + [otok(rn, 1, a)] + rtok("NX", rn, a, b), rtok("F%d" % side, rn, a, b), ext=HEXT, pick=True)

    turns = [0]

    def apart(rn, side, c0, c1):
        j = turns[0] % 4
        turns[0] += 1
        b, w = APART[j], 16 * (c1 - c0)
        raw = T.RW[:, 512 * j:512 * j + w]
        ac(raw, TBW.indirect(ov(rn, 1 + side, c0, c1)), TBT + [otok(rn, 1, c0)], ["RW%d" % j], ext=HEXT, pick=True)
        mm(run([(P[b][:, 0:w], T.NIB[:], nxt(rn, c0, c1))], True, False), ["NIB"] + rtok("NX", rn, c0, c1), ["@%d" % b])
        mm(run([(P[b][:, 0:w], T.IDB[:], raw)], False, True), ["RW%d" % j, "IDB"], ["@%d" % b])
        return lambda: af(fft(rn, side, c0, c1), P[b][:, 0:w], AF.Relu, -1.0, 0.0, ["@%d" % b], rtok("F%d" % side, rn, c0, c1))

    def far_tests(rn, c0, c1):
        for a, b in steps(c0, c1, FAR_STEP):
            other(rn, a, b)
        rest = [lambda: None]
        for side in (0, 1):
            for a, b in steps(c0, c1, FAR_STEP):
                rest.append(apart(rn, side, a, b))
                rest.pop(0)()
        rest.pop()()

    def inherited(out, rn, c0, c1):
        lst = []
        for h in range(c0 // 48, (c1 + 47) // 48):
            lo, hi = max(c0, 48 * h), min(c1, 48 * h + 48)
            for s in (0, 1):
                o = 48 * (rn - 2 + h) + 24 * s - 24 * h
                lst.append((out(lo - c0 + s, hi - c0), T.IDB[:], T.CN[:, o + lo // 2:o + hi // 2]))
        return lst, ["IDB"] + ["CN%d" % (rn - 2 + h) for h in range(c0 // 48, (c1 + 47) // 48)]

    def hand_down(rn, c0):
        j = rn - 1 + c0 // 24
        lst, r = [], []
        for side in (0, 1) if rn > 1 else ():
            l, r = inherited(lambda a, b: P[1][:, 24 * side + a:24 * side + b:2], rn, c0, c0 + 24)
            lst += l
        lst += [(P[1][:, 0:48], sel(i), T.FS[:, 768 * j + i:768 * j + 768:16]) for i in range(16)]
        mm(run(lst, True, True), ["Z"] + r + rtok("F0", rn, c0, c0 + 24) + rtok("F1", rn, c0, c0 + 24), ["@1"])
        ac(T.CN[:, 48 * j:48 * j + 48], P[1][:, 0:48], ["@1"], ["CN%d" % j])

    def mixed(c0, c1):
        n_ = c1 - c0
        ac(T.VW[:, 0:n_], P[2][:, 0:n_], ["@2"], ["VWx"])
        ac(T.VW[:, n_:3 * n_], P[3][:, 0:2 * n_], ["@3"], ["VWk"])
        for j, (x, gg) in enumerate(((0, 0), (0, 1), (1, 0), (1, 1))):
            mm(run([(P[6][:, x:3 * n_:2], sw(ZF, x, gg), T.VW[:, gg:3 * n_:2])], j == 0, j == 3), ["VWx", "VWk", "ZF0", "ZF1"], ["@6"])

    sin = lambda l, c0, c1: T.SIN[:, 16 * c0 + l:16 * c1:16]

    def halves(c0, c1):
        n_ = c1 - c0
        for q, l in enumerate((0, 2, 4)):
            ac(sin(l, c0, c1), P[6][:, q * n_:(q + 1) * n_], ["@6", "SIN"], tok("S%d" % l, c0, c1))
        for q, l in enumerate((0, 2, 4)):
            tt(sin(l + 1, c0, c1), P[6][:, q * n_:(q + 1) * n_], sin(l, c0, c1), A.subtract, ["@6", "SIN"] + tok("S%d" % l, c0, c1),
               tok("S%d" % (l + 1), c0, c1))

    def kp(side, c0, c1, st=1):
        return T.KP[:, 96 * side + c0:96 * side + c1:st]

    def places(rn, c0, c1):
        dump = P[5][:, 96 + c0:96 + c1]
        mm(run([(dump, T.IDB[:], T.JH[:, c0:c1]), (dump, T.IDB[:], T.JC[:, c0:c1])], True, False), ["IDB", "JH", "JC"], ["@5"])
        for side in (0, 1):
            lst = [(P[4][:, 96 * side + c0:96 * side + c1], sel(i), fft(rn, side, c0, c1, i, 16)) for i in range(16)]
            mm(run(lst, side == 0, side == 1), ["Z"] + rtok("F%d" % side, rn, c0, c1), ["@4"])
            if rn == 3 and side == 0:
                terms = [inherited(lambda a, b: P[4][:, o + a:o + b:2], 3, c0, c1) for o in (c0, 96 + c0)]
                mm(run(terms[0][0] + terms[1][0], False, False), terms[0][1], ["@4"])
        for side in (0, 1):
            af(kp(side, c0, c1), P[4][:, 96 * side + c0:96 * side + c1], AF.Relu, -1.0, 1.0, ["@4"], tok("KP%d" % side, c0, c1))
        E = 4 if rn == 3 else 1
        kt = tok("KP0", max(c0 - E, 0), c1) + tok("KP1", max(c0 - E, 0), c1)
        u0 = max(c0, E)
        lst = [(P[5][:, c0:c1], T.IDB[:] if E > 1 else T.TRI[:], kp(0, c0, c1))]
        for side in (0, 1):
            for e in range(E):
                if E > 1 or side:
                    lst.append((P[5][:, c0:c1:E], T.TRB[:], kp(side, c0 + e, c1, E)))
                lst.append((P[5][:, u0:c1:E], T.TRU[:], kp(side, u0 - E + e, c1 - E, E)))
        lst += [(dump, T.NBG[:], kp(0, c0, c1)), (dump, T.NBG[:], kp(1, c0, c1))]
        mm(run(lst, False, True), kt + ["TRB", "TRU", "TRI", "IDB", "NBG"], ["@5"])
        mm(run([(P[4][:, 192 + 96 * sd + c0 + x:192 + 96 * sd + c1:2], sw(ZX, x, gg), kp(sd, c0 + gg, c1, 2))
                for sd in (0, 1) for x in (0, 1) for gg in (0, 1)], True, True), kt + ["ZX0", "ZX1"], ["@4"])

    def scatter(rn, c0, c1):
        wn, wt = WIN[rn - 3], "W%d" % (rn - 3)
        init = T.SC[:, c0 - 1:c0] if c0 else 0.0
        op("v", lambda: vec.tensor_tensor_scan(T.SC[:, c0:c1], P[5][:, c0:c1], kp(1, c0, c1), init, A.add, A.add),
           ["@5"] + tok("KP1", c0, c1) + (tok("SC", c0 - 1, c0) if c0 else []), tok("SC", c0, c1))
        tt(T.SC[:, 96 + c0:96 + c1], P[5][:, 96 + c0:96 + c1], T.SC[:, c0:c1], A.max, ["@5"] + tok("SC", c0, c1), ["SO"])
        cp(T.OS[:, c0:c1], T.SC[:, 96 + c0:96 + c1], ["SO"], tok("OS", c0, c1))
        for sd in (0, 1):
            cp(sin(6 + sd, c0, c1), P[4][:, 192 + 96 * sd + c0:192 + 96 * sd + c1], ["@4", "SIN"], tok("S%d" % (6 + sd), c0, c1))
        src = T.SRC[:, 16 * c0:16 * c1]
        turn32(src, T.SIN[:, 16 * c0:16 * c1], sum([tok("S%d" % l, c0, c1) for l in range(8)], ["SIN"]), tok("SRC", c0, c1))
        op("v", lambda: vec.tensor_copy(wn[:, 0:WINW].indirect(T.OS[:, c0:c1]), src), tok("OS", c0, c1) + tok("SRC", c0, c1) + [wt], [wt],
           cost=picked(src, SCATTER))

    def press(rn):
        ca, cs, cb = PARTS[rn]
        near_tests(rn, 0, FIRST)
        mixed(0, 96)
        near_tests(rn, FIRST, ca)
        places(rn, 0, ca)
        near_tests(rn, ca, cs)
        halves(0, 96)
        if rn == 3:
            far_tests(2, 24, 48)
            hand_down(2, 24)
        scatter(rn, 0, ca)
        for a, b in ((ca, cb), (cb, 96)):
            if b > a:
                far_tests(rn, max(a, cs), b)
                places(rn, a, b)
                scatter(rn, a, b)

    def read_back(rn, c0, c1):
        wn = WIN[rn - 3]
        for d, b, w0, w in ((1, 7, 0, 24), (2, 6, 24, 16)):
            sl = (lambda i: wn[:, 96 * i + d:96 * i + d + 96]) if rn == 5 else (lambda i: wn[:, i + d:1536 + i + d:16])
            mm(run([(P[b][0:96, i:16 * w:16], sl(i), T.WS[:, w0:w0 + w]) for i in range(16)], True, True), ["W%d" % (rn - 3)] + WST, ["@%d" % b])
        row = lambda j, k=1: T.PT[0:96, 128 * j:128 * (j + k)]
        ts(row(0, 2), P[7][0:96, 0:256], -float(BIG), A.add, ["@7"], ["PT0"], 0.0, A.max)
        af(row(3), P[6][0:96, 0:128], AF.Relu, 1.0, -float(BIG), ["@6"], ["PT3"])
        ts(row(2), P[7][0:96, 256:384], -float(BIG), A.add, ["@7"], ["PT2"], 0.0, A.max)
        af(row(4), P[6][0:96, 128:256], AF.Relu, 1.0, -float(BIG), ["@6"], ["PT4"])
        term = lambda b, j: (P[b][:, 0:96], row(j), T.IDF[0:96, 0:96])
        mm(run([term(4, 0), term(4, 1)], True, False), ["PT0", "IDF"], ["@4"])
        mm(run([term(4, 3)], False, True), ["PT3"], ["@4"])
        mm(run([term(5, 2), term(5, 4)], True, True), ["PT2", "PT4"], ["@5"])
        empty = 16.0 if rn == 5 else 0.0
        ts(offp(rn - 2, c0, c1), P[4][:, c0:c1], empty, A.max, ["@4"], tok("OP%d" % (rn - 2), c0, c1))
        ts(offq(rn - 2, c0, c1), P[5][:, c0:c1], empty, A.max, ["@5"], tok("OQ%d" % (rn - 2), c0, c1))

    def rec(rn, e, nm, c0, c1):
        if rn > 3 or rn == 1:
            k = max(rn - 3, 0)
            gather(e, nm, ITW, lambda a, b: (offp if nm == "P" else offq)(k, a, b), c0, c1, ITT + tok("O%s%d" % (nm, k), c0, c1))
        else:
            q = 1 if nm == "P" else 0
            gather(e, nm, ITW, lambda a, b: ov(rn - 1, q, a, b), c0, c1, ITT + [otok(rn - 1, q, 0)])

    decide_base(1, 0, 24)
    rec(1, "v", "Q", 12, 24)
    rec(1, "a", "Q", 0, 12)
    key_terms("Q", [(0, 24, 0)], False, True)
    decide(1, 0, 24)
    for rn in (2, 3):
        C, W = 24 << (rn - 1), XW[rn - 1]
        hq, hp = SHARE[rn]
        rec(rn, "a", "Q", 0, hq)
        kid_lists(rn - 1, 0, C // 2)
        ac(T.XF[:, 0:W], P[2][:, 0:W], ["@2"], ["XF"])
        rec(rn, "v", "Q", hq, W)
        key_terms("Q", [(0, W, 0), (W, C, W - C // 2)], True, False)
        decide_base(rn, 0, C)
        rec(rn, "a", "P", 0, hp)
        rec(rn, "v", "P", hp, C)
        key_terms("P", [(0, C, 0)], False, True)
        kid_terms(0, C)
        kid_copy(C)
        decide(rn, 0, C)
    kid_lists(3, 0, 96)
    late_constants()
    for rn in (1, 2):
        near_tests(rn, 0, 24, 12)
        hand_down(rn, 0)
    press(3)
    for rn in (4, 5):
        read_back(rn - 1, 0, 96)
        for nm in "PQ":
            rec(rn, "a", nm, 0, 52 if nm == "P" else 48)
            rec(rn, "v", nm, 52 if nm == "P" else 48, 96)
        kid_terms(0, 96)
        key_terms("P", [(0, 96, 0)], True, False)
        decide_base(rn, 0, 96)
        key_terms("Q", [(0, 96, 0)], False, True)
        kid_copy(96)
        decide(rn, 0, 96)
        kid_lists(rn, 0, 96)
        press(rn)
    read_back(5, 0, 96)

    fi = lambda j: T.FIN[:, 96 * j:96 * j + 96]

    def sizes(nm, off, h):
        for e, c0, c1 in (("a", 0, h), ("v", h, 96)):
            gather(e, nm, TBW, lambda a, b: off(3, a, b), c0, c1, tok("O%s3" % nm, c0, c1))
        mm(run([(P[2][:, 0:96], sel(i), RR[nm][:, i:1536:16]) for i in range(16)], nm == "P", nm == "Q"), tok("R" + nm, 0, 96), ["@2"])
    cp(fi(0), P[4][:, 0:96], ["@4"], ["pp"])
    sizes("P", offp, 52)
    for o, j, b, out in ((A.min, 0, b0, T.ya), (A.max, 1, base(1), T.yb)):
        tt(fi(1 + j), P[5][:, 0:96], fi(0), o, ["@5", "pp"], ["m%d" % j])
        ts(T.YO[:, 96 * j:96 * j + 96], fi(1 + j), -float(b), A.add, ["m%d" % j], ["Y%d" % j], -1.0, A.max)
        dma("s", out[:], T.YO[:, 96 * j:96 * j + 96], ["Y%d" % j], ["o%d" % j])
    sizes("Q", offq, 56)
    ac(T.YO[:, 192:288], P[2][:, 0:96], ["@2"], ["YS"])
    dma("a", T.ys[:], T.YO[:, 192:288], ["YS"], ["o2"])
    op("s", None, ["o0", "o1", "o2"], (), kind="w")
    op("g", None, (), (), kind="w", ext=[("ls", engines_out(T, topo, core, sends))])

    hop = lambda j, i: HOP + (PE_HOP if ops[j]["e"] == "t" else 0.0)
    hold = lambda i: 0.06 if ops[i]["kind"] == "d" else ops[i]["cost"]
    when = {signal(rank + t, k): DUE.get(k, DUE["h"]) - (0.0 if late(t) else NEAR) for t in (1, 2, 3) for k in ITEMS}
    due = lambda nm: when.get(nm, 0.0)
    at_, busy = [], {e: [] for e in Q}
    for i, o in enumerate(ops):
        t0 = max([at_[j] + (ops[j]["cost"] + hop(j, i) if j in o["deps"] else hold(j)) for j in o["order"]]
                 + [due(nm) for nm, v in o["ext"]] + [0.0])
        for a, b in sorted(busy[o["e"]]):
            if b > t0 and a < t0 + hold(i) - SLACK:
                t0 = b
        at_.append(t0)
        busy[o["e"]].append((t0, t0 + hold(i)))
    issued = [ops[i] for i in sorted(range(len(ops)), key=lambda i: (at_[i], i))]

    for o in ops:
        for j in o["deps"]:
            ops[j]["need"] = True
    cnt = {}
    for o in issued:
        if o["kind"] == "c" and o["need"]:
            cnt[o["e"]] = cnt.get(o["e"], 0) + 1
            o["name"] = "c" + o["e"]
            o["val"] = cnt[o["e"]]
        elif o["kind"] == "d":
            o["val"] = 16
    seen = {}
    for o in issued:
        e = o["e"]
        want = {}
        for j in o["deps"]:
            want[ops[j]["name"]] = max(want.get(ops[j]["name"], 0), ops[j]["val"])
        for (nm, v) in o["ext"]:
            want[nm] = max(want.get(nm, 0), v)
        for nm in sorted(want):
            if seen.get((e, nm), 0) < want[nm]:
                Q[e].wait_ge(T.sem[nm], want[nm])
                seen[(e, nm)] = want[nm]
        if o["fn"] is None:
            continue
        ins = o["fn"]()
        if o["kind"] == "d":
            ins.then_inc(T.sem[o["name"]], 16)
        elif o["kind"] == "c" and o["need"]:
            ins.then_inc(T.sem[o["name"]], 1)
